import numpy as np
import ml_dtypes


def mxq(x, axis, fmt="e4m3"):
    dtype, down = {"e4m3": (ml_dtypes.float8_e4m3fn, 7), "e5m2": (ml_dtypes.float8_e5m2, 14)}[fmt]
    v = np.moveaxis(np.asarray(x, np.float32).astype(ml_dtypes.bfloat16).astype(np.float64), axis, -1)
    blocks = v.reshape(v.shape[:-1] + (-1, 32))
    amax = np.abs(blocks).max(-1, keepdims=True)
    byte = np.maximum(np.where(amax > 0, np.frexp(amax)[1] - 1 + 127, 0) - down, 1)
    scale = np.exp2(byte - 127.0)
    codes = (blocks / scale).astype(np.float32).astype(dtype).astype(np.float64)
    return np.moveaxis((codes * scale).reshape(v.shape), -1, axis)


WIDE = False


def mx_kscale(k):
    if not WIDE:
        return np.ones(k)
    levels = np.array([10, -10, 5, -5, 0])
    if k % 512:
        return np.exp2(np.random.permutation(np.resize(levels, k // 32))).repeat(32)
    a = np.empty((k // 512, 16))
    for p in range(k // 512):
        a[p, :8] = np.random.permutation(np.resize(levels, 8))
        for g in range(8):
            far = levels[np.abs(levels - a[p, g]) >= 10]
            a[p, g + 8] = far[np.random.randint(len(far))]
    return np.exp2(a.ravel()).repeat(32)


def f64(x):
    return np.asarray(x).astype(np.float64)


def striped(idx):
    return np.tile(idx.reshape(-1, 16).T, (8, 1)).astype(np.uint16)


def unstriped(offs):
    return offs[:16].T.reshape(-1).astype(np.int64)


def relu2(v):
    return np.maximum(v, 0.0) ** 2


K, T, E, C, N = 2048, 768, 9, 256, 128
TOP = 3


def by_expert(wq, xq):
    return np.concatenate([wq[e].T @ xq[:, e * C:(e + 1) * C] for e in range(E)], axis=1)


def setup_inputs():
    n = np.random.standard_normal
    s = mx_kscale(K)[:, None]
    deal = np.repeat(np.arange(E), C).reshape(TOP, T)[:, np.random.permutation(T)]
    deal = np.take_along_axis(deal, np.argsort(np.random.rand(TOP, T), axis=0), axis=0)
    for _ in range(8):
        s_, t_ = np.random.permutation(T).reshape(2, -1); r = np.random.randint(TOP, size=T // 2); x, y = deal[r, s_].copy(), deal[r, t_].copy()
        ok = ~((deal[:, s_] == y).any(0) | (deal[:, t_] == x).any(0)); deal[r[ok], s_[ok]] = y[ok]; deal[r[ok], t_[ok]] = x[ok]
    order = np.lexsort((np.random.rand(TOP * T), deal.reshape(-1)))
    slot_token = order % T; pos = np.empty(TOP * T, np.int64); pos[order] = np.arange(TOP * T); pos = pos.reshape(TOP, T)
    g = np.random.uniform(0.5, 1.5, (TOP, T)); g = g / g.sum(0)
    w_slot = np.empty(E * C)
    for r in range(TOP): w_slot[pos[r]] = g[r]
    return {
        "xT": (n((K, T)) * s).astype(np.float32),
        "w": (n((E, K, N)) / np.sqrt(K) / s[None]).astype(np.float32),
        "b": (0.3 * n((N, E))).astype(np.float32),
        "gate": np.tile(w_slot, (K, 1)).astype(np.float32),
        "offs": striped(slot_token),
        "pos1": striped(pos[0]),
        "pos2": striped(pos[1]),
        "pos3": striped(pos[2]),
    }


def reference(xT, w, b, gate, offs, pos1, pos2, pos3):
    idx = unstriped(offs)
    xq = mxq(f64(gate) * f64(xT)[:, idx], 0, "e4m3")
    y = by_expert(mxq(f64(w), 1, "e4m3"), xq)
    y = relu2(y + np.repeat(f64(b), C, axis=1))
    return y[:, unstriped(pos1)] + y[:, unstriped(pos2)] + y[:, unstriped(pos3)]

@@ -1,0 +1,168 @@
+from contextlib import ExitStack
+
+import concourse.mybir as mybir
+
+K, T, E, C, N = 2048, 768, 9, 256, 128
+S = E * C
+FLOPS = 2 * K * N * S
+BYTES = 4 * (K * T + E * K * N + N * E + S + N * T) + 2 * 128 * (S + 3 * T) // 16
+
+F32 = mybir.dt.float32
+BF16 = mybir.dt.bfloat16
+U32 = mybir.dt.uint32
+U16 = mybir.dt.uint16
+U8 = mybir.dt.uint8
+FP8X4 = mybir.dt.float8_e4m3fn_x4
+ACT = mybir.ActivationFunctionType
+ALU = mybir.AluOpType
+
+P = 128
+PACK = 4
+PASSES = K // (P * PACK)
+GROUP = 768
+GROUPS = S // GROUP
+SPARE = 16
+QUAD = 4
+
+
+def tile_moe_pre_lin_relu2_kernel(tc, xT, w, b, gate, offs, pos1, pos2, pos3, out):
+    nc = tc.nc
+    with ExitStack() as ctx:
+        keep = ctx.enter_context(tc.tile_pool(name="keep", bufs=1))
+        ring = ctx.enter_context(tc.tile_pool(name="ring", bufs=3))
+        psum = ctx.enter_context(tc.psum_pool(name="psum", bufs=6))
+
+        slot_tokens = keep.tile([P, S // 16], U16, name="slot_tokens")
+        nc.sync.dma_start(slot_tokens[:], offs)
+
+        x_rows = xT.rearrange("(g p j) t -> g j p t", p=P, j=PACK)
+        planes = {}
+        gates = []
+
+        def load_plane(g, j):
+            plane = keep.tile([P, T + SPARE], F32, name=f"plane{g}_{j}")
+            nc.vector.memset(plane[:, T:], 0.0)
+            nc.sync.dma_start(plane[:, :T], x_rows[g, j])
+            planes[g, j] = plane
+
+        def load_gate(q):
+            gt = keep.tile([P, GROUP], F32, name=f"gate{q}")
+            nc.sync.dma_start(gt[:], gate[0:P, q * GROUP:(q + 1) * GROUP])
+            gates.append(gt)
+
+        load_gate(0)
+        for g in range(PASSES):
+            for j in range(PACK):
+                load_plane(g, j)
+        w_raw = []
+
+        def load_w(e):
+            raw = ring.tile([P, PASSES, PACK, N], F32, name="w_raw", bufs=3)
+            nc.sync.dma_start(raw[:], w[e].rearrange("(g p j) n -> p g j n", p=P, j=PACK))
+            w_raw.append(raw)
+
+        for e in range(3):
+            load_w(e)
+        load_gate(1)
+        load_gate(2)
+        bias = keep.tile([P, E], F32, name="bias")
+        nc.sync.dma_start(bias[:], b)
+        lists = []
+        for r, pos in enumerate((pos1, pos2, pos3)):
+            lst = keep.tile([P, T // 16], U16, name=f"pos{r}")
+            nc.sync.dma_start(lst[:], pos)
+            lists.append(lst)
+        for e in range(3, E):
+            load_w(e)
+
+        w_codes = keep.tile([P, E, PASSES * N], U32, name="w_codes", align_bytes=64)
+        w_scales = keep.tile([P, E, PASSES * N], U8, name="w_scales", align_bytes=64)
+        x_codes = keep.tile([P, PASSES, S], U32, name="x_codes", align_bytes=64)
+        x_scales = keep.tile([P, PASSES, S], U8, name="x_scales", align_bytes=64)
+        y = keep.tile([P, S], F32, name="y")
+
+        def prepare_w(e):
+            packed = ring.tile([P, PASSES * N * PACK], BF16, name="w_packed", align_bytes=64, bufs=2)
+            nc.scalar.copy(
+                packed[:].rearrange("p (g c i j) -> p g c j i", g=PASSES, i=QUAD, j=PACK),
+                w_raw[e][:].rearrange("p g j (c i) -> p g c j i", i=QUAD),
+            )
+            nc.vector.quantize_mx(out=w_codes[:, e, :].bitcast(FP8X4), scales=w_scales[:, e, :], in_=packed[:])
+
+        def gather(g, s0, n):
+            q, o = divmod(s0, GROUP)
+            xg = ring.tile([P, PACK, n], F32, name="xg")
+            for j in range(PACK):
+                nc.vector.tensor_tensor(
+                    xg[:, j, :], planes[g, j][:].indirect(slot_tokens[:, s0 // 16:(s0 + n) // 16]),
+                    gates[q][:, o:o + n], ALU.mult)
+            packed = ring.tile([P, n * PACK], BF16, name="x_packed", align_bytes=64)
+            nc.scalar.copy(
+                packed[:].rearrange("p (c i j) -> p c j i", i=QUAD, j=PACK),
+                xg[:].rearrange("p j (c i) -> p c j i", i=QUAD),
+            )
+            return packed
+
+        def quantize(packed, g, s0, n):
+            o = 0
+            while o < n:
+                m = 512 if n - o >= 512 else n - o
+                nc.vector.quantize_mx(
+                    out=x_codes[:, g, s0 + o:s0 + o + m].bitcast(FP8X4), scales=x_scales[:, g, s0 + o:s0 + o + m],
+                    in_=packed[:, o * PACK:(o + m) * PACK])
+                o = o + m
+
+        accs = {}
+
+        def multiply(e, g):
+            if g == 0:
+                accs[e] = psum.tile([N, C], F32, name="acc")
+            nc.tensor.matmul_mx(
+                out=accs[e][:],
+                lhsT=w_codes[:, e, g * N:(g + 1) * N].bitcast(FP8X4), lhsT_scale=w_scales[:, e, g * N:(g + 1) * N],
+                rhs=x_codes[:, g, e * C:(e + 1) * C].bitcast(FP8X4), rhs_scale=x_scales[:, g, e * C:(e + 1) * C],
+                start=(g == 0), stop=(g == PASSES - 1))
+
+        def finish(e):
+            r = ring.tile([N, C], F32, name="r")
+            nc.scalar.activation(r[:], accs[e][:], ACT.Relu, bias=bias[:, e:e + 1])
+            nc.scalar.activation(y[:, e * C:(e + 1) * C], r[:], ACT.Square)
+
+        per = GROUP // C
+        for q in range(GROUPS):
+            last = q == GROUPS - 1
+            for g in range(PASSES):
+                if last and g == PASSES - 1:
+                    for e in range(q * per, (q + 1) * per):
+                        quantize(gather(g, e * C, C), g, e * C, C)
+                        multiply(e, g)
+                        finish(e)
+                    continue
+                quantize(gather(g, q * GROUP, GROUP), g, q * GROUP, GROUP)
+                if q == 0 and g > 0:
+                    prepare_w(g - 1)
+                if q == 0 and g == PASSES - 1:
+                    prepare_w(3)
+                if q == 1:
+                    prepare_w(4 + g)
+                if last:
+                    if g == 0:
+                        prepare_w(8)
+                    for e in range(q * per, (q + 1) * per):
+                        multiply(e, g)
+            if not last:
+                for e in range(q * per, (q + 1) * per):
+                    for g in range(PASSES):
+                        multiply(e, g)
+                    finish(e)
+
+        half = T // 2
+        for h in range(2):
+            cols = slice(h * half // 16, (h + 1) * half // 16)
+            s1 = ring.tile([P, half], F32, name="s1", bufs=2)
+            s2 = ring.tile([P, half], F32, name="s2", bufs=2)
+            s3 = ring.tile([P, half], F32, name="s3", bufs=2)
+            nc.vector.tensor_copy(s1[:], y[:].indirect(lists[0][:, cols]))
+            nc.vector.tensor_tensor(s2[:], y[:].indirect(lists[1][:, cols]), s1[:], ALU.add)
+            nc.vector.tensor_tensor(s3[:], y[:].indirect(lists[2][:, cols]), s2[:], ALU.add)
+            nc.sync.dma_start(out[:, h * half:(h + 1) * half], s3[:])

@@ -19,41 +19,51 @@ ALU = mybir.AluOpType
 P = 128
 PACK = 4
 PASSES = K // (P * PACK)
-GROUP = 768
-GROUPS = S // GROUP
-SPARE = 16
+GROUPS = (1280, 1024)
+WINDOW = 1288
+HEAD = 512
+TAIL = (512, 256, 128, 128)
 QUAD = 4
+HALF = C // 2
+
+
+def widths(n):
+    out_w = []
+    while n > 0:
+        m = 1024
+        while m > n:
+            m = m // 2
+        out_w.append(m)
+        n = n - m
+    return out_w
 
 
 def tile_moe_pre_lin_relu2_kernel(tc, xT, w, b, gate, offs, pos1, pos2, pos3, out):
     nc = tc.nc
     with ExitStack() as ctx:
         keep = ctx.enter_context(tc.tile_pool(name="keep", bufs=1))
-        ring = ctx.enter_context(tc.tile_pool(name="ring", bufs=3))
-        psum = ctx.enter_context(tc.psum_pool(name="psum", bufs=6))
+        ring = ctx.enter_context(tc.tile_pool(name="ring", bufs=2))
+        psum = ctx.enter_context(tc.psum_pool(name="psum", bufs=8))
 
         slot_tokens = keep.tile([P, S // 16], U16, name="slot_tokens")
         nc.sync.dma_start(slot_tokens[:], offs)
 
         x_rows = xT.rearrange("(g p j) t -> g j p t", p=P, j=PACK)
         planes = {}
-        gates = []
+        gates = keep.tile([P, S], F32, name="gates")
 
-        def load_plane(g, j):
-            plane = keep.tile([P, T + SPARE], F32, name=f"plane{g}_{j}")
-            nc.vector.memset(plane[:, T:], 0.0)
-            nc.sync.dma_start(plane[:, :T], x_rows[g, j])
+        def load_plane(g, j, queue):
+            plane = keep.tile([P, WINDOW], F32, name=f"plane{g}_{j}")
+
+            queue.dma_start(plane[:, :T], x_rows[g, j])
             planes[g, j] = plane
 
-        def load_gate(q):
-            gt = keep.tile([P, GROUP], F32, name=f"gate{q}")
-            nc.sync.dma_start(gt[:], gate[0:P, q * GROUP:(q + 1) * GROUP])
-            gates.append(gt)
+        def load_gate(s0, s1):
+            nc.sync.dma_start(gates[:, s0:s1], gate[0:P, s0:s1])
 
-        load_gate(0)
-        for g in range(PASSES):
-            for j in range(PACK):
-                load_plane(g, j)
+        load_plane(0, 0, nc.scalar)
+        load_gate(0, HEAD)
+        load_gate(HEAD, GROUPS[0])
         w_raw = []
 
         def load_w(e):
@@ -61,10 +71,13 @@ def tile_moe_pre_lin_relu2_kernel(tc, xT, w, b, gate, offs, pos1, pos2, pos3, ou
             nc.sync.dma_start(raw[:], w[e].rearrange("(g p j) n -> p g j n", p=P, j=PACK))
             w_raw.append(raw)
 
-        for e in range(3):
-            load_w(e)
-        load_gate(1)
-        load_gate(2)
+        for g in range(PASSES):
+            for j in range(PACK):
+                if (g, j) != (0, 0):
+                    load_plane(g, j, nc.sync)
+                if (g, j) in ((1, 0), (1, 2), (2, 0)):
+                    load_w(len(w_raw))
+        load_gate(GROUPS[0], S)
         bias = keep.tile([P, E], F32, name="bias")
         nc.sync.dma_start(bias[:], b)
         lists = []
@@ -75,94 +88,84 @@ def tile_moe_pre_lin_relu2_kernel(tc, xT, w, b, gate, offs, pos1, pos2, pos3, ou
         for e in range(3, E):
             load_w(e)
 
-        w_codes = keep.tile([P, E, PASSES * N], U32, name="w_codes", align_bytes=64)
-        w_scales = keep.tile([P, E, PASSES * N], U8, name="w_scales", align_bytes=64)
-        x_codes = keep.tile([P, PASSES, S], U32, name="x_codes", align_bytes=64)
-        x_scales = keep.tile([P, PASSES, S], U8, name="x_scales", align_bytes=64)
+        w_codes = keep.tile([P, E * PASSES * N], U32, name="w_codes", align_bytes=64)
+        w_scales = keep.tile([P, E * PASSES * N], U8, name="w_scales", align_bytes=64)
         y = keep.tile([P, S], F32, name="y")
 
         def prepare_w(e):
-            packed = ring.tile([P, PASSES * N * PACK], BF16, name="w_packed", align_bytes=64, bufs=2)
+            packed = ring.tile([P, PASSES * N * PACK], BF16, name="w_packed", align_bytes=64, bufs=3)
             nc.scalar.copy(
                 packed[:].rearrange("p (g c i j) -> p g c j i", g=PASSES, i=QUAD, j=PACK),
                 w_raw[e][:].rearrange("p g j (c i) -> p g c j i", i=QUAD),
             )
-            nc.vector.quantize_mx(out=w_codes[:, e, :].bitcast(FP8X4), scales=w_scales[:, e, :], in_=packed[:])
-
-        def gather(g, s0, n):
-            q, o = divmod(s0, GROUP)
-            xg = ring.tile([P, PACK, n], F32, name="xg")
-            for j in range(PACK):
-                nc.vector.tensor_tensor(
-                    xg[:, j, :], planes[g, j][:].indirect(slot_tokens[:, s0 // 16:(s0 + n) // 16]),
-                    gates[q][:, o:o + n], ALU.mult)
-            packed = ring.tile([P, n * PACK], BF16, name="x_packed", align_bytes=64)
-            nc.scalar.copy(
-                packed[:].rearrange("p (c i j) -> p c j i", i=QUAD, j=PACK),
-                xg[:].rearrange("p j (c i) -> p c j i", i=QUAD),
-            )
-            return packed
-
-        def quantize(packed, g, s0, n):
-            o = 0
-            while o < n:
-                m = 512 if n - o >= 512 else n - o
-                nc.vector.quantize_mx(
-                    out=x_codes[:, g, s0 + o:s0 + o + m].bitcast(FP8X4), scales=x_scales[:, g, s0 + o:s0 + o + m],
-                    in_=packed[:, o * PACK:(o + m) * PACK])
-                o = o + m
+            cols = slice(e * PASSES * N, (e + 1) * PASSES * N)
+            nc.vector.quantize_mx(out=w_codes[:, cols].bitcast(FP8X4), scales=w_scales[:, cols], in_=packed[:])
 
         accs = {}
 
-        def multiply(e, g):
+        def multiply(s0, m, g, codes, scales, o):
+            e = s0 // C
             if g == 0:
-                accs[e] = psum.tile([N, C], F32, name="acc")
+                accs[s0] = psum.tile([N, m], F32, name="acc")
+            cols = slice((e * PASSES + g) * N, (e * PASSES + g + 1) * N)
             nc.tensor.matmul_mx(
-                out=accs[e][:],
-                lhsT=w_codes[:, e, g * N:(g + 1) * N].bitcast(FP8X4), lhsT_scale=w_scales[:, e, g * N:(g + 1) * N],
-                rhs=x_codes[:, g, e * C:(e + 1) * C].bitcast(FP8X4), rhs_scale=x_scales[:, g, e * C:(e + 1) * C],
+                out=accs[s0][:],
+                lhsT=w_codes[:, cols].bitcast(FP8X4), lhsT_scale=w_scales[:, cols],
+                rhs=codes[:, o:o + m].bitcast(FP8X4), rhs_scale=scales[:, o:o + m],
                 start=(g == 0), stop=(g == PASSES - 1))
 
-        def finish(e):
-            r = ring.tile([N, C], F32, name="r")
-            nc.scalar.activation(r[:], accs[e][:], ACT.Relu, bias=bias[:, e:e + 1])
-            nc.scalar.activation(y[:, e * C:(e + 1) * C], r[:], ACT.Square)
+        def finish(s0, m):
+            e = s0 // C
+            r = ring.tile([N, m], F32, name="r", bufs=2)
+            nc.scalar.activation(r[:], accs[s0][:], ACT.Relu, bias=bias[:, e:e + 1])
+            nc.scalar.activation(y[:, s0:s0 + m], r[:], ACT.Square)
 
-        per = GROUP // C
-        for q in range(GROUPS):
-            last = q == GROUPS - 1
-            for g in range(PASSES):
-                if last and g == PASSES - 1:
-                    for e in range(q * per, (q + 1) * per):
-                        quantize(gather(g, e * C, C), g, e * C, C)
-                        multiply(e, g)
-                        finish(e)
-                    continue
-                quantize(gather(g, q * GROUP, GROUP), g, q * GROUP, GROUP)
-                if q == 0 and g > 0:
-                    prepare_w(g - 1)
-                if q == 0 and g == PASSES - 1:
-                    prepare_w(3)
-                if q == 1:
-                    prepare_w(4 + g)
-                if last:
-                    if g == 0:
-                        prepare_w(8)
-                    for e in range(q * per, (q + 1) * per):
-                        multiply(e, g)
-            if not last:
-                for e in range(q * per, (q + 1) * per):
-                    for g in range(PASSES):
-                        multiply(e, g)
-                    finish(e)
+        sums = [(e * C, C) for e in range(E - 1)] + [(S - C, HALF), (S - HALF, HALF)]
 
-        half = T // 2
-        for h in range(2):
-            cols = slice(h * half // 16, (h + 1) * half // 16)
-            s1 = ring.tile([P, half], F32, name="s1", bufs=2)
-            s2 = ring.tile([P, half], F32, name="s2", bufs=2)
-            s3 = ring.tile([P, half], F32, name="s3", bufs=2)
-            nc.vector.tensor_copy(s1[:], y[:].indirect(lists[0][:, cols]))
-            nc.vector.tensor_tensor(s2[:], y[:].indirect(lists[1][:, cols]), s1[:], ALU.add)
-            nc.vector.tensor_tensor(s3[:], y[:].indirect(lists[2][:, cols]), s2[:], ALU.add)
-            nc.sync.dma_start(out[:, h * half:(h + 1) * half], s3[:])
+        held = []
+        for c, (start, n, g) in enumerate([(0, 1280, 0), (0, 1280, 1), (0, 1280, 2), (0, 1280, 3), (1280, 1024, 0), (1280, 1024, 1), (1280, 512, 2), (1280, 512, 3), (1792, 512, 2), (1792, 256, 3), (2048, 128, 3), (2176, 128, 3)]):
+            xg = ring.tile([P, PACK, n], F32, name="xg")
+            packed = ring.tile([P, PACK * n], BF16, name="x_packed", align_bytes=64)
+            codes = ring.tile([P, n], U32, name="x_codes", align_bytes=64, bufs=3)
+            scales = ring.tile([P, n], U8, name="x_scales", align_bytes=64, bufs=3)
+            for j in range(PACK):
+                cuts = (0, HEAD, n) if (c, j) == (0, 0) else (0, n)
+                for a, z in zip(cuts, cuts[1:]):
+                    s0, s1 = start + a, start + z
+                    nc.vector.tensor_tensor(
+                        xg[:, j, a:z], planes[g, j][:].indirect(slot_tokens[:, s0 // 16:s1 // 16]),
+                        gates[:, s0:s1], ALU.mult)
+            a = 0
+            for wd in widths(n):
+                dst = packed[:, PACK * a:PACK * (a + wd)]
+                nc.scalar.copy(
+                    dst.rearrange("p (c i j) -> p c j i", i=QUAD, j=PACK),
+                    xg[:, :, a:a + wd].rearrange("p j (c i) -> p c j i", i=QUAD),
+                )
+                nc.vector.quantize_mx(
+                    out=codes[:, a:a + wd].bitcast(FP8X4), scales=scales[:, a:a + wd], in_=dst)
+                a = a + wd
+            held.extend((s0, sm, g, codes, scales, s0 - start) for s0, sm in sums if start <= s0 < start + n)
+            for e in {0: (0, 1, 2), 1: (3, 4, 5), 2: (6, 7, 8)}.get(c, ()):
+                prepare_w(e)
+            if c >= 1:
+                for args in held:
+                    multiply(*args)
+                    if args[2] == PASSES - 1:
+                        finish(args[0], args[1])
+                held = []
+
+        cuts = (0, 480, 768)
+        total = ring.tile([P, 3 * T], F32, name="xg")
+        parts = []
+        for a, z in zip(cuts, cuts[1:]):
+            parts.append((a, z, [total[:, r * T + a:r * T + z] for r in range(3)]))
+        for r in range(3):
+            for a, z, s in parts:
+                window = y[:].indirect(lists[r][:, a // 16:z // 16])
+                if r == 0:
+                    nc.vector.tensor_copy(s[0], window)
+                else:
+                    nc.vector.tensor_tensor(s[r], window, s[r - 1], ALU.add)
+                if r == 2:
+                    (nc.sync if a == 0 else nc.scalar).dma_start(out[:, a:z], s[2])

@@ -19,23 +19,14 @@ ALU = mybir.AluOpType
 P = 128
 PACK = 4
 PASSES = K // (P * PACK)
-GROUPS = (1280, 1024)
-WINDOW = 1288
-HEAD = 512
-TAIL = (512, 256, 128, 128)
+WINDOW = S + 8
+HEAD_CUTS = (0, 256, 768, 1792, S)
+WIDE = 1024
+LAST_PIECES = (1024, 512, 256, 256, 128, 128)
 QUAD = 4
 HALF = C // 2
-
-
-def widths(n):
-    out_w = []
-    while n > 0:
-        m = 1024
-        while m > n:
-            m = m // 2
-        out_w.append(m)
-        n = n - m
-    return out_w
+W_GROUPS = ((0, 4), (4, 8), (8, 9))
+OUT_CUTS = ((0, 384, T), (0, 384, T), (0, 352, 672, T))
 
 
 def tile_moe_pre_lin_relu2_kernel(tc, xT, w, b, gate, offs, pos1, pos2, pos3, out):
@@ -43,41 +34,38 @@ def tile_moe_pre_lin_relu2_kernel(tc, xT, w, b, gate, offs, pos1, pos2, pos3, ou
     with ExitStack() as ctx:
         keep = ctx.enter_context(tc.tile_pool(name="keep", bufs=1))
         ring = ctx.enter_context(tc.tile_pool(name="ring", bufs=2))
-        psum = ctx.enter_context(tc.psum_pool(name="psum", bufs=8))
+        psum = ctx.enter_context(tc.psum_pool(name="psum", bufs=1))
 
         slot_tokens = keep.tile([P, S // 16], U16, name="slot_tokens")
         nc.sync.dma_start(slot_tokens[:], offs)
 
         x_rows = xT.rearrange("(g p j) t -> g j p t", p=P, j=PACK)
-        planes = {}
+        w_rows = w.rearrange("e (g p j) n -> g p e (j n)", p=P, j=PACK)
         gates = keep.tile([P, S], F32, name="gates")
+        planes = {}
+        w_raw = {}
 
-        def load_plane(g, j, queue):
-            plane = keep.tile([P, WINDOW], F32, name=f"plane{g}_{j}")
-
-            queue.dma_start(plane[:, :T], x_rows[g, j])
+        def load_plane(g, j):
+            plane = ring.tile([P, WINDOW], F32, name="plane", bufs=5)
+            nc.sync.dma_start(plane[:, :T], x_rows[g, j])
             planes[g, j] = plane
 
         def load_gate(s0, s1):
             nc.sync.dma_start(gates[:, s0:s1], gate[0:P, s0:s1])
 
-        load_plane(0, 0, nc.scalar)
-        load_gate(0, HEAD)
-        load_gate(HEAD, GROUPS[0])
-        w_raw = []
+        def load_w(g):
+            for e0, e1 in W_GROUPS:
+                raw = ring.tile([P, e1 - e0, PACK * N], F32, name=f"w_raw{e1 - e0}")
+                nc.sync.dma_start(raw[:], w_rows[g][:, e0:e1, :])
+                w_raw[g, e0] = raw
 
-        def load_w(e):
-            raw = ring.tile([P, PASSES, PACK, N], F32, name="w_raw", bufs=3)
-            nc.sync.dma_start(raw[:], w[e].rearrange("(g p j) n -> p g j n", p=P, j=PACK))
-            w_raw.append(raw)
-
-        for g in range(PASSES):
-            for j in range(PACK):
-                if (g, j) != (0, 0):
-                    load_plane(g, j, nc.sync)
-                if (g, j) in ((1, 0), (1, 2), (2, 0)):
-                    load_w(len(w_raw))
-        load_gate(GROUPS[0], S)
+        load_gate(HEAD_CUTS[0], HEAD_CUTS[1])
+        load_plane(0, 0)
+        for a, z in zip(HEAD_CUTS[1:], HEAD_CUTS[2:]):
+            load_gate(a, z)
+        for j in range(1, PACK):
+            load_plane(0, j)
+        load_w(0)
         bias = keep.tile([P, E], F32, name="bias")
         nc.sync.dma_start(bias[:], b)
         lists = []
@@ -85,87 +73,99 @@ def tile_moe_pre_lin_relu2_kernel(tc, xT, w, b, gate, offs, pos1, pos2, pos3, ou
             lst = keep.tile([P, T // 16], U16, name=f"pos{r}")
             nc.sync.dma_start(lst[:], pos)
             lists.append(lst)
-        for e in range(3, E):
-            load_w(e)
 
-        w_codes = keep.tile([P, E * PASSES * N], U32, name="w_codes", align_bytes=64)
-        w_scales = keep.tile([P, E * PASSES * N], U8, name="w_scales", align_bytes=64)
         y = keep.tile([P, S], F32, name="y")
 
-        def prepare_w(e):
-            packed = ring.tile([P, PASSES * N * PACK], BF16, name="w_packed", align_bytes=64, bufs=3)
-            nc.scalar.copy(
-                packed[:].rearrange("p (g c i j) -> p g c j i", g=PASSES, i=QUAD, j=PACK),
-                w_raw[e][:].rearrange("p g j (c i) -> p g c j i", i=QUAD),
-            )
-            cols = slice(e * PASSES * N, (e + 1) * PASSES * N)
-            nc.vector.quantize_mx(out=w_codes[:, cols].bitcast(FP8X4), scales=w_scales[:, cols], in_=packed[:])
+        def prepare_w(g):
+            packed = ring.tile([P, E * N * PACK], BF16, name="w_packed", align_bytes=64, bufs=1)
+            for e0, e1 in W_GROUPS:
+                nc.scalar.copy(
+                    packed[:, e0 * N * PACK:e1 * N * PACK].rearrange(
+                        "p (e c i j) -> p e c j i", e=e1 - e0, i=QUAD, j=PACK),
+                    w_raw[g, e0][:].rearrange("p e (j c i) -> p e c j i", j=PACK, i=QUAD),
+                )
+            codes = ring.tile([P, E * N], U32, name="w_codes", align_bytes=64)
+            scales = ring.tile([P, E * N], U8, name="w_scales", align_bytes=64)
+            for e0, e1 in ((0, E - 1), (E - 1, E)):
+                nc.vector.quantize_mx(
+                    out=codes[:, e0 * N:e1 * N].bitcast(FP8X4), scales=scales[:, e0 * N:e1 * N],
+                    in_=packed[:, e0 * N * PACK:e1 * N * PACK])
+            return codes, scales
 
-        accs = {}
+        banks = [[(0, C), (C, C)], [(2 * C, C), (3 * C, C)]]
+        banks = banks + [[(e * C, C)] for e in range(4, E - 1)] + [[(S - C, HALF)], [(S - HALF, HALF)]]
+        accs = []
+        for i, sums in enumerate(banks):
+            accs.append(psum.tile([N, sum(m for s0, m in sums)], F32, name=f"acc{i}"))
 
-        def multiply(s0, m, g, codes, scales, o):
-            e = s0 // C
-            if g == 0:
-                accs[s0] = psum.tile([N, m], F32, name="acc")
-            cols = slice((e * PASSES + g) * N, (e * PASSES + g + 1) * N)
-            nc.tensor.matmul_mx(
-                out=accs[s0][:],
-                lhsT=w_codes[:, cols].bitcast(FP8X4), lhsT_scale=w_scales[:, cols],
-                rhs=codes[:, o:o + m].bitcast(FP8X4), rhs_scale=scales[:, o:o + m],
-                start=(g == 0), stop=(g == PASSES - 1))
+        def multiply(g, start, n, codes, scales, w_codes, w_scales):
+            for acc, sums in zip(accs, banks):
+                if not start <= sums[0][0] < start + n:
+                    continue
+                for s0, m in sums:
+                    e = s0 // C
+                    nc.tensor.matmul_mx(
+                        out=acc[:, s0 - sums[0][0]:s0 - sums[0][0] + m],
+                        lhsT=w_codes[:, e * N:(e + 1) * N].bitcast(FP8X4), lhsT_scale=w_scales[:, e * N:(e + 1) * N],
+                        rhs=codes[:, s0 - start:s0 - start + m].bitcast(FP8X4),
+                        rhs_scale=scales[:, s0 - start:s0 - start + m],
+                        start=(g == 0 and s0 == sums[0][0]), stop=(g == PASSES - 1 and s0 == sums[-1][0]))
+                if g == PASSES - 1:
+                    for s0, m in sums:
+                        e = s0 // C
+                        r = ring.tile([N, m], F32, name="r")
+                        nc.scalar.activation(
+                            r[:], acc[:, s0 - sums[0][0]:s0 - sums[0][0] + m], ACT.Relu, bias=bias[:, e:e + 1])
+                        nc.scalar.activation(y[:, s0:s0 + m], r[:], ACT.Square)
 
-        def finish(s0, m):
-            e = s0 // C
-            r = ring.tile([N, m], F32, name="r", bufs=2)
-            nc.scalar.activation(r[:], accs[s0][:], ACT.Relu, bias=bias[:, e:e + 1])
-            nc.scalar.activation(y[:, s0:s0 + m], r[:], ACT.Square)
-
-        sums = [(e * C, C) for e in range(E - 1)] + [(S - C, HALF), (S - HALF, HALF)]
-
-        held = []
-        for c, (start, n, g) in enumerate([(0, 1280, 0), (0, 1280, 1), (0, 1280, 2), (0, 1280, 3), (1280, 1024, 0), (1280, 1024, 1), (1280, 512, 2), (1280, 512, 3), (1792, 512, 2), (1792, 256, 3), (2048, 128, 3), (2176, 128, 3)]):
+        def gather(g, start, n, cuts):
             xg = ring.tile([P, PACK, n], F32, name="xg")
-            packed = ring.tile([P, PACK * n], BF16, name="x_packed", align_bytes=64)
+            for j in range(PACK):
+                for a, z in zip(cuts[j], cuts[j][1:]):
+                    nc.vector.tensor_tensor(
+                        xg[:, j, a:z], planes[g, j][:].indirect(slot_tokens[:, (start + a) // 16:(start + z) // 16]),
+                        gates[:, start + a:start + z], ALU.mult)
+            return xg
+
+        def quantise(xg, a, n):
+            packed = ring.tile([P, PACK * n], BF16, name="x_packed", align_bytes=64, bufs=3)
             codes = ring.tile([P, n], U32, name="x_codes", align_bytes=64, bufs=3)
             scales = ring.tile([P, n], U8, name="x_scales", align_bytes=64, bufs=3)
-            for j in range(PACK):
-                cuts = (0, HEAD, n) if (c, j) == (0, 0) else (0, n)
-                for a, z in zip(cuts, cuts[1:]):
-                    s0, s1 = start + a, start + z
-                    nc.vector.tensor_tensor(
-                        xg[:, j, a:z], planes[g, j][:].indirect(slot_tokens[:, s0 // 16:s1 // 16]),
-                        gates[:, s0:s1], ALU.mult)
-            a = 0
-            for wd in widths(n):
-                dst = packed[:, PACK * a:PACK * (a + wd)]
-                nc.scalar.copy(
-                    dst.rearrange("p (c i j) -> p c j i", i=QUAD, j=PACK),
-                    xg[:, :, a:a + wd].rearrange("p j (c i) -> p c j i", i=QUAD),
-                )
-                nc.vector.quantize_mx(
-                    out=codes[:, a:a + wd].bitcast(FP8X4), scales=scales[:, a:a + wd], in_=dst)
-                a = a + wd
-            held.extend((s0, sm, g, codes, scales, s0 - start) for s0, sm in sums if start <= s0 < start + n)
-            for e in {0: (0, 1, 2), 1: (3, 4, 5), 2: (6, 7, 8)}.get(c, ()):
-                prepare_w(e)
-            if c >= 1:
-                for args in held:
-                    multiply(*args)
-                    if args[2] == PASSES - 1:
-                        finish(args[0], args[1])
-                held = []
+            nc.scalar.copy(
+                packed[:].rearrange("p (c i j) -> p c j i", i=QUAD, j=PACK),
+                xg[:, :, a:a + n].rearrange("p j (c i) -> p c j i", i=QUAD),
+            )
+            nc.vector.quantize_mx(out=codes[:].bitcast(FP8X4), scales=scales[:], in_=packed[:])
+            return codes, scales
 
-        cuts = (0, 480, 768)
-        total = ring.tile([P, 3 * T], F32, name="xg")
-        parts = []
-        for a, z in zip(cuts, cuts[1:]):
-            parts.append((a, z, [total[:, r * T + a:r * T + z] for r in range(3)]))
+        for g in range(PASSES):
+            if g + 1 < PASSES:
+                for j in range(PACK):
+                    load_plane(g + 1, j)
+                load_w(g + 1)
+            if g + 1 < PASSES:
+                xg = gather(g, 0, S, [HEAD_CUTS if (g, j) == (0, 0) else (0, S) for j in range(PACK)])
+                w_codes, w_scales = prepare_w(g)
+                for a in range(0, S, WIDE):
+                    n = min(WIDE, S - a)
+                    codes, scales = quantise(xg, a, n)
+                    multiply(g, a, n, codes, scales, w_codes, w_scales)
+            else:
+                w_codes, w_scales = prepare_w(g)
+                a = 0
+                for n in LAST_PIECES:
+                    xg = gather(g, a, n, [(0, n)] * PACK)
+                    codes, scales = quantise(xg, 0, n)
+                    multiply(g, a, n, codes, scales, w_codes, w_scales)
+                    a = a + n
+
+        total = ring.tile([P, 3, T], F32, name="xg")
         for r in range(3):
-            for a, z, s in parts:
+            for a, z in zip(OUT_CUTS[r], OUT_CUTS[r][1:]):
                 window = y[:].indirect(lists[r][:, a // 16:z // 16])
                 if r == 0:
-                    nc.vector.tensor_copy(s[0], window)
+                    nc.vector.tensor_copy(total[:, 0, a:z], window)
                 else:
-                    nc.vector.tensor_tensor(s[r], window, s[r - 1], ALU.add)
+                    nc.vector.tensor_tensor(total[:, r, a:z], window, total[:, r - 1, a:z], ALU.add)
                 if r == 2:
-                    (nc.sync if a == 0 else nc.scalar).dma_start(out[:, a:z], s[2])
+                    (nc.sync if z == T or a == 0 else nc.scalar).dma_start(out[:, a:z], total[:, r, a:z])

@@ -19,14 +19,26 @@ ALU = mybir.AluOpType
 P = 128
 PACK = 4
 PASSES = K // (P * PACK)
-WINDOW = S + 8
-HEAD_CUTS = (0, 256, 768, 1792, S)
-WIDE = 1024
-LAST_PIECES = (1024, 512, 256, 256, 128, 128)
-QUAD = 4
 HALF = C // 2
-W_GROUPS = ((0, 4), (4, 8), (8, 9))
+QUAD = 4
+WIDE = 4 * C
+SPARE = 8
+HEAD_CUTS = (0, C, 3 * C, 6 * C, S)
+LAST_CUTS = (0, C, C + HALF, 2 * C)
 OUT_CUTS = ((0, 384, T), (0, 384, T), (0, 352, 672, T))
+EARLY = 6
+W_COLS = PASSES * N
+
+
+def widths(n):
+    out_w = []
+    while n > 0:
+        m = WIDE
+        while m > n:
+            m = m // 2
+        out_w.append(m)
+        n = n - m
+    return out_w
 
 
 def tile_moe_pre_lin_relu2_kernel(tc, xT, w, b, gate, offs, pos1, pos2, pos3, out):
@@ -40,32 +52,36 @@ def tile_moe_pre_lin_relu2_kernel(tc, xT, w, b, gate, offs, pos1, pos2, pos3, ou
         nc.sync.dma_start(slot_tokens[:], offs)
 
         x_rows = xT.rearrange("(g p j) t -> g j p t", p=P, j=PACK)
-        w_rows = w.rearrange("e (g p j) n -> g p e (j n)", p=P, j=PACK)
         gates = keep.tile([P, S], F32, name="gates")
         planes = {}
-        w_raw = {}
+        w_raw = []
 
-        def load_plane(g, j):
-            plane = ring.tile([P, WINDOW], F32, name="plane", bufs=5)
-            nc.sync.dma_start(plane[:, :T], x_rows[g, j])
+        def load_plane(g, j, queue):
+            if g == 2:
+                plane = keep.tile([P, WIDE + SPARE], F32, name=f"plane2_{j}")
+            else:
+                plane = ring.tile([P, (S if g < 2 else WIDE) + SPARE], F32, name="plane", bufs=PACK)
+            queue.dma_start(plane[:, :T], x_rows[g, j])
             planes[g, j] = plane
 
-        def load_gate(s0, s1):
-            nc.sync.dma_start(gates[:, s0:s1], gate[0:P, s0:s1])
+        def load_w(e):
+            raw = ring.tile([P, PASSES, PACK, N], F32, name="stage", align_bytes=64, bufs=4)
+            nc.sync.dma_start(raw[:], w[e].rearrange("(g p j) n -> p g j n", p=P, j=PACK))
+            w_raw.append(raw)
 
-        def load_w(g):
-            for e0, e1 in W_GROUPS:
-                raw = ring.tile([P, e1 - e0, PACK * N], F32, name=f"w_raw{e1 - e0}")
-                nc.sync.dma_start(raw[:], w_rows[g][:, e0:e1, :])
-                w_raw[g, e0] = raw
-
-        load_gate(HEAD_CUTS[0], HEAD_CUTS[1])
-        load_plane(0, 0)
-        for a, z in zip(HEAD_CUTS[1:], HEAD_CUTS[2:]):
-            load_gate(a, z)
+        load_plane(0, 0, nc.scalar)
+        for a, z in zip(HEAD_CUTS, HEAD_CUTS[1:]):
+            nc.sync.dma_start(gates[:, a:z], gate[0:P, a:z])
         for j in range(1, PACK):
-            load_plane(0, j)
-        load_w(0)
+            load_plane(0, j, nc.sync)
+            load_w(2 * j - 2)
+            load_w(2 * j - 1)
+        for j in range(PACK):
+            load_plane(1, j, nc.sync)
+            if EARLY + j < E:
+                load_w(EARLY + j)
+        for j in range(PACK):
+            load_plane(2, j, nc.sync)
         bias = keep.tile([P, E], F32, name="bias")
         nc.sync.dma_start(bias[:], b)
         lists = []
@@ -73,93 +89,134 @@ def tile_moe_pre_lin_relu2_kernel(tc, xT, w, b, gate, offs, pos1, pos2, pos3, ou
             lst = keep.tile([P, T // 16], U16, name=f"pos{r}")
             nc.sync.dma_start(lst[:], pos)
             lists.append(lst)
+        for j in range(PACK):
+            load_plane(3, j, nc.sync)
 
+        w_codes = keep.tile([P, E * W_COLS], U32, name="w_codes", align_bytes=64)
+        w_scales = keep.tile([P, E * W_COLS], U8, name="w_scales", align_bytes=64)
         y = keep.tile([P, S], F32, name="y")
 
-        def prepare_w(g):
-            packed = ring.tile([P, E * N * PACK], BF16, name="w_packed", align_bytes=64, bufs=1)
-            for e0, e1 in W_GROUPS:
-                nc.scalar.copy(
-                    packed[:, e0 * N * PACK:e1 * N * PACK].rearrange(
-                        "p (e c i j) -> p e c j i", e=e1 - e0, i=QUAD, j=PACK),
-                    w_raw[g, e0][:].rearrange("p e (j c i) -> p e c j i", j=PACK, i=QUAD),
-                )
-            codes = ring.tile([P, E * N], U32, name="w_codes", align_bytes=64)
-            scales = ring.tile([P, E * N], U8, name="w_scales", align_bytes=64)
-            for e0, e1 in ((0, E - 1), (E - 1, E)):
+        def prepare_w(e0, e1, packed):
+            for a in range(e0, e1, 2):
+                z = min(a + 2, e1)
+                for e in range(a, z):
+                    nc.scalar.copy(
+                        packed[:, (e - e0) * W_COLS * PACK:(e - e0 + 1) * W_COLS * PACK].rearrange(
+                            "p (g c i j) -> p g c j i", g=PASSES, i=QUAD, j=PACK),
+                        w_raw[e][:].rearrange("p g j (c i) -> p g c j i", i=QUAD),
+                    )
                 nc.vector.quantize_mx(
-                    out=codes[:, e0 * N:e1 * N].bitcast(FP8X4), scales=scales[:, e0 * N:e1 * N],
-                    in_=packed[:, e0 * N * PACK:e1 * N * PACK])
-            return codes, scales
+                    out=w_codes[:, a * W_COLS:z * W_COLS].bitcast(FP8X4), scales=w_scales[:, a * W_COLS:z * W_COLS],
+                    in_=packed[:, (a - e0) * W_COLS * PACK:(z - e0) * W_COLS * PACK])
 
         banks = [[(0, C), (C, C)], [(2 * C, C), (3 * C, C)]]
         banks = banks + [[(e * C, C)] for e in range(4, E - 1)] + [[(S - C, HALF)], [(S - HALF, HALF)]]
-        accs = []
+        accs = {}
         for i, sums in enumerate(banks):
-            accs.append(psum.tile([N, sum(m for s0, m in sums)], F32, name=f"acc{i}"))
+            bank = psum.tile([N, sum(m for s0, m in sums)], F32, name=f"bank{i}")
+            for s0, m in sums:
+                accs[s0] = (bank[:, s0 - sums[0][0]:s0 - sums[0][0] + m], m, s0 == sums[0][0], s0 == sums[-1][0])
 
-        def multiply(g, start, n, codes, scales, w_codes, w_scales):
-            for acc, sums in zip(accs, banks):
-                if not start <= sums[0][0] < start + n:
-                    continue
-                for s0, m in sums:
-                    e = s0 // C
+        def multiply(g, start, n, codes, scales):
+            for s0 in sorted(accs):
+                acc, m, opens, closes = accs[s0]
+                if start <= s0 < start + n:
+                    cols = slice((s0 // C * PASSES + g) * N, (s0 // C * PASSES + g + 1) * N)
                     nc.tensor.matmul_mx(
-                        out=acc[:, s0 - sums[0][0]:s0 - sums[0][0] + m],
-                        lhsT=w_codes[:, e * N:(e + 1) * N].bitcast(FP8X4), lhsT_scale=w_scales[:, e * N:(e + 1) * N],
+                        out=acc,
+                        lhsT=w_codes[:, cols].bitcast(FP8X4), lhsT_scale=w_scales[:, cols],
                         rhs=codes[:, s0 - start:s0 - start + m].bitcast(FP8X4),
                         rhs_scale=scales[:, s0 - start:s0 - start + m],
-                        start=(g == 0 and s0 == sums[0][0]), stop=(g == PASSES - 1 and s0 == sums[-1][0]))
-                if g == PASSES - 1:
-                    for s0, m in sums:
-                        e = s0 // C
-                        r = ring.tile([N, m], F32, name="r")
-                        nc.scalar.activation(
-                            r[:], acc[:, s0 - sums[0][0]:s0 - sums[0][0] + m], ACT.Relu, bias=bias[:, e:e + 1])
-                        nc.scalar.activation(y[:, s0:s0 + m], r[:], ACT.Square)
+                        start=(g == 0 and opens), stop=(g == PASSES - 1 and closes))
 
-        def gather(g, start, n, cuts):
-            xg = ring.tile([P, PACK, n], F32, name="xg")
-            for j in range(PACK):
-                for a, z in zip(cuts[j], cuts[j][1:]):
-                    nc.vector.tensor_tensor(
-                        xg[:, j, a:z], planes[g, j][:].indirect(slot_tokens[:, (start + a) // 16:(start + z) // 16]),
-                        gates[:, start + a:start + z], ALU.mult)
+        def bias_relu(e):
+            nc.scalar.activation(y[:, e * C:(e + 1) * C], accs[e * C][0], ACT.Relu, bias=bias[:, e:e + 1])
+
+        def square(e0, e1):
+            nc.scalar.activation(y[:, e0 * C:e1 * C], y[:, e0 * C:e1 * C], ACT.Square)
+
+        steps = [(0, S, 0), (0, S, 1), (0, 4 * C, 2), (0, 4 * C, 3), (4 * C, 3 * C, 2), (4 * C, 3 * C, 3),
+                 (7 * C, 2 * C, 2), (7 * C, 2 * C, 3)]
+        last_step = len(steps) - 1
+
+        def gather(c):
+            start, n, g = steps[c]
+            xg = ring.tile([P, PACK, n], F32, name="xg", align_bytes=64)
+            if c < last_step:
+                parts = [(j, a, z) for j in range(PACK)
+                         for a, z in (zip(HEAD_CUTS, HEAD_CUTS[1:]) if (c, j) == (0, 0) else ((0, n),))]
+            else:
+                parts = [(j, a, z) for a, z in zip(LAST_CUTS, LAST_CUTS[1:]) for j in range(PACK)]
+            for j, a, z in parts:
+                s0, s1 = start + a, start + z
+                nc.vector.tensor_tensor(
+                    xg[:, j, a:z], planes[g, j][:].indirect(slot_tokens[:, s0 // 16:s1 // 16]),
+                    gates[:, s0:s1], ALU.mult)
             return xg
 
-        def quantise(xg, a, n):
-            packed = ring.tile([P, PACK * n], BF16, name="x_packed", align_bytes=64, bufs=3)
-            codes = ring.tile([P, n], U32, name="x_codes", align_bytes=64, bufs=3)
-            scales = ring.tile([P, n], U8, name="x_scales", align_bytes=64, bufs=3)
+        def interleave(dst, src):
             nc.scalar.copy(
-                packed[:].rearrange("p (c i j) -> p c j i", i=QUAD, j=PACK),
-                xg[:, :, a:a + n].rearrange("p j (c i) -> p c j i", i=QUAD),
+                dst.rearrange("p (c i j) -> p c j i", i=QUAD, j=PACK),
+                src.rearrange("p j (c i) -> p c j i", i=QUAD),
             )
-            nc.vector.quantize_mx(out=codes[:].bitcast(FP8X4), scales=scales[:], in_=packed[:])
-            return codes, scales
 
-        for g in range(PASSES):
-            if g + 1 < PASSES:
-                for j in range(PACK):
-                    load_plane(g + 1, j)
-                load_w(g + 1)
-            if g + 1 < PASSES:
-                xg = gather(g, 0, S, [HEAD_CUTS if (g, j) == (0, 0) else (0, S) for j in range(PACK)])
-                w_codes, w_scales = prepare_w(g)
-                for a in range(0, S, WIDE):
-                    n = min(WIDE, S - a)
-                    codes, scales = quantise(xg, a, n)
-                    multiply(g, a, n, codes, scales, w_codes, w_scales)
-            else:
-                w_codes, w_scales = prepare_w(g)
+        def quantise(c, xg):
+            start, n, g = steps[c]
+            made = []
+            if c < last_step - 1:
                 a = 0
-                for n in LAST_PIECES:
-                    xg = gather(g, a, n, [(0, n)] * PACK)
-                    codes, scales = quantise(xg, 0, n)
-                    multiply(g, a, n, codes, scales, w_codes, w_scales)
-                    a = a + n
+                for wd in widths(n):
+                    packed = ring.tile([P, PACK * wd], BF16, name="stage", align_bytes=64, bufs=4)
+                    codes = ring.tile([P, wd], U32, name="x_codes", align_bytes=64, bufs=4)
+                    scales = ring.tile([P, wd], U8, name="x_scales", align_bytes=64, bufs=4)
+                    interleave(packed[:], xg[:, :, a:a + wd])
+                    nc.vector.quantize_mx(out=codes[:].bitcast(FP8X4), scales=scales[:], in_=packed[:])
+                    made.append((g, start + a, wd, codes, scales))
+                    a = a + wd
+                return made, packed
+            packed = ring.tile([P, PACK * n], BF16, name="stage", align_bytes=64, bufs=4)
+            codes = ring.tile([P, n], U32, name="x_codes", align_bytes=64, bufs=4)
+            scales = ring.tile([P, n], U8, name="x_scales", align_bytes=64, bufs=4)
+            cuts = LAST_CUTS if c == last_step else (0, C, n)
+            for a, z in zip(cuts, cuts[1:]):
+                interleave(packed[:, PACK * a:PACK * z], xg[:, :, a:z])
+                nc.vector.quantize_mx(
+                    out=codes[:, a:z].bitcast(FP8X4), scales=scales[:, a:z], in_=packed[:, PACK * a:PACK * z])
+            return [(g, start, n, codes, scales)], packed
 
-        total = ring.tile([P, 3, T], F32, name="xg")
+        gathered = gather(0)
+        early = ring.tile([P, EARLY * W_COLS * PACK], BF16, name="xg", align_bytes=64)
+        prepare_w(0, EARLY, early)
+        for c in range(len(steps)):
+            ahead = gather(c + 1) if c < last_step else None
+            made, packed = quantise(c, gathered)
+            gathered = ahead
+            if c == 0:
+                late = keep.tile([P, (E - EARLY) * W_COLS * PACK], BF16, name="late", align_bytes=64)
+                prepare_w(EARLY, E, late)
+            for args in made:
+                multiply(*args)
+            if c == 4:
+                for e in range(4):
+                    bias_relu(e)
+                square(0, 4)
+            if c == 6:
+                for e in range(4, 7):
+                    bias_relu(e)
+
+        square(4, 7)
+        bias_relu(7)
+        square(7, 8)
+
+        spare = packed[:, PACK * (C + HALF):].bitcast(F32)
+        for a in (0, HALF):
+            nc.vector.tensor_scalar(
+                spare[:, a:a + HALF], accs[S - C + a][0], bias[:, E - 1:E], 0.0, op0=ALU.add, op1=ALU.max)
+        for a in (0, HALF):
+            nc.vector.tensor_tensor(
+                y[:, S - C + a:S - C + a + HALF], spare[:, a:a + HALF], spare[:, a:a + HALF], ALU.mult)
+
+        total = ring.tile([P, 3, T], F32, name="xg", align_bytes=64)
         for r in range(3):
             for a, z in zip(OUT_CUTS[r], OUT_CUTS[r][1:]):
                 window = y[:].indirect(lists[r][:, a // 16:z // 16])

@@ -52,7 +52,7 @@ def tile_moe_pre_lin_relu2_kernel(tc, xT, w, b, gate, offs, pos1, pos2, pos3, ou
         nc.sync.dma_start(slot_tokens[:], offs)
 
         x_rows = xT.rearrange("(g p j) t -> g j p t", p=P, j=PACK)
-        gates = keep.tile([P, S], F32, name="gates")
+        gates = keep.tile([P, S + 32], F32, name="gates")
         planes = {}
         w_raw = []
 
@@ -74,8 +74,9 @@ def tile_moe_pre_lin_relu2_kernel(tc, xT, w, b, gate, offs, pos1, pos2, pos3, ou
             nc.sync.dma_start(gates[:, a:z], gate[0:P, a:z])
         for j in range(1, PACK):
             load_plane(0, j, nc.sync)
-            load_w(2 * j - 2)
-            load_w(2 * j - 1)
+            load_w(j - 1)
+        for e in range(PACK - 1, EARLY):
+            load_w(e)
         for j in range(PACK):
             load_plane(1, j, nc.sync)
             if EARLY + j < E:

@@ -23,9 +23,9 @@ HALF = C // 2
 QUAD = 4
 WIDE = 4 * C
 SPARE = 8
-HEAD_CUTS = (0, C, 3 * C, 6 * C, S)
+HEAD_CUTS = (0, HALF, 3 * HALF, 7 * HALF, 13 * HALF, S)
 LAST_CUTS = (0, C, C + HALF, 2 * C)
-OUT_CUTS = ((0, 384, T), (0, 384, T), (0, 352, 672, T))
+OUT_CUTS = ((0, 448, T), (0, 448, T), (0, 448, 672, T))
 EARLY = 6
 W_COLS = PASSES * N
 

@@ -49,7 +49,6 @@ def tile_moe_pre_lin_relu2_kernel(tc, xT, w, b, gate, offs, pos1, pos2, pos3, ou
         psum = ctx.enter_context(tc.psum_pool(name="psum", bufs=1))
 
         slot_tokens = keep.tile([P, S // 16], U16, name="slot_tokens")
-        nc.sync.dma_start(slot_tokens[:], offs)
 
         x_rows = xT.rearrange("(g p j) t -> g j p t", p=P, j=PACK)
         gates = keep.tile([P, S + 32], F32, name="gates")
@@ -72,6 +71,8 @@ def tile_moe_pre_lin_relu2_kernel(tc, xT, w, b, gate, offs, pos1, pos2, pos3, ou
         load_plane(0, 0, nc.scalar)
         for a, z in zip(HEAD_CUTS, HEAD_CUTS[1:]):
             nc.sync.dma_start(gates[:, a:z], gate[0:P, a:z])
+            if a == 0:
+                nc.sync.dma_start(slot_tokens[:], offs)
         for j in range(1, PACK):
             load_plane(0, j, nc.sync)
             load_w(j - 1)

@@ -56,10 +56,10 @@ def tile_moe_pre_lin_relu2_kernel(tc, xT, w, b, gate, offs, pos1, pos2, pos3, ou
         w_raw = []
 
         def load_plane(g, j, queue):
-            if g == 2:
-                plane = keep.tile([P, WIDE + SPARE], F32, name=f"plane2_{j}")
+            if g == PASSES - 1:
+                plane = keep.tile([P, WIDE + SPARE], F32, name=f"last_plane{j}")
             else:
-                plane = ring.tile([P, (S if g < 2 else WIDE) + SPARE], F32, name="plane", bufs=PACK)
+                plane = ring.tile([P, S + SPARE], F32, name="plane", bufs=PACK)
             queue.dma_start(plane[:, :T], x_rows[g, j])
             planes[g, j] = plane
 
@@ -83,7 +83,7 @@ def tile_moe_pre_lin_relu2_kernel(tc, xT, w, b, gate, offs, pos1, pos2, pos3, ou
             if EARLY + j < E:
                 load_w(EARLY + j)
         for j in range(PACK):
-            load_plane(2, j, nc.sync)
+            load_plane(3, j, nc.sync)
         bias = keep.tile([P, E], F32, name="bias")
         nc.sync.dma_start(bias[:], b)
         lists = []
@@ -92,7 +92,7 @@ def tile_moe_pre_lin_relu2_kernel(tc, xT, w, b, gate, offs, pos1, pos2, pos3, ou
             nc.sync.dma_start(lst[:], pos)
             lists.append(lst)
         for j in range(PACK):
-            load_plane(3, j, nc.sync)
+            load_plane(2, j, nc.sync)
 
         w_codes = keep.tile([P, E * W_COLS], U32, name="w_codes", align_bytes=64)
         w_scales = keep.tile([P, E * W_COLS], U8, name="w_scales", align_bytes=64)
@@ -137,7 +137,7 @@ def tile_moe_pre_lin_relu2_kernel(tc, xT, w, b, gate, offs, pos1, pos2, pos3, ou
         def square(e0, e1):
             nc.scalar.activation(y[:, e0 * C:e1 * C], y[:, e0 * C:e1 * C], ACT.Square)
 
-        steps = [(0, S, 0), (0, S, 1), (0, 4 * C, 2), (0, 4 * C, 3), (4 * C, 3 * C, 2), (4 * C, 3 * C, 3),
+        steps = [(0, S, 0), (0, S, 1), (0, 7 * C, 2), (0, 4 * C, 3), (4 * C, 3 * C, 3),
                  (7 * C, 2 * C, 2), (7 * C, 2 * C, 3)]
         last_step = len(steps) - 1
 
@@ -198,11 +198,11 @@ def tile_moe_pre_lin_relu2_kernel(tc, xT, w, b, gate, offs, pos1, pos2, pos3, ou
                 prepare_w(EARLY, E, late)
             for args in made:
                 multiply(*args)
-            if c == 4:
+            if c == 3:
                 for e in range(4):
                     bias_relu(e)
                 square(0, 4)
-            if c == 6:
+            if c == 5:
                 for e in range(4, 7):
                     bias_relu(e)
 

@@ -19,6 +19,7 @@ ALU = mybir.AluOpType
 P = 128
 PACK = 4
 PASSES = K // (P * PACK)
+LAST = PASSES - 1
 HALF = C // 2
 QUAD = 4
 WIDE = 4 * C
@@ -30,17 +31,6 @@ EARLY = 6
 W_COLS = PASSES * N
 
 
-def widths(n):
-    out_w = []
-    while n > 0:
-        m = WIDE
-        while m > n:
-            m = m // 2
-        out_w.append(m)
-        n = n - m
-    return out_w
-
-
 def tile_moe_pre_lin_relu2_kernel(tc, xT, w, b, gate, offs, pos1, pos2, pos3, out):
     nc = tc.nc
     with ExitStack() as ctx:
@@ -49,22 +39,18 @@ def tile_moe_pre_lin_relu2_kernel(tc, xT, w, b, gate, offs, pos1, pos2, pos3, ou
         psum = ctx.enter_context(tc.psum_pool(name="psum", bufs=1))
 
         slot_tokens = keep.tile([P, S // 16], U16, name="slot_tokens")
-
         x_rows = xT.rearrange("(g p j) t -> g j p t", p=P, j=PACK)
         gates = keep.tile([P, S + 32], F32, name="gates")
         planes = {}
         w_raw = []
 
         def load_plane(g, j, queue):
-            if g == PASSES - 1:
-                plane = keep.tile([P, WIDE + SPARE], F32, name=f"last_plane{j}")
-            else:
-                plane = ring.tile([P, S + SPARE], F32, name="plane", bufs=PACK)
+            plane = ring.tile([P, (S if g < LAST else 5 * C) + SPARE], F32, name="plane", align_bytes=64, bufs=PACK)
             queue.dma_start(plane[:, :T], x_rows[g, j])
             planes[g, j] = plane
 
         def load_w(e):
-            raw = ring.tile([P, PASSES, PACK, N], F32, name="stage", align_bytes=64, bufs=4)
+            raw = ring.tile([P, PASSES, PACK, N], F32, name="stage", align_bytes=64, bufs=EARLY)
             nc.sync.dma_start(raw[:], w[e].rearrange("(g p j) n -> p g j n", p=P, j=PACK))
             w_raw.append(raw)
 
@@ -73,17 +59,17 @@ def tile_moe_pre_lin_relu2_kernel(tc, xT, w, b, gate, offs, pos1, pos2, pos3, ou
             nc.sync.dma_start(gates[:, a:z], gate[0:P, a:z])
             if a == 0:
                 nc.sync.dma_start(slot_tokens[:], offs)
-        for j in range(1, PACK):
+        for j in range(1, PACK - 1):
             load_plane(0, j, nc.sync)
             load_w(j - 1)
-        for e in range(PACK - 1, EARLY):
+        for e in range(PACK - 2, EARLY - 1):
             load_w(e)
+        load_plane(0, PACK - 1, nc.sync)
+        load_w(EARLY - 1)
         for j in range(PACK):
             load_plane(1, j, nc.sync)
             if EARLY + j < E:
                 load_w(EARLY + j)
-        for j in range(PACK):
-            load_plane(3, j, nc.sync)
         bias = keep.tile([P, E], F32, name="bias")
         nc.sync.dma_start(bias[:], b)
         lists = []
@@ -91,25 +77,31 @@ def tile_moe_pre_lin_relu2_kernel(tc, xT, w, b, gate, offs, pos1, pos2, pos3, ou
             lst = keep.tile([P, T // 16], U16, name=f"pos{r}")
             nc.sync.dma_start(lst[:], pos)
             lists.append(lst)
-        for j in range(PACK):
-            load_plane(2, j, nc.sync)
+        for g in range(2, PASSES):
+            for j in range(PACK):
+                load_plane(g, j, nc.sync)
 
-        w_codes = keep.tile([P, E * W_COLS], U32, name="w_codes", align_bytes=64)
+        w_codes = keep.tile([P, (E - 1) * W_COLS], U32, name="w_codes", align_bytes=64)
         w_scales = keep.tile([P, E * W_COLS], U8, name="w_scales", align_bytes=64)
+        late = keep.tile([P, (E - EARLY) * W_COLS * PACK], BF16, name="late", align_bytes=64)
+        held = keep.tile([P, LAST * C * PACK], BF16, name="held", align_bytes=64)
+        held_scales = keep.tile([P, LAST * C], U8, name="held_scales", align_bytes=64)
         y = keep.tile([P, S], F32, name="y")
+        weights = {}
 
-        def prepare_w(e0, e1, packed):
-            for a in range(e0, e1, 2):
-                z = min(a + 2, e1)
-                for e in range(a, z):
-                    nc.scalar.copy(
-                        packed[:, (e - e0) * W_COLS * PACK:(e - e0 + 1) * W_COLS * PACK].rearrange(
-                            "p (g c i j) -> p g c j i", g=PASSES, i=QUAD, j=PACK),
-                        w_raw[e][:].rearrange("p g j (c i) -> p g c j i", i=QUAD),
-                    )
-                nc.vector.quantize_mx(
-                    out=w_codes[:, a * W_COLS:z * W_COLS].bitcast(FP8X4), scales=w_scales[:, a * W_COLS:z * W_COLS],
-                    in_=packed[:, (a - e0) * W_COLS * PACK:(z - e0) * W_COLS * PACK])
+        def round_w(e, dst):
+            nc.scalar.copy(
+                dst.rearrange("p (g c i j) -> p g c j i", g=PASSES, i=QUAD, j=PACK),
+                w_raw[e][:].rearrange("p g j (c i) -> p g c j i", i=QUAD))
+
+        def quantise(codes, scales, src):
+            nc.vector.quantize_mx(out=codes.bitcast(FP8X4), scales=scales, in_=src)
+
+        def prepare_pair(e, rounded):
+            for i in range(2):
+                round_w(e + i, rounded[:, i * W_COLS * PACK:(i + 1) * W_COLS * PACK])
+                weights[e + i] = w_codes[:, (e + i) * W_COLS:(e + i + 1) * W_COLS]
+            quantise(w_codes[:, e * W_COLS:(e + 2) * W_COLS], w_scales[:, e * W_COLS:(e + 2) * W_COLS], rounded)
 
         banks = [[(0, C), (C, C)], [(2 * C, C), (3 * C, C)]]
         banks = banks + [[(e * C, C)] for e in range(4, E - 1)] + [[(S - C, HALF)], [(S - HALF, HALF)]]
@@ -123,97 +115,109 @@ def tile_moe_pre_lin_relu2_kernel(tc, xT, w, b, gate, offs, pos1, pos2, pos3, ou
             for s0 in sorted(accs):
                 acc, m, opens, closes = accs[s0]
                 if start <= s0 < start + n:
-                    cols = slice((s0 // C * PASSES + g) * N, (s0 // C * PASSES + g + 1) * N)
+                    e = s0 // C
                     nc.tensor.matmul_mx(
                         out=acc,
-                        lhsT=w_codes[:, cols].bitcast(FP8X4), lhsT_scale=w_scales[:, cols],
+                        lhsT=weights[e][:, g * N:(g + 1) * N].bitcast(FP8X4),
+                        lhsT_scale=w_scales[:, e * W_COLS + g * N:e * W_COLS + (g + 1) * N],
                         rhs=codes[:, s0 - start:s0 - start + m].bitcast(FP8X4),
                         rhs_scale=scales[:, s0 - start:s0 - start + m],
-                        start=(g == 0 and opens), stop=(g == PASSES - 1 and closes))
+                        start=(g == 0 and opens), stop=(g == LAST and closes))
 
-        def bias_relu(e):
-            nc.scalar.activation(y[:, e * C:(e + 1) * C], accs[e * C][0], ACT.Relu, bias=bias[:, e:e + 1])
+        def finish(e0, e1):
+            for e in range(e0, e1):
+                nc.scalar.activation(y[:, e * C:(e + 1) * C], accs[e * C][0], ACT.Relu, bias=bias[:, e:e + 1])
+            for e in range(e0, e1, 2):
+                cols = slice(e * C, min(e + 2, e1) * C)
+                nc.scalar.activation(y[:, cols], y[:, cols], ACT.Square)
 
-        def square(e0, e1):
-            nc.scalar.activation(y[:, e0 * C:e1 * C], y[:, e0 * C:e1 * C], ACT.Square)
-
-        steps = [(0, S, 0), (0, S, 1), (0, 7 * C, 2), (0, 4 * C, 3), (4 * C, 3 * C, 3),
-                 (7 * C, 2 * C, 2), (7 * C, 2 * C, 3)]
-        last_step = len(steps) - 1
-
-        def gather(c):
-            start, n, g = steps[c]
+        def gather(g, start, n, cuts):
             xg = ring.tile([P, PACK, n], F32, name="xg", align_bytes=64)
-            if c < last_step:
-                parts = [(j, a, z) for j in range(PACK)
-                         for a, z in (zip(HEAD_CUTS, HEAD_CUTS[1:]) if (c, j) == (0, 0) else ((0, n),))]
-            else:
-                parts = [(j, a, z) for a, z in zip(LAST_CUTS, LAST_CUTS[1:]) for j in range(PACK)]
-            for j, a, z in parts:
-                s0, s1 = start + a, start + z
-                nc.vector.tensor_tensor(
-                    xg[:, j, a:z], planes[g, j][:].indirect(slot_tokens[:, s0 // 16:s1 // 16]),
-                    gates[:, s0:s1], ALU.mult)
+            for j in range(PACK):
+                for a, z in (zip(cuts, cuts[1:]) if j == 0 else ((0, n),)):
+                    s0, s1 = start + a, start + z
+                    nc.vector.tensor_tensor(
+                        xg[:, j, a:z], planes[g, j][:].indirect(slot_tokens[:, s0 // 16:s1 // 16]),
+                        gates[:, s0:s1], ALU.mult)
             return xg
 
         def interleave(dst, src):
             nc.scalar.copy(
                 dst.rearrange("p (c i j) -> p c j i", i=QUAD, j=PACK),
-                src.rearrange("p j (c i) -> p c j i", i=QUAD),
-            )
+                src.rearrange("p j (c i) -> p c j i", i=QUAD))
 
-        def quantise(c, xg):
-            start, n, g = steps[c]
+        def contract(g, start, xg, cuts):
             made = []
-            if c < last_step - 1:
-                a = 0
-                for wd in widths(n):
-                    packed = ring.tile([P, PACK * wd], BF16, name="stage", align_bytes=64, bufs=4)
-                    codes = ring.tile([P, wd], U32, name="x_codes", align_bytes=64, bufs=4)
-                    scales = ring.tile([P, wd], U8, name="x_scales", align_bytes=64, bufs=4)
-                    interleave(packed[:], xg[:, :, a:a + wd])
-                    nc.vector.quantize_mx(out=codes[:].bitcast(FP8X4), scales=scales[:], in_=packed[:])
-                    made.append((g, start + a, wd, codes, scales))
-                    a = a + wd
-                return made, packed
-            packed = ring.tile([P, PACK * n], BF16, name="stage", align_bytes=64, bufs=4)
-            codes = ring.tile([P, n], U32, name="x_codes", align_bytes=64, bufs=4)
-            scales = ring.tile([P, n], U8, name="x_scales", align_bytes=64, bufs=4)
-            cuts = LAST_CUTS if c == last_step else (0, C, n)
             for a, z in zip(cuts, cuts[1:]):
-                interleave(packed[:, PACK * a:PACK * z], xg[:, :, a:z])
-                nc.vector.quantize_mx(
-                    out=codes[:, a:z].bitcast(FP8X4), scales=scales[:, a:z], in_=packed[:, PACK * a:PACK * z])
-            return [(g, start, n, codes, scales)], packed
+                rounded = ring.tile([P, PACK * (z - a)], BF16, name="stage", align_bytes=64, bufs=EARLY)
+                codes = ring.tile([P, z - a], U32, name="x_codes", align_bytes=64, bufs=4)
+                scales = ring.tile([P, z - a], U8, name="x_scales", align_bytes=64, bufs=4)
+                interleave(rounded[:], xg[:, :, a:z])
+                quantise(codes[:], scales[:], rounded[:])
+                made.append((g, start + a, z - a, codes, scales))
+            return made
 
-        gathered = gather(0)
+        groups = ((0, 5 * C), (5 * C, 2 * C), (7 * C, 2 * C))
+
+        gathered = gather(0, 0, S, HEAD_CUTS)
         early = ring.tile([P, EARLY * W_COLS * PACK], BF16, name="xg", align_bytes=64)
-        prepare_w(0, EARLY, early)
-        for c in range(len(steps)):
-            ahead = gather(c + 1) if c < last_step else None
-            made, packed = quantise(c, gathered)
+        for e in range(0, EARLY, 2):
+            prepare_pair(e, early[:, e * W_COLS * PACK:(e + 2) * W_COLS * PACK])
+        for g in range(LAST):
+            n = S if g + 1 < LAST else groups[0][1]
+            ahead = gather(g + 1, 0, n, (0, n))
+            made = contract(g, 0, gathered, (0, WIDE, 2 * WIDE))
+            interleave(held[:, g * C * PACK:(g + 1) * C * PACK], gathered[:, :, S - C:])
             gathered = ahead
-            if c == 0:
-                late = keep.tile([P, (E - EARLY) * W_COLS * PACK], BF16, name="late", align_bytes=64)
-                prepare_w(EARLY, E, late)
+            if g == 0:
+                prepare_pair(EARLY, late[:, :2 * W_COLS * PACK])
+                round_w(E - 1, late[:, 2 * W_COLS * PACK:])
             for args in made:
                 multiply(*args)
-            if c == 3:
-                for e in range(4):
-                    bias_relu(e)
-                square(0, 4)
-            if c == 5:
-                for e in range(4, 7):
-                    bias_relu(e)
 
-        square(4, 7)
-        bias_relu(7)
-        square(7, 8)
+        second = gather(LAST, *groups[1], (0, groups[1][1]))
+        for args in contract(LAST, 0, gathered, (0, WIDE, 5 * C)):
+            multiply(*args)
+        third = gather(LAST, *groups[2], (0, groups[2][1]))
+        made = contract(LAST, groups[1][0], second, (0, 2 * C))
+        finish(0, 5)
+        for args in made:
+            multiply(*args)
 
-        spare = packed[:, PACK * (C + HALF):].bitcast(F32)
+        held_codes = ring.tile([P, W_COLS + LAST * C], U32, name="plane", align_bytes=64, bufs=PACK)
+        weights[E - 1] = held_codes[:, :W_COLS]
+        quantise(weights[E - 1], w_scales[:, (E - 1) * W_COLS:], late[:, 2 * W_COLS * PACK:])
+        start, n = groups[2]
+        rounded = ring.tile([P, PACK * n], BF16, name="stage", align_bytes=64, bufs=EARLY)
+        codes = ring.tile([P, n], U32, name="x_codes", align_bytes=64, bufs=4)
+        scales = ring.tile([P, n], U8, name="x_scales", align_bytes=64, bufs=4)
+
+        def contract_held(g0, g1):
+            quantise(held_codes[:, W_COLS + g0 * C:W_COLS + g1 * C], held_scales[:, g0 * C:g1 * C],
+                     held[:, g0 * C * PACK:g1 * C * PACK])
+            for g in range(g0, g1):
+                multiply(g, S - C, C, held_codes[:, W_COLS + g * C:W_COLS + (g + 1) * C],
+                         held_scales[:, g * C:(g + 1) * C])
+
+        def contract_last(a, z):
+            interleave(rounded[:, PACK * a:PACK * z], third[:, :, a:z])
+            quantise(codes[:, a:z], scales[:, a:z], rounded[:, PACK * a:PACK * z])
+            multiply(LAST, start + a, z - a, codes[:, a:z], scales[:, a:z])
+
+        contract_held(0, 2)
+        contract_last(0, C)
+        contract_held(2, LAST)
+        contract_last(C, C + HALF)
+        contract_last(C + HALF, n)
+        for e in range(5, E - 1):
+            nc.scalar.activation(y[:, e * C:(e + 1) * C], accs[e * C][0], ACT.Relu, bias=bias[:, e:e + 1])
+        nc.scalar.activation(y[:, 5 * C:7 * C], y[:, 5 * C:7 * C], ACT.Square)
+
+        spare = rounded[:, PACK * (C + HALF):].bitcast(F32)
         for a in (0, HALF):
             nc.vector.tensor_scalar(
                 spare[:, a:a + HALF], accs[S - C + a][0], bias[:, E - 1:E], 0.0, op0=ALU.add, op1=ALU.max)
+        nc.vector.tensor_tensor(y[:, start:start + C], y[:, start:start + C], y[:, start:start + C], ALU.mult)
         for a in (0, HALF):
             nc.vector.tensor_tensor(
                 y[:, S - C + a:S - C + a + HALF], spare[:, a:a + HALF], spare[:, a:a + HALF], ALU.mult)

@@ -25,7 +25,6 @@ QUAD = 4
 WIDE = 4 * C
 SPARE = 8
 HEAD_CUTS = (0, HALF, 3 * HALF, 7 * HALF, 13 * HALF, S)
-LAST_CUTS = (0, C, C + HALF, 2 * C)
 OUT_CUTS = ((0, 448, T), (0, 448, T), (0, 448, 672, T))
 EARLY = 6
 W_COLS = PASSES * N
@@ -104,7 +103,7 @@ def tile_moe_pre_lin_relu2_kernel(tc, xT, w, b, gate, offs, pos1, pos2, pos3, ou
             quantise(w_codes[:, e * W_COLS:(e + 2) * W_COLS], w_scales[:, e * W_COLS:(e + 2) * W_COLS], rounded)
 
         banks = [[(0, C), (C, C)], [(2 * C, C), (3 * C, C)]]
-        banks = banks + [[(e * C, C)] for e in range(4, E - 1)] + [[(S - C, HALF)], [(S - HALF, HALF)]]
+        banks = banks + [[(e * C, C)] for e in (4, 5, 6, 8)] + [[(7 * C, HALF)], [(7 * C + HALF, HALF)]]
         accs = {}
         for i, sums in enumerate(banks):
             bank = psum.tile([N, sum(m for s0, m in sums)], F32, name=f"bank{i}")
@@ -131,10 +130,11 @@ def tile_moe_pre_lin_relu2_kernel(tc, xT, w, b, gate, offs, pos1, pos2, pos3, ou
                 cols = slice(e * C, min(e + 2, e1) * C)
                 nc.scalar.activation(y[:, cols], y[:, cols], ACT.Square)
 
-        def gather(g, start, n, cuts):
+        def gather(g, start, n, first_cuts, last_cuts):
             xg = ring.tile([P, PACK, n], F32, name="xg", align_bytes=64)
             for j in range(PACK):
-                for a, z in (zip(cuts, cuts[1:]) if j == 0 else ((0, n),)):
+                cuts = first_cuts if j == 0 else last_cuts if j == PACK - 1 else [(0, n)]
+                for a, z in cuts:
                     s0, s1 = start + a, start + z
                     nc.vector.tensor_tensor(
                         xg[:, j, a:z], planes[g, j][:].indirect(slot_tokens[:, s0 // 16:s1 // 16]),
@@ -159,13 +159,13 @@ def tile_moe_pre_lin_relu2_kernel(tc, xT, w, b, gate, offs, pos1, pos2, pos3, ou
 
         groups = ((0, 5 * C), (5 * C, 2 * C), (7 * C, 2 * C))
 
-        gathered = gather(0, 0, S, HEAD_CUTS)
+        gathered = gather(0, 0, S, list(zip(HEAD_CUTS, HEAD_CUTS[1:])), [(0, S)])
         early = ring.tile([P, EARLY * W_COLS * PACK], BF16, name="xg", align_bytes=64)
         for e in range(0, EARLY, 2):
             prepare_pair(e, early[:, e * W_COLS * PACK:(e + 2) * W_COLS * PACK])
         for g in range(LAST):
             n = S if g + 1 < LAST else groups[0][1]
-            ahead = gather(g + 1, 0, n, (0, n))
+            ahead = gather(g + 1, 0, n, [(0, n)], [(0, n)])
             made = contract(g, 0, gathered, (0, WIDE, 2 * WIDE))
             interleave(held[:, g * C * PACK:(g + 1) * C * PACK], gathered[:, :, S - C:])
             gathered = ahead
@@ -175,10 +175,10 @@ def tile_moe_pre_lin_relu2_kernel(tc, xT, w, b, gate, offs, pos1, pos2, pos3, ou
             for args in made:
                 multiply(*args)
 
-        second = gather(LAST, *groups[1], (0, groups[1][1]))
+        second = gather(LAST, *groups[1], [(0, 2 * C)], [(0, 2 * C)])
         for args in contract(LAST, 0, gathered, (0, WIDE, 5 * C)):
             multiply(*args)
-        third = gather(LAST, *groups[2], (0, groups[2][1]))
+        third = gather(LAST, *groups[2], [(0, 2 * C)], [(C, 2 * C), (0, C)])
         made = contract(LAST, groups[1][0], second, (0, 2 * C))
         finish(0, 5)
         for args in made:
@@ -204,23 +204,24 @@ def tile_moe_pre_lin_relu2_kernel(tc, xT, w, b, gate, offs, pos1, pos2, pos3, ou
             quantise(codes[:, a:z], scales[:, a:z], rounded[:, PACK * a:PACK * z])
             multiply(LAST, start + a, z - a, codes[:, a:z], scales[:, a:z])
 
-        contract_held(0, 2)
-        contract_last(0, C)
-        contract_held(2, LAST)
-        contract_last(C, C + HALF)
-        contract_last(C + HALF, n)
-        for e in range(5, E - 1):
+        for g in range(LAST):
+            contract_held(g, g + 1)
+        contract_last(C, n)
+        contract_last(0, HALF)
+        contract_last(HALF, C)
+        for e in (5, 6, 8):
             nc.scalar.activation(y[:, e * C:(e + 1) * C], accs[e * C][0], ACT.Relu, bias=bias[:, e:e + 1])
-        nc.scalar.activation(y[:, 5 * C:7 * C], y[:, 5 * C:7 * C], ACT.Square)
+        nc.vector.tensor_tensor(y[:, 5 * C:6 * C], y[:, 5 * C:6 * C], y[:, 5 * C:6 * C], ALU.mult)
+        for e in (6, 8):
+            nc.scalar.activation(y[:, e * C:(e + 1) * C], y[:, e * C:(e + 1) * C], ACT.Square)
 
-        spare = rounded[:, PACK * (C + HALF):].bitcast(F32)
+        spare = rounded[:, PACK * HALF:PACK * C].bitcast(F32)
         for a in (0, HALF):
             nc.vector.tensor_scalar(
-                spare[:, a:a + HALF], accs[S - C + a][0], bias[:, E - 1:E], 0.0, op0=ALU.add, op1=ALU.max)
-        nc.vector.tensor_tensor(y[:, start:start + C], y[:, start:start + C], y[:, start:start + C], ALU.mult)
+                spare[:, a:a + HALF], accs[start + a][0], bias[:, 7:8], 0.0, op0=ALU.add, op1=ALU.max)
         for a in (0, HALF):
             nc.vector.tensor_tensor(
-                y[:, S - C + a:S - C + a + HALF], spare[:, a:a + HALF], spare[:, a:a + HALF], ALU.mult)
+                y[:, start + a:start + a + HALF], spare[:, a:a + HALF], spare[:, a:a + HALF], ALU.mult)
 
         total = ring.tile([P, 3, T], F32, name="xg", align_bytes=64)
         for r in range(3):

@@ -102,8 +102,8 @@ def tile_moe_pre_lin_relu2_kernel(tc, xT, w, b, gate, offs, pos1, pos2, pos3, ou
                 weights[e + i] = w_codes[:, (e + i) * W_COLS:(e + i + 1) * W_COLS]
             quantise(w_codes[:, e * W_COLS:(e + 2) * W_COLS], w_scales[:, e * W_COLS:(e + 2) * W_COLS], rounded)
 
-        banks = [[(0, C), (C, C)], [(2 * C, C), (3 * C, C)]]
-        banks = banks + [[(e * C, C)] for e in (4, 5, 6, 8)] + [[(7 * C, HALF)], [(7 * C + HALF, HALF)]]
+        banks = [[(0, C), (C, C)], [(2 * C, C), (3 * C, C)], [(5 * C, C), (6 * C, C)]]
+        banks = banks + [[(e * C, C)] for e in (4, 8)] + [[(7 * C, HALF)], [(7 * C + HALF, HALF)]]
         accs = {}
         for i, sums in enumerate(banks):
             bank = psum.tile([N, sum(m for s0, m in sums)], F32, name=f"bank{i}")
@@ -130,15 +130,17 @@ def tile_moe_pre_lin_relu2_kernel(tc, xT, w, b, gate, offs, pos1, pos2, pos3, ou
                 cols = slice(e * C, min(e + 2, e1) * C)
                 nc.scalar.activation(y[:, cols], y[:, cols], ACT.Square)
 
-        def gather(g, start, n, first_cuts, last_cuts):
+        def gather_plane(xg, g, j, start, cuts):
+            for a, z in cuts:
+                s0, s1 = start + a, start + z
+                nc.vector.tensor_tensor(
+                    xg[:, j, a:z], planes[g, j][:].indirect(slot_tokens[:, s0 // 16:s1 // 16]),
+                    gates[:, s0:s1], ALU.mult)
+
+        def gather(g, start, n, first_cuts, rows=PACK):
             xg = ring.tile([P, PACK, n], F32, name="xg", align_bytes=64)
-            for j in range(PACK):
-                cuts = first_cuts if j == 0 else last_cuts if j == PACK - 1 else [(0, n)]
-                for a, z in cuts:
-                    s0, s1 = start + a, start + z
-                    nc.vector.tensor_tensor(
-                        xg[:, j, a:z], planes[g, j][:].indirect(slot_tokens[:, s0 // 16:s1 // 16]),
-                        gates[:, s0:s1], ALU.mult)
+            for j in range(rows):
+                gather_plane(xg, g, j, start, first_cuts if j == 0 else [(0, n)])
             return xg
 
         def interleave(dst, src):
@@ -159,13 +161,13 @@ def tile_moe_pre_lin_relu2_kernel(tc, xT, w, b, gate, offs, pos1, pos2, pos3, ou
 
         groups = ((0, 5 * C), (5 * C, 2 * C), (7 * C, 2 * C))
 
-        gathered = gather(0, 0, S, list(zip(HEAD_CUTS, HEAD_CUTS[1:])), [(0, S)])
+        gathered = gather(0, 0, S, list(zip(HEAD_CUTS, HEAD_CUTS[1:])))
         early = ring.tile([P, EARLY * W_COLS * PACK], BF16, name="xg", align_bytes=64)
         for e in range(0, EARLY, 2):
             prepare_pair(e, early[:, e * W_COLS * PACK:(e + 2) * W_COLS * PACK])
         for g in range(LAST):
             n = S if g + 1 < LAST else groups[0][1]
-            ahead = gather(g + 1, 0, n, [(0, n)], [(0, n)])
+            ahead = gather(g + 1, 0, n, [(0, n)])
             made = contract(g, 0, gathered, (0, WIDE, 2 * WIDE))
             interleave(held[:, g * C * PACK:(g + 1) * C * PACK], gathered[:, :, S - C:])
             gathered = ahead
@@ -175,12 +177,20 @@ def tile_moe_pre_lin_relu2_kernel(tc, xT, w, b, gate, offs, pos1, pos2, pos3, ou
             for args in made:
                 multiply(*args)
 
-        second = gather(LAST, *groups[1], [(0, 2 * C)], [(0, 2 * C)])
-        for args in contract(LAST, 0, gathered, (0, WIDE, 5 * C)):
+        second = gather(LAST, *groups[1], [(0, 2 * C)])
+        for args in contract(LAST, 0, gathered, (0, WIDE)):
             multiply(*args)
-        third = gather(LAST, *groups[2], [(0, 2 * C)], [(C, 2 * C), (0, C)])
+        fifth = ring.tile([P, PACK * C], BF16, name="stage", align_bytes=64, bufs=EARLY)
+        interleave(fifth[:], gathered[:, :, WIDE:])
+        third = gather(LAST, *groups[2], [(0, 2 * C)], PACK - 1)
+        fifth_codes = ring.tile([P, C], U32, name="x_codes", align_bytes=64, bufs=4)
+        fifth_scales = ring.tile([P, C], U8, name="x_scales", align_bytes=64, bufs=4)
+        quantise(fifth_codes[:], fifth_scales[:], fifth[:])
+        multiply(LAST, WIDE, C, fifth_codes, fifth_scales)
+        gather_plane(third, LAST, PACK - 1, groups[2][0], [(C, 2 * C), (0, C)])
         made = contract(LAST, groups[1][0], second, (0, 2 * C))
-        finish(0, 5)
+        finish(0, 4)
+        nc.scalar.activation(y[:, 4 * C:5 * C], accs[4 * C][0], ACT.Relu, bias=bias[:, 4:5])
         for args in made:
             multiply(*args)
 
@@ -209,8 +219,10 @@ def tile_moe_pre_lin_relu2_kernel(tc, xT, w, b, gate, offs, pos1, pos2, pos3, ou
         contract_last(C, n)
         contract_last(0, HALF)
         contract_last(HALF, C)
-        for e in (5, 6, 8):
+        for e in (5, 6):
             nc.scalar.activation(y[:, e * C:(e + 1) * C], accs[e * C][0], ACT.Relu, bias=bias[:, e:e + 1])
+        nc.scalar.activation(y[:, 4 * C:5 * C], y[:, 4 * C:5 * C], ACT.Square)
+        nc.scalar.activation(y[:, 8 * C:], accs[8 * C][0], ACT.Relu, bias=bias[:, 8:])
         nc.vector.tensor_tensor(y[:, 5 * C:6 * C], y[:, 5 * C:6 * C], y[:, 5 * C:6 * C], ALU.mult)
         for e in (6, 8):
             nc.scalar.activation(y[:, e * C:(e + 1) * C], y[:, e * C:(e + 1) * C], ACT.Square)

@@ -187,6 +187,12 @@ def tile_moe_pre_lin_relu2_kernel(tc, xT, w, b, gate, offs, pos1, pos2, pos3, ou
         fifth_scales = ring.tile([P, C], U8, name="x_scales", align_bytes=64, bufs=4)
         quantise(fifth_codes[:], fifth_scales[:], fifth[:])
         multiply(LAST, WIDE, C, fifth_codes, fifth_scales)
+        unread = psum.tile([N, 2 * C], F32, name="unread")
+        for i in range(3):
+            nc.tensor.matmul_mx(
+                out=unread[:], lhsT=fifth_codes[:, :N].bitcast(FP8X4), lhsT_scale=fifth_scales[:, :N],
+                rhs=weights[i].bitcast(FP8X4), rhs_scale=w_scales[:, i * W_COLS:(i + 1) * W_COLS],
+                start=True, stop=True)
         gather_plane(third, LAST, PACK - 1, groups[2][0], [(C, 2 * C), (0, C)])
         made = contract(LAST, groups[1][0], second, (0, 2 * C))
         finish(0, 4)

@@ -83,8 +83,8 @@ def tile_moe_pre_lin_relu2_kernel(tc, xT, w, b, gate, offs, pos1, pos2, pos3, ou
         w_codes = keep.tile([P, (E - 1) * W_COLS], U32, name="w_codes", align_bytes=64)
         w_scales = keep.tile([P, E * W_COLS], U8, name="w_scales", align_bytes=64)
         late = keep.tile([P, (E - EARLY) * W_COLS * PACK], BF16, name="late", align_bytes=64)
-        held = keep.tile([P, LAST * C * PACK], BF16, name="held", align_bytes=64)
-        held_scales = keep.tile([P, LAST * C], U8, name="held_scales", align_bytes=64)
+        held = keep.tile([P, PASSES * C * PACK], BF16, name="held", align_bytes=64)
+        held_scales = keep.tile([P, PASSES * C], U8, name="held_scales", align_bytes=64)
         y = keep.tile([P, S], F32, name="y")
         weights = {}
 
@@ -168,8 +168,12 @@ def tile_moe_pre_lin_relu2_kernel(tc, xT, w, b, gate, offs, pos1, pos2, pos3, ou
         for g in range(LAST):
             n = S if g + 1 < LAST else groups[0][1]
             ahead = gather(g + 1, 0, n, [(0, n)])
-            made = contract(g, 0, gathered, (0, WIDE, 2 * WIDE))
-            interleave(held[:, g * C * PACK:(g + 1) * C * PACK], gathered[:, :, S - C:])
+            if g + 1 < LAST:
+                made = contract(g, 0, gathered, (0, WIDE, 2 * WIDE))
+                interleave(held[:, g * C * PACK:(g + 1) * C * PACK], gathered[:, :, S - C:])
+            else:
+                made = contract(g, 0, gathered, (0, WIDE, 6 * C, 7 * C))
+                interleave(held[:, g * C * PACK:], gathered[:, :, S - 2 * C:])
             gathered = ahead
             if g == 0:
                 prepare_pair(EARLY, late[:, :2 * W_COLS * PACK])
@@ -200,7 +204,7 @@ def tile_moe_pre_lin_relu2_kernel(tc, xT, w, b, gate, offs, pos1, pos2, pos3, ou
         for args in made:
             multiply(*args)
 
-        held_codes = ring.tile([P, W_COLS + LAST * C], U32, name="plane", align_bytes=64, bufs=PACK)
+        held_codes = ring.tile([P, W_COLS + PASSES * C], U32, name="plane", align_bytes=64, bufs=PACK)
         weights[E - 1] = held_codes[:, :W_COLS]
         quantise(weights[E - 1], w_scales[:, (E - 1) * W_COLS:], late[:, 2 * W_COLS * PACK:])
         start, n = groups[2]
@@ -208,20 +212,18 @@ def tile_moe_pre_lin_relu2_kernel(tc, xT, w, b, gate, offs, pos1, pos2, pos3, ou
         codes = ring.tile([P, n], U32, name="x_codes", align_bytes=64, bufs=4)
         scales = ring.tile([P, n], U8, name="x_scales", align_bytes=64, bufs=4)
 
-        def contract_held(g0, g1):
-            quantise(held_codes[:, W_COLS + g0 * C:W_COLS + g1 * C], held_scales[:, g0 * C:g1 * C],
-                     held[:, g0 * C * PACK:g1 * C * PACK])
-            for g in range(g0, g1):
-                multiply(g, S - C, C, held_codes[:, W_COLS + g * C:W_COLS + (g + 1) * C],
-                         held_scales[:, g * C:(g + 1) * C])
+        def contract_held(i, g, e):
+            cols = slice(i * C, (i + 1) * C)
+            quantise(held_codes[:, W_COLS:][:, cols], held_scales[:, cols], held[:, i * C * PACK:(i + 1) * C * PACK])
+            multiply(g, e * C, C, held_codes[:, W_COLS:][:, cols], held_scales[:, cols])
 
         def contract_last(a, z):
             interleave(rounded[:, PACK * a:PACK * z], third[:, :, a:z])
             quantise(codes[:, a:z], scales[:, a:z], rounded[:, PACK * a:PACK * z])
             multiply(LAST, start + a, z - a, codes[:, a:z], scales[:, a:z])
 
-        for g in range(LAST):
-            contract_held(g, g + 1)
+        for i, (g, e) in enumerate(((0, 8), (1, 8), (2, 7), (2, 8))):
+            contract_held(i, g, e)
         contract_last(C, n)
         contract_last(0, HALF)
         contract_last(HALF, C)

@@ -26,7 +26,8 @@ WIDE = 4 * C
 SPARE = 8
 HEAD_CUTS = (0, HALF, 3 * HALF, 7 * HALF, 13 * HALF, S)
 OUT_CUTS = ((0, 448, T), (0, 448, T), (0, 448, 672, T))
-EARLY = 6
+EARLY = 4
+MIDDLE = 6
 W_COLS = PASSES * N
 
 
@@ -49,7 +50,7 @@ def tile_moe_pre_lin_relu2_kernel(tc, xT, w, b, gate, offs, pos1, pos2, pos3, ou
             planes[g, j] = plane
 
         def load_w(e):
-            raw = ring.tile([P, PASSES, PACK, N], F32, name="stage", align_bytes=64, bufs=EARLY)
+            raw = ring.tile([P, PASSES, PACK, N], F32, name="stage", align_bytes=64, bufs=MIDDLE)
             nc.sync.dma_start(raw[:], w[e].rearrange("(g p j) n -> p g j n", p=P, j=PACK))
             w_raw.append(raw)
 
@@ -67,8 +68,8 @@ def tile_moe_pre_lin_relu2_kernel(tc, xT, w, b, gate, offs, pos1, pos2, pos3, ou
         load_w(EARLY - 1)
         for j in range(PACK):
             load_plane(1, j, nc.sync)
-            if EARLY + j < E:
-                load_w(EARLY + j)
+            load_w(EARLY + j)
+        load_w(E - 1)
         bias = keep.tile([P, E], F32, name="bias")
         nc.sync.dma_start(bias[:], b)
         lists = []
@@ -82,10 +83,10 @@ def tile_moe_pre_lin_relu2_kernel(tc, xT, w, b, gate, offs, pos1, pos2, pos3, ou
 
         w_codes = keep.tile([P, (E - 1) * W_COLS], U32, name="w_codes", align_bytes=64)
         w_scales = keep.tile([P, E * W_COLS], U8, name="w_scales", align_bytes=64)
-        late = keep.tile([P, (E - EARLY) * W_COLS * PACK], BF16, name="late", align_bytes=64)
+        late = keep.tile([P, (E - MIDDLE) * W_COLS * PACK], BF16, name="late", align_bytes=64)
         held = keep.tile([P, PASSES * C * PACK], BF16, name="held", align_bytes=64)
         held_scales = keep.tile([P, PASSES * C], U8, name="held_scales", align_bytes=64)
-        y = keep.tile([P, S], F32, name="y")
+        y = keep.tile([P, S], F32, name="y", align_bytes=64)
         weights = {}
 
         def round_w(e, dst):
@@ -151,7 +152,7 @@ def tile_moe_pre_lin_relu2_kernel(tc, xT, w, b, gate, offs, pos1, pos2, pos3, ou
         def contract(g, start, xg, cuts):
             made = []
             for a, z in zip(cuts, cuts[1:]):
-                rounded = ring.tile([P, PACK * (z - a)], BF16, name="stage", align_bytes=64, bufs=EARLY)
+                rounded = ring.tile([P, PACK * (z - a)], BF16, name="stage", align_bytes=64, bufs=MIDDLE)
                 codes = ring.tile([P, z - a], U32, name="x_codes", align_bytes=64, bufs=4)
                 scales = ring.tile([P, z - a], U8, name="x_scales", align_bytes=64, bufs=4)
                 interleave(rounded[:], xg[:, :, a:z])
@@ -176,7 +177,8 @@ def tile_moe_pre_lin_relu2_kernel(tc, xT, w, b, gate, offs, pos1, pos2, pos3, ou
                 interleave(held[:, g * C * PACK:], gathered[:, :, S - 2 * C:])
             gathered = ahead
             if g == 0:
-                prepare_pair(EARLY, late[:, :2 * W_COLS * PACK])
+                prepare_pair(EARLY, y[:].bitcast(BF16)[:, :2 * W_COLS * PACK])
+                prepare_pair(MIDDLE, late[:, :2 * W_COLS * PACK])
                 round_w(E - 1, late[:, 2 * W_COLS * PACK:])
             for args in made:
                 multiply(*args)
@@ -184,7 +186,7 @@ def tile_moe_pre_lin_relu2_kernel(tc, xT, w, b, gate, offs, pos1, pos2, pos3, ou
         second = gather(LAST, *groups[1], [(0, 2 * C)])
         for args in contract(LAST, 0, gathered, (0, WIDE)):
             multiply(*args)
-        fifth = ring.tile([P, PACK * C], BF16, name="stage", align_bytes=64, bufs=EARLY)
+        fifth = ring.tile([P, PACK * C], BF16, name="stage", align_bytes=64, bufs=MIDDLE)
         interleave(fifth[:], gathered[:, :, WIDE:])
         third = gather(LAST, *groups[2], [(0, 2 * C)], PACK - 1)
         fifth_codes = ring.tile([P, C], U32, name="x_codes", align_bytes=64, bufs=4)
@@ -208,7 +210,7 @@ def tile_moe_pre_lin_relu2_kernel(tc, xT, w, b, gate, offs, pos1, pos2, pos3, ou
         weights[E - 1] = held_codes[:, :W_COLS]
         quantise(weights[E - 1], w_scales[:, (E - 1) * W_COLS:], late[:, 2 * W_COLS * PACK:])
         start, n = groups[2]
-        rounded = ring.tile([P, PACK * n], BF16, name="stage", align_bytes=64, bufs=EARLY)
+        rounded = ring.tile([P, PACK * n], BF16, name="stage", align_bytes=64, bufs=MIDDLE)
         codes = ring.tile([P, n], U32, name="x_codes", align_bytes=64, bufs=4)
         scales = ring.tile([P, n], U8, name="x_scales", align_bytes=64, bufs=4)
 

@@ -23,12 +23,11 @@ LAST = PASSES - 1
 HALF = C // 2
 QUAD = 4
 WIDE = 4 * C
+OWN = 2 * WIDE
 SPARE = 8
-HEAD_CUTS = (0, HALF, 3 * HALF, 7 * HALF, 13 * HALF, S)
-OUT_CUTS = ((0, 448, T), (0, 448, T), (0, 448, 672, T))
-EARLY = 4
-MIDDLE = 6
-W_COLS = PASSES * N
+W_GROUPS = ((0, 4), (4, 8), (8, 9))
+TAIL_CUTS = (0, 2 * C, 3 * C, 3 * C + HALF, WIDE)
+OUT_CUTS = (0, 160, 512, T)
 
 
 def tile_moe_pre_lin_relu2_kernel(tc, xT, w, b, gate, offs, pos1, pos2, pos3, out):
@@ -40,36 +39,36 @@ def tile_moe_pre_lin_relu2_kernel(tc, xT, w, b, gate, offs, pos1, pos2, pos3, ou
 
         slot_tokens = keep.tile([P, S // 16], U16, name="slot_tokens")
         x_rows = xT.rearrange("(g p j) t -> g j p t", p=P, j=PACK)
-        gates = keep.tile([P, S + 32], F32, name="gates")
+        w_rows = w.rearrange("e (g p j) n -> g p e (j n)", p=P, j=PACK)
+        gates = keep.tile([P, S], F32, name="gates")
         planes = {}
-        w_raw = []
+        w_raw = {}
 
         def load_plane(g, j, queue):
-            plane = ring.tile([P, (S if g < LAST else 5 * C) + SPARE], F32, name="plane", align_bytes=64, bufs=PACK)
+            plane = ring.tile([P, WIDE + SPARE], F32, name="plane", align_bytes=64, bufs=2 * PACK)
             queue.dma_start(plane[:, :T], x_rows[g, j])
             planes[g, j] = plane
 
-        def load_w(e):
-            raw = ring.tile([P, PASSES, PACK, N], F32, name="stage", align_bytes=64, bufs=MIDDLE)
-            nc.sync.dma_start(raw[:], w[e].rearrange("(g p j) n -> p g j n", p=P, j=PACK))
-            w_raw.append(raw)
+        def load_w(g, i):
+            e0, e1 = W_GROUPS[i]
+            raw = ring.tile([P, e1 - e0, PACK * N], F32, name="w_raw", align_bytes=64, bufs=3)
+            nc.sync.dma_start(raw[:], w_rows[g][:, e0:e1])
+            w_raw[g, i] = raw
+
+        def load_gate(a, z):
+            nc.sync.dma_start(gates[:, a:z], gate[0:P, a:z])
 
         load_plane(0, 0, nc.scalar)
-        for a, z in zip(HEAD_CUTS, HEAD_CUTS[1:]):
-            nc.sync.dma_start(gates[:, a:z], gate[0:P, a:z])
-            if a == 0:
-                nc.sync.dma_start(slot_tokens[:], offs)
-        for j in range(1, PACK - 1):
-            load_plane(0, j, nc.sync)
-            load_w(j - 1)
-        for e in range(PACK - 2, EARLY - 1):
-            load_w(e)
-        load_plane(0, PACK - 1, nc.sync)
-        load_w(EARLY - 1)
-        for j in range(PACK):
-            load_plane(1, j, nc.sync)
-            load_w(EARLY + j)
-        load_w(E - 1)
+        nc.sync.dma_start(slot_tokens[:], offs)
+        load_gate(OWN, S)
+        load_plane(0, 1, nc.sync)
+        load_w(0, 0)
+        load_plane(0, 2, nc.sync)
+        load_plane(0, 3, nc.sync)
+        load_w(0, 1)
+        load_gate(0, WIDE)
+        load_w(0, 2)
+        load_gate(WIDE, OWN)
         bias = keep.tile([P, E], F32, name="bias")
         nc.sync.dma_start(bias[:], b)
         lists = []
@@ -77,34 +76,33 @@ def tile_moe_pre_lin_relu2_kernel(tc, xT, w, b, gate, offs, pos1, pos2, pos3, ou
             lst = keep.tile([P, T // 16], U16, name=f"pos{r}")
             nc.sync.dma_start(lst[:], pos)
             lists.append(lst)
-        for g in range(2, PASSES):
+        for g in range(1, PASSES):
             for j in range(PACK):
                 load_plane(g, j, nc.sync)
+            for i in range(len(W_GROUPS)):
+                load_w(g, i)
 
-        w_codes = keep.tile([P, (E - 1) * W_COLS], U32, name="w_codes", align_bytes=64)
-        w_scales = keep.tile([P, E * W_COLS], U8, name="w_scales", align_bytes=64)
-        late = keep.tile([P, (E - MIDDLE) * W_COLS * PACK], BF16, name="late", align_bytes=64)
-        held = keep.tile([P, PASSES * C * PACK], BF16, name="held", align_bytes=64)
-        held_scales = keep.tile([P, PASSES * C], U8, name="held_scales", align_bytes=64)
+        w_codes = [keep.tile([P, E * N], U32, name=f"w_codes{g}", align_bytes=64) for g in range(PASSES)]
+        w_scales = [keep.tile([P, E * N], U8, name=f"w_scales{g}", align_bytes=64) for g in range(PASSES)]
         y = keep.tile([P, S], F32, name="y", align_bytes=64)
-        weights = {}
-
-        def round_w(e, dst):
-            nc.scalar.copy(
-                dst.rearrange("p (g c i j) -> p g c j i", g=PASSES, i=QUAD, j=PACK),
-                w_raw[e][:].rearrange("p g j (c i) -> p g c j i", i=QUAD))
 
         def quantise(codes, scales, src):
             nc.vector.quantize_mx(out=codes.bitcast(FP8X4), scales=scales, in_=src)
 
-        def prepare_pair(e, rounded):
-            for i in range(2):
-                round_w(e + i, rounded[:, i * W_COLS * PACK:(i + 1) * W_COLS * PACK])
-                weights[e + i] = w_codes[:, (e + i) * W_COLS:(e + i + 1) * W_COLS]
-            quantise(w_codes[:, e * W_COLS:(e + 2) * W_COLS], w_scales[:, e * W_COLS:(e + 2) * W_COLS], rounded)
+        def round_w(g, i):
+            e0, e1 = W_GROUPS[i]
+            rounded = ring.tile([P, (e1 - e0) * N * PACK], BF16, name="w_rounded", align_bytes=64, bufs=3)
+            nc.vector.tensor_copy(
+                rounded[:].rearrange("p (e c i j) -> p e c j i", e=e1 - e0, i=QUAD, j=PACK),
+                w_raw[g, i][:].rearrange("p e (j c i) -> p e c j i", j=PACK, i=QUAD))
+            return rounded
 
-        banks = [[(0, C), (C, C)], [(2 * C, C), (3 * C, C)], [(5 * C, C), (6 * C, C)]]
-        banks = banks + [[(e * C, C)] for e in (4, 8)] + [[(7 * C, HALF)], [(7 * C + HALF, HALF)]]
+        def quantise_w(g, i, rounded):
+            e0, e1 = W_GROUPS[i]
+            quantise(w_codes[g][:, e0 * N:e1 * N], w_scales[g][:, e0 * N:e1 * N], rounded[:])
+
+        banks = [[(0, C), (C, C)], [(2 * C, C), (3 * C, C)], [(4 * C, C), (5 * C, C)]]
+        banks = banks + [[(e * C, C)] for e in (6, 8)] + [[(7 * C, HALF)], [(7 * C + HALF, HALF)]]
         accs = {}
         for i, sums in enumerate(banks):
             bank = psum.tile([N, sum(m for s0, m in sums)], F32, name=f"bank{i}")
@@ -118,8 +116,8 @@ def tile_moe_pre_lin_relu2_kernel(tc, xT, w, b, gate, offs, pos1, pos2, pos3, ou
                     e = s0 // C
                     nc.tensor.matmul_mx(
                         out=acc,
-                        lhsT=weights[e][:, g * N:(g + 1) * N].bitcast(FP8X4),
-                        lhsT_scale=w_scales[:, e * W_COLS + g * N:e * W_COLS + (g + 1) * N],
+                        lhsT=w_codes[g][:, e * N:(e + 1) * N].bitcast(FP8X4),
+                        lhsT_scale=w_scales[g][:, e * N:(e + 1) * N],
                         rhs=codes[:, s0 - start:s0 - start + m].bitcast(FP8X4),
                         rhs_scale=scales[:, s0 - start:s0 - start + m],
                         start=(g == 0 and opens), stop=(g == LAST and closes))
@@ -127,131 +125,96 @@ def tile_moe_pre_lin_relu2_kernel(tc, xT, w, b, gate, offs, pos1, pos2, pos3, ou
         def finish(e0, e1):
             for e in range(e0, e1):
                 nc.scalar.activation(y[:, e * C:(e + 1) * C], accs[e * C][0], ACT.Relu, bias=bias[:, e:e + 1])
-            for e in range(e0, e1, 2):
-                cols = slice(e * C, min(e + 2, e1) * C)
-                nc.scalar.activation(y[:, cols], y[:, cols], ACT.Square)
+            nc.scalar.activation(y[:, e0 * C:e1 * C], y[:, e0 * C:e1 * C], ACT.Square)
 
-        def gather_plane(xg, g, j, start, cuts):
-            for a, z in cuts:
-                s0, s1 = start + a, start + z
-                nc.vector.tensor_tensor(
-                    xg[:, j, a:z], planes[g, j][:].indirect(slot_tokens[:, s0 // 16:s1 // 16]),
-                    gates[:, s0:s1], ALU.mult)
-
-        def gather(g, start, n, first_cuts, rows=PACK):
-            xg = ring.tile([P, PACK, n], F32, name="xg", align_bytes=64)
-            for j in range(rows):
-                gather_plane(xg, g, j, start, first_cuts if j == 0 else [(0, n)])
+        def gather(g, start, cuts):
+            xg = ring.tile([P, PACK, WIDE], F32, name="xg", align_bytes=64, bufs=3)
+            for a, z in zip(cuts, cuts[1:]):
+                for j in range(PACK):
+                    picks = slot_tokens[:, (start + a) // 16:(start + z) // 16]
+                    nc.scalar.activation(xg[:, j, a:z], planes[g, j][:].indirect(picks), ACT.Copy)
             return xg
 
-        def interleave(dst, src):
-            nc.scalar.copy(
-                dst.rearrange("p (c i j) -> p c j i", i=QUAD, j=PACK),
-                src.rearrange("p j (c i) -> p c j i", i=QUAD))
+        def gate_round(xg, start, a, z):
+            rounded = ring.tile([P, PACK * (z - a)], BF16, name="x_rounded", align_bytes=64)
+            weights = gates[:, start + a:start + z].rearrange("p (c i) -> p c i", i=QUAD)
+            nc.vector.tensor_tensor(
+                rounded[:].rearrange("p (c i j) -> p c j i", i=QUAD, j=PACK),
+                xg[:, :, a:z].rearrange("p j (c i) -> p c j i", i=QUAD),
+                weights.unsqueeze(2).to_broadcast([P, (z - a) // QUAD, PACK, QUAD]), ALU.mult)
+            return rounded
 
-        def contract(g, start, xg, cuts):
-            made = []
-            for a, z in zip(cuts, cuts[1:]):
-                rounded = ring.tile([P, PACK * (z - a)], BF16, name="stage", align_bytes=64, bufs=MIDDLE)
-                codes = ring.tile([P, z - a], U32, name="x_codes", align_bytes=64, bufs=4)
-                scales = ring.tile([P, z - a], U8, name="x_scales", align_bytes=64, bufs=4)
-                interleave(rounded[:], xg[:, :, a:z])
-                quantise(codes[:], scales[:], rounded[:])
-                made.append((g, start + a, z - a, codes, scales))
-            return made
+        def contract(g, start, n, rounded):
+            codes = ring.tile([P, n], U32, name="x_codes", align_bytes=64, bufs=3)
+            scales = ring.tile([P, n], U8, name="x_scales", align_bytes=64, bufs=3)
+            quantise(codes[:], scales[:], rounded[:])
+            multiply(g, start, n, codes, scales)
 
-        groups = ((0, 5 * C), (5 * C, 2 * C), (7 * C, 2 * C))
+        def gather_own(g):
+            xo = ring.tile([P, PACK, C], F32, name="own", align_bytes=64)
+            for j in range(PACK):
+                nc.vector.tensor_tensor(
+                    xo[:, j, :], planes[g, j][:].indirect(slot_tokens[:, OWN // 16:]), gates[:, OWN:], ALU.mult)
+            return xo
 
-        gathered = gather(0, 0, S, list(zip(HEAD_CUTS, HEAD_CUTS[1:])))
-        early = ring.tile([P, EARLY * W_COLS * PACK], BF16, name="xg", align_bytes=64)
-        for e in range(0, EARLY, 2):
-            prepare_pair(e, early[:, e * W_COLS * PACK:(e + 2) * W_COLS * PACK])
+        def round_own(xo):
+            rounded = ring.tile([P, PACK * C], BF16, name="own_rounded", align_bytes=64)
+            nc.vector.tensor_copy(
+                rounded[:].rearrange("p (c i j) -> p c j i", i=QUAD, j=PACK),
+                xo[:].rearrange("p j (c i) -> p c j i", i=QUAD))
+            return rounded
+
+        first = gather(0, 0, (0, WIDE))
+        xo = gather_own(0)
+        made = [round_w(0, i) for i in range(len(W_GROUPS))]
+        own = round_own(xo)
+        for i, rounded in enumerate(made):
+            quantise_w(0, i, rounded)
+        contract(0, OWN, C, own)
         for g in range(LAST):
-            n = S if g + 1 < LAST else groups[0][1]
-            ahead = gather(g + 1, 0, n, [(0, n)])
-            if g + 1 < LAST:
-                made = contract(g, 0, gathered, (0, WIDE, 2 * WIDE))
-                interleave(held[:, g * C * PACK:(g + 1) * C * PACK], gathered[:, :, S - C:])
-            else:
-                made = contract(g, 0, gathered, (0, WIDE, 6 * C, 7 * C))
-                interleave(held[:, g * C * PACK:], gathered[:, :, S - 2 * C:])
-            gathered = ahead
-            if g == 0:
-                prepare_pair(EARLY, y[:].bitcast(BF16)[:, :2 * W_COLS * PACK])
-                prepare_pair(MIDDLE, late[:, :2 * W_COLS * PACK])
-                round_w(E - 1, late[:, 2 * W_COLS * PACK:])
-            for args in made:
-                multiply(*args)
+            second = gather(g, WIDE, (0, WIDE))
+            rounded = gate_round(first, 0, 0, WIDE)
+            made = [round_w(g + 1, 0)]
+            contract(g, 0, WIDE, rounded)
+            made = made + [round_w(g + 1, i) for i in (1, 2)]
+            for i, w_rounded in enumerate(made):
+                quantise_w(g + 1, i, w_rounded)
+            first = gather(g + 1, 0, (0, WIDE))
+            rounded = gate_round(second, WIDE, 0, WIDE)
+            xo = gather_own(g + 1)
+            contract(g, WIDE, WIDE, rounded)
+            contract(g + 1, OWN, C, round_own(xo))
 
-        second = gather(LAST, *groups[1], [(0, 2 * C)])
-        for args in contract(LAST, 0, gathered, (0, WIDE)):
-            multiply(*args)
-        fifth = ring.tile([P, PACK * C], BF16, name="stage", align_bytes=64, bufs=MIDDLE)
-        interleave(fifth[:], gathered[:, :, WIDE:])
-        third = gather(LAST, *groups[2], [(0, 2 * C)], PACK - 1)
-        fifth_codes = ring.tile([P, C], U32, name="x_codes", align_bytes=64, bufs=4)
-        fifth_scales = ring.tile([P, C], U8, name="x_scales", align_bytes=64, bufs=4)
-        quantise(fifth_codes[:], fifth_scales[:], fifth[:])
-        multiply(LAST, WIDE, C, fifth_codes, fifth_scales)
-        unread = psum.tile([N, 2 * C], F32, name="unread")
-        for i in range(3):
-            nc.tensor.matmul_mx(
-                out=unread[:], lhsT=fifth_codes[:, :N].bitcast(FP8X4), lhsT_scale=fifth_scales[:, :N],
-                rhs=weights[i].bitcast(FP8X4), rhs_scale=w_scales[:, i * W_COLS:(i + 1) * W_COLS],
-                start=True, stop=True)
-        gather_plane(third, LAST, PACK - 1, groups[2][0], [(C, 2 * C), (0, C)])
-        made = contract(LAST, groups[1][0], second, (0, 2 * C))
+        second = gather(LAST, WIDE, TAIL_CUTS)
+        pieces = [(first, 0, 0, WIDE)] + [(second, WIDE, a, z) for a, z in zip(TAIL_CUTS, TAIL_CUTS[1:])]
+        rounded = gate_round(*pieces[0])
+        for (xg, start, a, z), ahead in zip(pieces, pieces[1:] + [None]):
+            nxt = gate_round(*ahead) if ahead else None
+            contract(LAST, start + a, z - a, rounded)
+            rounded = nxt
+        finish(8, 9)
         finish(0, 4)
-        nc.scalar.activation(y[:, 4 * C:5 * C], accs[4 * C][0], ACT.Relu, bias=bias[:, 4:5])
-        for args in made:
-            multiply(*args)
-
-        held_codes = ring.tile([P, W_COLS + PASSES * C], U32, name="plane", align_bytes=64, bufs=PACK)
-        weights[E - 1] = held_codes[:, :W_COLS]
-        quantise(weights[E - 1], w_scales[:, (E - 1) * W_COLS:], late[:, 2 * W_COLS * PACK:])
-        start, n = groups[2]
-        rounded = ring.tile([P, PACK * n], BF16, name="stage", align_bytes=64, bufs=MIDDLE)
-        codes = ring.tile([P, n], U32, name="x_codes", align_bytes=64, bufs=4)
-        scales = ring.tile([P, n], U8, name="x_scales", align_bytes=64, bufs=4)
-
-        def contract_held(i, g, e):
-            cols = slice(i * C, (i + 1) * C)
-            quantise(held_codes[:, W_COLS:][:, cols], held_scales[:, cols], held[:, i * C * PACK:(i + 1) * C * PACK])
-            multiply(g, e * C, C, held_codes[:, W_COLS:][:, cols], held_scales[:, cols])
-
-        def contract_last(a, z):
-            interleave(rounded[:, PACK * a:PACK * z], third[:, :, a:z])
-            quantise(codes[:, a:z], scales[:, a:z], rounded[:, PACK * a:PACK * z])
-            multiply(LAST, start + a, z - a, codes[:, a:z], scales[:, a:z])
-
-        for i, (g, e) in enumerate(((0, 8), (1, 8), (2, 7), (2, 8))):
-            contract_held(i, g, e)
-        contract_last(C, n)
-        contract_last(0, HALF)
-        contract_last(HALF, C)
-        for e in (5, 6):
-            nc.scalar.activation(y[:, e * C:(e + 1) * C], accs[e * C][0], ACT.Relu, bias=bias[:, e:e + 1])
-        nc.scalar.activation(y[:, 4 * C:5 * C], y[:, 4 * C:5 * C], ACT.Square)
-        nc.scalar.activation(y[:, 8 * C:], accs[8 * C][0], ACT.Relu, bias=bias[:, 8:])
-        nc.vector.tensor_tensor(y[:, 5 * C:6 * C], y[:, 5 * C:6 * C], y[:, 5 * C:6 * C], ALU.mult)
-        for e in (6, 8):
-            nc.scalar.activation(y[:, e * C:(e + 1) * C], y[:, e * C:(e + 1) * C], ACT.Square)
-
-        spare = rounded[:, PACK * HALF:PACK * C].bitcast(F32)
+        finish(4, 6)
+        finish(6, 7)
+        relu = ring.tile([P, C], F32, name="own", align_bytes=64)
         for a in (0, HALF):
             nc.vector.tensor_scalar(
-                spare[:, a:a + HALF], accs[start + a][0], bias[:, 7:8], 0.0, op0=ALU.add, op1=ALU.max)
-        for a in (0, HALF):
-            nc.vector.tensor_tensor(
-                y[:, start + a:start + a + HALF], spare[:, a:a + HALF], spare[:, a:a + HALF], ALU.mult)
+                relu[:, a:a + HALF], accs[7 * C + a][0], bias[:, 7:8], 0.0, op0=ALU.add, op1=ALU.max)
+        nc.vector.tensor_tensor(y[:, 7 * C:8 * C], relu[:], relu[:], ALU.mult)
 
-        total = ring.tile([P, 3, T], F32, name="xg", align_bytes=64)
-        for r in range(3):
-            for a, z in zip(OUT_CUTS[r], OUT_CUTS[r][1:]):
-                window = y[:].indirect(lists[r][:, a // 16:z // 16])
-                if r == 0:
-                    nc.vector.tensor_copy(total[:, 0, a:z], window)
-                else:
-                    nc.vector.tensor_tensor(total[:, r, a:z], window, total[:, r - 1, a:z], ALU.add)
-                if r == 2:
-                    (nc.sync if z == T or a == 0 else nc.scalar).dma_start(out[:, a:z], total[:, r, a:z])
+        total = ring.tile([P, 4, T], F32, name="xg", align_bytes=64, bufs=3)
+
+        def fetch(r, a, z):
+            return y[:].indirect(lists[r][:, a // 16:z // 16])
+
+        a, z = OUT_CUTS[:2]
+        nc.vector.tensor_copy(total[:, 0, a:z], fetch(0, a, z))
+        nc.vector.tensor_tensor(total[:, 1, a:z], fetch(1, a, z), total[:, 0, a:z], ALU.add)
+        nc.vector.tensor_tensor(total[:, 3, a:z], fetch(2, a, z), total[:, 1, a:z], ALU.add)
+        nc.sync.dma_start(out[:, a:z], total[:, 3, a:z])
+        for a, z in zip(OUT_CUTS[1:], OUT_CUTS[2:]):
+            nc.scalar.activation(total[:, 0, a:z], fetch(0, a, z), ACT.Copy)
+            nc.scalar.activation(total[:, 1, a:z], fetch(1, a, z), ACT.Copy)
+            nc.vector.tensor_tensor(total[:, 2, a:z], fetch(2, a, z), total[:, 0, a:z], ALU.add)
+            nc.vector.tensor_tensor(total[:, 3, a:z], total[:, 2, a:z], total[:, 1, a:z], ALU.add)
+            nc.sync.dma_start(out[:, a:z], total[:, 3, a:z])

@@ -1,6 +1,7 @@
 from contextlib import ExitStack
 
 import concourse.mybir as mybir
+from concourse.masks import make_identity
 
 K, T, E, C, N = 2048, 768, 9, 256, 128
 S = E * C
@@ -19,14 +20,13 @@ ALU = mybir.AluOpType
 P = 128
 PACK = 4
 PASSES = K // (P * PACK)
-LAST = PASSES - 1
 HALF = C // 2
 QUAD = 4
-WIDE = 4 * C
-OWN = 2 * WIDE
+BANK = 512
+WIDE = 2 * BANK
 SPARE = 8
-W_GROUPS = ((0, 4), (4, 8), (8, 9))
-TAIL_CUTS = (0, 2 * C, 3 * C, 3 * C + HALF, WIDE)
+GROUPS = ((0, 5), (5, E))
+FIRST_OWN = 3 * HALF
 OUT_CUTS = (0, 160, 512, T)
 
 
@@ -37,38 +37,49 @@ def tile_moe_pre_lin_relu2_kernel(tc, xT, w, b, gate, offs, pos1, pos2, pos3, ou
         ring = ctx.enter_context(tc.tile_pool(name="ring", bufs=2))
         psum = ctx.enter_context(tc.psum_pool(name="psum", bufs=1))
 
+        steps = [(e0, e1, g) for e0, e1 in GROUPS for g in range(PASSES)]
+        last = len(steps) - 1
+        owns = [FIRST_OWN] + [C] * (last - 1) + [0]
+
         slot_tokens = keep.tile([P, S // 16], U16, name="slot_tokens")
         x_rows = xT.rearrange("(g p j) t -> g j p t", p=P, j=PACK)
         w_rows = w.rearrange("e (g p j) n -> g p e (j n)", p=P, j=PACK)
-        gates = keep.tile([P, S], F32, name="gates")
         planes = {}
         w_raw = {}
 
         def load_plane(g, j, queue):
-            plane = ring.tile([P, WIDE + SPARE], F32, name="plane", align_bytes=64, bufs=2 * PACK)
+            plane = keep.tile([P, WIDE + SPARE], F32, name=f"plane{g}{j}", align_bytes=64)
             queue.dma_start(plane[:, :T], x_rows[g, j])
             planes[g, j] = plane
 
-        def load_w(g, i):
-            e0, e1 = W_GROUPS[i]
+        def load_w(s):
+            e0, e1, g = steps[s]
             raw = ring.tile([P, e1 - e0, PACK * N], F32, name="w_raw", align_bytes=64, bufs=3)
             nc.sync.dma_start(raw[:], w_rows[g][:, e0:e1])
-            w_raw[g, i] = raw
+            w_raw[s] = raw
 
-        def load_gate(a, z):
-            nc.sync.dma_start(gates[:, a:z], gate[0:P, a:z])
+        own_gates = {}
+
+        def load_gate(end, n):
+            tile = keep.tile([P, n], F32, name=f"gate{end}", align_bytes=64)
+            nc.sync.dma_start(tile[:], gate[0:P, end - n:end])
+            own_gates[end] = (tile, n)
 
         load_plane(0, 0, nc.scalar)
         nc.sync.dma_start(slot_tokens[:], offs)
-        load_gate(OWN, S)
+        load_gate(GROUPS[0][1] * C, FIRST_OWN)
         load_plane(0, 1, nc.sync)
-        load_w(0, 0)
+        gate_rows = keep.tile([P, P], F32, name="gate_rows")
+        nc.sync.dma_start(gate_rows[:], gate.rearrange("r (c p) -> (r c) p", p=P)[0:P])
         load_plane(0, 2, nc.sync)
+        load_w(0)
         load_plane(0, 3, nc.sync)
-        load_w(0, 1)
-        load_gate(0, WIDE)
-        load_w(0, 2)
-        load_gate(WIDE, OWN)
+        for g in range(1, PASSES):
+            load_plane(g, 0, nc.sync)
+            load_w(g)
+            for j in range(1, PACK):
+                load_plane(g, j, nc.sync)
+        load_gate(S, C)
         bias = keep.tile([P, E], F32, name="bias")
         nc.sync.dma_start(bias[:], b)
         lists = []
@@ -76,133 +87,211 @@ def tile_moe_pre_lin_relu2_kernel(tc, xT, w, b, gate, offs, pos1, pos2, pos3, ou
             lst = keep.tile([P, T // 16], U16, name=f"pos{r}")
             nc.sync.dma_start(lst[:], pos)
             lists.append(lst)
-        for g in range(1, PASSES):
-            for j in range(PACK):
-                load_plane(g, j, nc.sync)
-            for i in range(len(W_GROUPS)):
-                load_w(g, i)
+        for s in range(PASSES, len(steps)):
+            load_w(s)
 
-        w_codes = [keep.tile([P, E * N], U32, name=f"w_codes{g}", align_bytes=64) for g in range(PASSES)]
-        w_scales = [keep.tile([P, E * N], U8, name=f"w_scales{g}", align_bytes=64) for g in range(PASSES)]
+        identity = keep.tile([P, P], F32, name="identity")
+        make_identity(nc, identity[:])
+        turned = psum.tile([P, BANK], F32, name="bank7")
+        nc.tensor.transpose(turned[:, :P], gate_rows[:], identity[:])
+        gate_cols = keep.tile([P, S // P], F32, name="gate_cols")
+        nc.vector.tensor_copy(gate_cols[:], turned[:, :S // P])
+        gate_banks = {}
+        for i, (e0, e1) in enumerate(GROUPS):
+            for h in range(WIDE // BANK):
+                bank = psum.tile([P, BANK], F32, name=f"bank{2 * i + h}")
+                s0 = e0 * C + h * BANK
+                for c in range(BANK // P):
+                    col = s0 // P + c
+                    nc.tensor.transpose(
+                        bank[:, c * P:(c + 1) * P], gate_cols[:, col:col + 1].to_broadcast([P, P]), identity[:])
+                gate_banks[s0] = bank
+
         y = keep.tile([P, S], F32, name="y", align_bytes=64)
+        accs = {}
+        to_go = {}
+
+        def open_banks(banks):
+            for name, sums in banks:
+                bank = psum.tile([N, BANK], F32, name=name)
+                to_go[name] = [PASSES * len(sums)] * 2
+                for s0, m in sums:
+                    accs[s0] = (bank[:, s0 - sums[0][0]:s0 - sums[0][0] + m], m, name)
 
         def quantise(codes, scales, src):
             nc.vector.quantize_mx(out=codes.bitcast(FP8X4), scales=scales, in_=src)
 
-        def round_w(g, i):
-            e0, e1 = W_GROUPS[i]
-            rounded = ring.tile([P, (e1 - e0) * N * PACK], BF16, name="w_rounded", align_bytes=64, bufs=3)
-            nc.vector.tensor_copy(
-                rounded[:].rearrange("p (e c i j) -> p e c j i", e=e1 - e0, i=QUAD, j=PACK),
-                w_raw[g, i][:].rearrange("p e (j c i) -> p e c j i", j=PACK, i=QUAD))
+        w_made = {}
+        x_made = {}
+
+        def staging():
+            rounded = ring.tile([P, PACK * (WIDE + FIRST_OWN + GROUPS[0][1] * N)], BF16, name="rounded",
+                                align_bytes=64, bufs=1)
+            return rounded[:, :PACK * WIDE], rounded[:, PACK * WIDE:PACK * (WIDE + FIRST_OWN)], \
+                rounded[:, PACK * (WIDE + FIRST_OWN):]
+
+        def weights_of(s, room):
+            e0, e1, g = steps[s]
+            rounded = room[:, :(e1 - e0) * N * PACK]
+            codes = ring.tile([P, (e1 - e0) * N], U32, name="w_codes", align_bytes=64, bufs=3)
+            scales = ring.tile([P, (e1 - e0) * N], U8, name="w_scales", align_bytes=64, bufs=3)
+            w_made[s] = (codes, scales)
             return rounded
 
-        def quantise_w(g, i, rounded):
-            e0, e1 = W_GROUPS[i]
-            quantise(w_codes[g][:, e0 * N:e1 * N], w_scales[g][:, e0 * N:e1 * N], rounded[:])
+        def quantise_w(s, rounded, a, z):
+            codes, scales = w_made[s]
+            quantise(codes[:, a * N:z * N], scales[:, a * N:z * N], rounded[:, a * N * PACK:z * N * PACK])
 
-        banks = [[(0, C), (C, C)], [(2 * C, C), (3 * C, C)], [(4 * C, C), (5 * C, C)]]
-        banks = banks + [[(e * C, C)] for e in (6, 8)] + [[(7 * C, HALF)], [(7 * C + HALF, HALF)]]
-        accs = {}
-        for i, sums in enumerate(banks):
-            bank = psum.tile([N, sum(m for s0, m in sums)], F32, name=f"bank{i}")
-            for s0, m in sums:
-                accs[s0] = (bank[:, s0 - sums[0][0]:s0 - sums[0][0] + m], m, s0 == sums[0][0], s0 == sums[-1][0])
+        def tokens_of(s):
+            e0, e1, g = steps[s]
+            codes = ring.tile([P, (e1 - e0) * C], U32, name="x_codes", align_bytes=64, bufs=3)
+            scales = ring.tile([P, (e1 - e0) * C], U8, name="x_scales", align_bytes=64, bufs=3)
+            x_made[s] = (codes, scales)
 
-        def multiply(g, start, n, codes, scales):
+        def quantise_x(s, a, z, src):
+            codes, scales = x_made[s]
+            quantise(codes[:, a:z], scales[:, a:z], src)
+
+        def multiply(s, a, z):
+            e0, e1, g = steps[s]
+            x_codes, x_scales = x_made[s]
+            w_codes, w_scales = w_made[s]
             for s0 in sorted(accs):
-                acc, m, opens, closes = accs[s0]
-                if start <= s0 < start + n:
-                    e = s0 // C
+                acc, m, name = accs[s0]
+                c0 = s0 - e0 * C
+                if a <= c0 < z:
+                    n0 = c0 // C * N
+                    total, left = to_go[name]
+                    to_go[name] = [total, left - 1]
                     nc.tensor.matmul_mx(
                         out=acc,
-                        lhsT=w_codes[g][:, e * N:(e + 1) * N].bitcast(FP8X4),
-                        lhsT_scale=w_scales[g][:, e * N:(e + 1) * N],
-                        rhs=codes[:, s0 - start:s0 - start + m].bitcast(FP8X4),
-                        rhs_scale=scales[:, s0 - start:s0 - start + m],
-                        start=(g == 0 and opens), stop=(g == LAST and closes))
+                        lhsT=w_codes[:, n0:n0 + N].bitcast(FP8X4), lhsT_scale=w_scales[:, n0:n0 + N],
+                        rhs=x_codes[:, c0:c0 + m].bitcast(FP8X4), rhs_scale=x_scales[:, c0:c0 + m],
+                        start=(left == total), stop=(left == 1))
 
-        def finish(e0, e1):
-            for e in range(e0, e1):
-                nc.scalar.activation(y[:, e * C:(e + 1) * C], accs[e * C][0], ACT.Relu, bias=bias[:, e:e + 1])
-            nc.scalar.activation(y[:, e0 * C:e1 * C], y[:, e0 * C:e1 * C], ACT.Square)
+        def relu(s0):
+            acc, m, name = accs[s0]
+            nc.scalar.activation(y[:, s0:s0 + m], acc, ACT.Relu, bias=bias[:, s0 // C:s0 // C + 1])
 
-        def gather(g, start, cuts):
-            xg = ring.tile([P, PACK, WIDE], F32, name="xg", align_bytes=64, bufs=3)
+        def square(a, z):
+            nc.scalar.activation(y[:, a:z], y[:, a:z], ACT.Square)
+
+        def gather(s, cuts):
+            e0, e1, g = steps[s]
+            xg = ring.tile([P, PACK, WIDE], F32, name="xg", align_bytes=64)
             for a, z in zip(cuts, cuts[1:]):
                 for j in range(PACK):
-                    picks = slot_tokens[:, (start + a) // 16:(start + z) // 16]
+                    picks = slot_tokens[:, (e0 * C + a) // 16:(e0 * C + z) // 16]
                     nc.scalar.activation(xg[:, j, a:z], planes[g, j][:].indirect(picks), ACT.Copy)
             return xg
 
-        def gate_round(xg, start, a, z):
-            rounded = ring.tile([P, PACK * (z - a)], BF16, name="x_rounded", align_bytes=64)
-            weights = gates[:, start + a:start + z].rearrange("p (c i) -> p c i", i=QUAD)
+        def gate_round(s, rounded, xg, a, z):
+            h = a // BANK * BANK
+            weights = gate_banks[steps[s][0] * C + h][:, a - h:z - h].rearrange("p (c i) -> p c i", i=QUAD)
             nc.vector.tensor_tensor(
-                rounded[:].rearrange("p (c i j) -> p c j i", i=QUAD, j=PACK),
+                rounded[:, PACK * a:PACK * z].rearrange("p (c i j) -> p c j i", i=QUAD, j=PACK),
                 xg[:, :, a:z].rearrange("p j (c i) -> p c j i", i=QUAD),
                 weights.unsqueeze(2).to_broadcast([P, (z - a) // QUAD, PACK, QUAD]), ALU.mult)
-            return rounded
 
-        def contract(g, start, n, rounded):
-            codes = ring.tile([P, n], U32, name="x_codes", align_bytes=64, bufs=3)
-            scales = ring.tile([P, n], U8, name="x_scales", align_bytes=64, bufs=3)
-            quantise(codes[:], scales[:], rounded[:])
-            multiply(g, start, n, codes, scales)
+        def gather_own(s, xo, j):
+            e0, e1, g = steps[s]
+            end, n = e1 * C, owns[s]
+            tile, held = own_gates[end]
+            nc.vector.tensor_tensor(
+                xo[:, j, :], planes[g, j][:].indirect(slot_tokens[:, (end - n) // 16:end // 16]),
+                tile[:, held - n:], ALU.mult)
 
-        def gather_own(g):
-            xo = ring.tile([P, PACK, C], F32, name="own", align_bytes=64)
-            for j in range(PACK):
-                nc.vector.tensor_tensor(
-                    xo[:, j, :], planes[g, j][:].indirect(slot_tokens[:, OWN // 16:]), gates[:, OWN:], ALU.mult)
-            return xo
-
-        def round_own(xo):
-            rounded = ring.tile([P, PACK * C], BF16, name="own_rounded", align_bytes=64)
+        def interleave(dst, src):
             nc.vector.tensor_copy(
-                rounded[:].rearrange("p (c i j) -> p c j i", i=QUAD, j=PACK),
-                xo[:].rearrange("p j (c i) -> p c j i", i=QUAD))
-            return rounded
+                dst.rearrange("p (c i j) -> p c j i", i=QUAD, j=PACK),
+                src.rearrange("p j (c i) -> p c j i", i=QUAD))
 
-        first = gather(0, 0, (0, WIDE))
-        xo = gather_own(0)
-        made = [round_w(0, i) for i in range(len(W_GROUPS))]
-        own = round_own(xo)
-        for i, rounded in enumerate(made):
-            quantise_w(0, i, rounded)
-        contract(0, OWN, C, own)
-        for g in range(LAST):
-            second = gather(g, WIDE, (0, WIDE))
-            rounded = gate_round(first, 0, 0, WIDE)
-            made = [round_w(g + 1, 0)]
-            contract(g, 0, WIDE, rounded)
-            made = made + [round_w(g + 1, i) for i in (1, 2)]
-            for i, w_rounded in enumerate(made):
-                quantise_w(g + 1, i, w_rounded)
-            first = gather(g + 1, 0, (0, WIDE))
-            rounded = gate_round(second, WIDE, 0, WIDE)
-            xo = gather_own(g + 1)
-            contract(g, WIDE, WIDE, rounded)
-            contract(g + 1, OWN, C, round_own(xo))
+        def finish_own(s, xo, w_rounded, room):
+            e0, e1, g = steps[s]
+            width = (e1 - e0) * C
+            cut = 2 * ((e1 - e0) // 2) if (e1 - e0) % 2 else (e1 - e0) // 2
+            if owns[s]:
+                rounded = room[:, :PACK * owns[s]]
+                interleave(rounded, xo[:])
+            quantise_w(s, w_rounded, 0, cut)
+            if owns[s]:
+                quantise_x(s, width - owns[s], width, rounded)
+            quantise_w(s, w_rounded, cut, e1 - e0)
+            multiply(s, width - owns[s], width)
 
-        second = gather(LAST, WIDE, TAIL_CUTS)
-        pieces = [(first, 0, 0, WIDE)] + [(second, WIDE, a, z) for a, z in zip(TAIL_CUTS, TAIL_CUTS[1:])]
-        rounded = gate_round(*pieces[0])
-        for (xg, start, a, z), ahead in zip(pieces, pieces[1:] + [None]):
-            nxt = gate_round(*ahead) if ahead else None
-            contract(LAST, start + a, z - a, rounded)
-            rounded = nxt
-        finish(8, 9)
-        finish(0, 4)
-        finish(4, 6)
-        finish(6, 7)
-        relu = ring.tile([P, C], F32, name="own", align_bytes=64)
-        for a in (0, HALF):
-            nc.vector.tensor_scalar(
-                relu[:, a:a + HALF], accs[7 * C + a][0], bias[:, 7:8], 0.0, op0=ALU.add, op1=ALU.max)
-        nc.vector.tensor_tensor(y[:, 7 * C:8 * C], relu[:], relu[:], ALU.mult)
+        open_banks([("bank4", [(0, C), (C, C)]), ("bank5", [(2 * C, C), (3 * C, C)]), ("bank6", [(4 * C, C)])])
+        xg = gather(0, (0, GROUPS[0][1] * C - owns[0]))
+        tokens_of(0)
+        xo = ring.tile([P, PACK, owns[0]], F32, name="own", align_bytes=64)
+        for j in range(PACK - 1):
+            gather_own(0, xo, j)
+        rounded, own_room, w_room = staging()
+        w_rounded = weights_of(0, w_room)
+        e0, e1, g = steps[0]
+        for a, z in ((0, e1 - 1), (e1 - 1, e1)):
+            nc.vector.tensor_copy(
+                w_rounded[:, a * N * PACK:z * N * PACK].rearrange(
+                    "p (e c i j) -> p e c j i", e=z - a, i=QUAD, j=PACK),
+                w_raw[0][:, a:z].rearrange("p e (j c i) -> p e c j i", j=PACK, i=QUAD))
+        gather_own(0, xo, PACK - 1)
+        finish_own(0, xo, w_rounded, own_room)
+        xo = ring.tile([P, PACK, C], F32, name="own", align_bytes=64)
+        gather_own(1, xo, 0)
 
-        total = ring.tile([P, 4, T], F32, name="xg", align_bytes=64, bufs=3)
+        tail_cuts = (0, 2 * C, 3 * C, 3 * C + HALF, WIDE)
+        for s in range(last):
+            e0, e1, g = steps[s]
+            n = (e1 - e0) * C - owns[s]
+            f0, f1, h = steps[s + 1]
+            ahead = gather(s + 1, (0, (f1 - f0) * C - owns[s + 1]) if s + 1 < last else tail_cuts)
+            rounded, own_room, w_room = staging()
+            gate_round(s, rounded, xg, 0, BANK)
+            gate_round(s, rounded, xg, BANK, n)
+            w_rounded = weights_of(s + 1, w_room)
+            nc.gpsimd.tensor_scalar(
+                w_rounded.rearrange("p (e n j) -> p e n j", n=N, j=PACK),
+                w_raw[s + 1][:].rearrange("p e (j n) -> p e n j", j=PACK),
+                1.0, 0.0, op0=ALU.mult, op1=ALU.add)
+            tokens_of(s + 1)
+            for j in range(1, PACK if owns[s + 1] else 0):
+                gather_own(s + 1, xo, j)
+            for a, z in ((0, n),) if n == WIDE else ((0, BANK), (BANK, n)):
+                quantise_x(s, a, z, rounded[:, PACK * a:PACK * z])
+            multiply(s, 0, n)
+            if s + 1 == PASSES:
+                open_banks([
+                    ("bank7", [(5 * C, C), (6 * C, C)]), ("bank0", [(7 * C, C), (8 * C, HALF)]),
+                    ("bank1", [(8 * C + HALF, HALF)])])
+            if s == PASSES:
+                for e in range(*GROUPS[0]):
+                    relu(e * C)
+                square(0, GROUPS[0][1] * C)
+            finish_own(s + 1, xo, w_rounded, own_room)
+            if s + 2 < last:
+                xo = ring.tile([P, PACK, C], F32, name="own", align_bytes=64)
+                gather_own(s + 2, xo, 0)
+            xg = ahead
+
+        rounded = staging()[0]
+        pieces = list(zip(tail_cuts, tail_cuts[1:]))
+        gate_round(last, rounded, xg, *pieces[0])
+        for (a, z), ahead in zip(pieces, pieces[1:] + [None]):
+            if ahead:
+                gate_round(last, rounded, xg, *ahead)
+            quantise_x(last, a, z, rounded[:, PACK * a:PACK * z])
+            multiply(last, a, z)
+        relu(5 * C)
+        relu(6 * C)
+        square(5 * C, 7 * C)
+        relu(7 * C)
+        relu(8 * C)
+        square(7 * C, 8 * C + HALF)
+        positive = ring.tile([P, HALF], F32, name="own", align_bytes=64)
+        nc.vector.tensor_scalar(
+            positive[:], accs[8 * C + HALF][0], bias[:, E - 1:], 0.0, op0=ALU.add, op1=ALU.max)
+        nc.vector.tensor_tensor(y[:, S - HALF:], positive[:], positive[:], ALU.mult)
+
+        total = ring.tile([P, 4, T], F32, name="xg", align_bytes=64)
 
         def fetch(r, a, z):
             return y[:].indirect(lists[r][:, a // 16:z // 16])

@@ -26,7 +26,9 @@ BANK = 512
 WIDE = 2 * BANK
 SPARE = 8
 GROUPS = ((0, 5), (5, E))
-FIRST_OWN = 3 * HALF
+OWNS = (448, 256, 256, 256, 192, 192, 288, 0)
+SHARE = HALF
+MOST = GROUPS[0][1] * C
 OUT_CUTS = (0, 160, 512, T)
 
 
@@ -39,7 +41,8 @@ def tile_moe_pre_lin_relu2_kernel(tc, xT, w, b, gate, offs, pos1, pos2, pos3, ou
 
         steps = [(e0, e1, g) for e0, e1 in GROUPS for g in range(PASSES)]
         last = len(steps) - 1
-        owns = [FIRST_OWN] + [C] * (last - 1) + [0]
+        owns = OWNS
+        shares = [SHARE] * (last - 1) + [0]
 
         slot_tokens = keep.tile([P, S // 16], U16, name="slot_tokens")
         x_rows = xT.rearrange("(g p j) t -> g j p t", p=P, j=PACK)
@@ -58,28 +61,28 @@ def tile_moe_pre_lin_relu2_kernel(tc, xT, w, b, gate, offs, pos1, pos2, pos3, ou
             nc.sync.dma_start(raw[:], w_rows[g][:, e0:e1])
             w_raw[s] = raw
 
-        own_gates = {}
+        shared_gates = {}
 
-        def load_gate(end, n):
-            tile = keep.tile([P, n], F32, name=f"gate{end}", align_bytes=64)
-            nc.sync.dma_start(tile[:], gate[0:P, end - n:end])
-            own_gates[end] = (tile, n)
+        def load_gate(end):
+            tile = keep.tile([P, SHARE], F32, name=f"gate{end}", align_bytes=64)
+            nc.sync.dma_start(tile[:], gate[0:P, end - SHARE:end])
+            shared_gates[end] = tile
 
         load_plane(0, 0, nc.scalar)
         nc.sync.dma_start(slot_tokens[:], offs)
-        load_gate(GROUPS[0][1] * C, FIRST_OWN)
         load_plane(0, 1, nc.sync)
         gate_rows = keep.tile([P, P], F32, name="gate_rows")
         nc.sync.dma_start(gate_rows[:], gate.rearrange("r (c p) -> (r c) p", p=P)[0:P])
         load_plane(0, 2, nc.sync)
         load_w(0)
         load_plane(0, 3, nc.sync)
+        load_gate(MOST)
         for g in range(1, PASSES):
             load_plane(g, 0, nc.sync)
             load_w(g)
             for j in range(1, PACK):
                 load_plane(g, j, nc.sync)
-        load_gate(S, C)
+        load_gate(S)
         bias = keep.tile([P, E], F32, name="bias")
         nc.sync.dma_start(bias[:], b)
         lists = []
@@ -97,15 +100,14 @@ def tile_moe_pre_lin_relu2_kernel(tc, xT, w, b, gate, offs, pos1, pos2, pos3, ou
         gate_cols = keep.tile([P, S // P], F32, name="gate_cols")
         nc.vector.tensor_copy(gate_cols[:], turned[:, :S // P])
         gate_banks = {}
-        for i, (e0, e1) in enumerate(GROUPS):
-            for h in range(WIDE // BANK):
-                bank = psum.tile([P, BANK], F32, name=f"bank{2 * i + h}")
-                s0 = e0 * C + h * BANK
-                for c in range(BANK // P):
-                    col = s0 // P + c
-                    nc.tensor.transpose(
-                        bank[:, c * P:(c + 1) * P], gate_cols[:, col:col + 1].to_broadcast([P, P]), identity[:])
-                gate_banks[s0] = bank
+        for name, s0, n in (("bank0", 0, BANK), ("bank1", BANK, BANK), ("bank7", WIDE, MOST - SHARE - WIDE),
+                            ("bank2", MOST, BANK), ("bank3", MOST + BANK, BANK)):
+            bank = psum.tile([P, BANK], F32, name=name)
+            for c in range(n // P):
+                col = s0 // P + c
+                nc.tensor.transpose(
+                    bank[:, c * P:(c + 1) * P], gate_cols[:, col:col + 1].to_broadcast([P, P]), identity[:])
+            gate_banks[s0] = bank
 
         y = keep.tile([P, S], F32, name="y", align_bytes=64)
         accs = {}
@@ -125,10 +127,8 @@ def tile_moe_pre_lin_relu2_kernel(tc, xT, w, b, gate, offs, pos1, pos2, pos3, ou
         x_made = {}
 
         def staging():
-            rounded = ring.tile([P, PACK * (WIDE + FIRST_OWN + GROUPS[0][1] * N)], BF16, name="rounded",
-                                align_bytes=64, bufs=1)
-            return rounded[:, :PACK * WIDE], rounded[:, PACK * WIDE:PACK * (WIDE + FIRST_OWN)], \
-                rounded[:, PACK * (WIDE + FIRST_OWN):]
+            rounded = ring.tile([P, PACK * (MOST + GROUPS[0][1] * N)], BF16, name="rounded", align_bytes=64, bufs=1)
+            return rounded[:, :PACK * MOST], rounded[:, PACK * MOST:]
 
         def weights_of(s, room):
             e0, e1, g = steps[s]
@@ -178,11 +178,15 @@ def tile_moe_pre_lin_relu2_kernel(tc, xT, w, b, gate, offs, pos1, pos2, pos3, ou
 
         def gather(s, cuts):
             e0, e1, g = steps[s]
-            xg = ring.tile([P, PACK, WIDE], F32, name="xg", align_bytes=64)
+            xg = ring.tile([P, PACK, MOST], F32, name="xg", align_bytes=64)
             for a, z in zip(cuts, cuts[1:]):
                 for j in range(PACK):
                     picks = slot_tokens[:, (e0 * C + a) // 16:(e0 * C + z) // 16]
                     nc.scalar.activation(xg[:, j, a:z], planes[g, j][:].indirect(picks), ACT.Copy)
+            a, z = cuts[-1], (e1 - e0) * C
+            for j in range(PACK if z > a else 0):
+                picks = slot_tokens[:, (e0 * C + a) // 16:(e0 * C + z) // 16]
+                nc.vector.tensor_copy(xg[:, j, a:z], planes[g, j][:].indirect(picks))
             return xg
 
         def gate_round(s, rounded, xg, a, z):
@@ -193,85 +197,54 @@ def tile_moe_pre_lin_relu2_kernel(tc, xT, w, b, gate, offs, pos1, pos2, pos3, ou
                 xg[:, :, a:z].rearrange("p j (c i) -> p c j i", i=QUAD),
                 weights.unsqueeze(2).to_broadcast([P, (z - a) // QUAD, PACK, QUAD]), ALU.mult)
 
-        def gather_own(s, xo, j):
-            e0, e1, g = steps[s]
-            end, n = e1 * C, owns[s]
-            tile, held = own_gates[end]
-            nc.vector.tensor_tensor(
-                xo[:, j, :], planes[g, j][:].indirect(slot_tokens[:, (end - n) // 16:end // 16]),
-                tile[:, held - n:], ALU.mult)
-
-        def interleave(dst, src):
-            nc.vector.tensor_copy(
-                dst.rearrange("p (c i j) -> p c j i", i=QUAD, j=PACK),
-                src.rearrange("p j (c i) -> p c j i", i=QUAD))
-
-        def finish_own(s, xo, w_rounded, room):
-            e0, e1, g = steps[s]
-            width = (e1 - e0) * C
-            cut = 2 * ((e1 - e0) // 2) if (e1 - e0) % 2 else (e1 - e0) // 2
-            if owns[s]:
-                rounded = room[:, :PACK * owns[s]]
-                interleave(rounded, xo[:])
-            quantise_w(s, w_rounded, 0, cut)
-            if owns[s]:
-                quantise_x(s, width - owns[s], width, rounded)
-            quantise_w(s, w_rounded, cut, e1 - e0)
-            multiply(s, width - owns[s], width)
-
         open_banks([("bank4", [(0, C), (C, C)]), ("bank5", [(2 * C, C), (3 * C, C)]), ("bank6", [(4 * C, C)])])
-        xg = gather(0, (0, GROUPS[0][1] * C - owns[0]))
-        tokens_of(0)
-        xo = ring.tile([P, PACK, owns[0]], F32, name="own", align_bytes=64)
-        for j in range(PACK - 1):
-            gather_own(0, xo, j)
-        rounded, own_room, w_room = staging()
-        w_rounded = weights_of(0, w_room)
+        xg = gather(0, (0, MOST - owns[0]))
+        w_rounded = weights_of(0, staging()[1])
         e0, e1, g = steps[0]
         for a, z in ((0, e1 - 1), (e1 - 1, e1)):
             nc.vector.tensor_copy(
                 w_rounded[:, a * N * PACK:z * N * PACK].rearrange(
                     "p (e c i j) -> p e c j i", e=z - a, i=QUAD, j=PACK),
                 w_raw[0][:, a:z].rearrange("p e (j c i) -> p e c j i", j=PACK, i=QUAD))
-        gather_own(0, xo, PACK - 1)
-        finish_own(0, xo, w_rounded, own_room)
-        xo = ring.tile([P, PACK, C], F32, name="own", align_bytes=64)
-        gather_own(1, xo, 0)
+        for a, z in ((0, e1 - 1), (e1 - 1, e1)):
+            quantise_w(0, w_rounded, a, z)
 
         tail_cuts = (0, 2 * C, 3 * C, 3 * C + HALF, WIDE)
         for s in range(last):
             e0, e1, g = steps[s]
-            n = (e1 - e0) * C - owns[s]
+            n = (e1 - e0) * C
             f0, f1, h = steps[s + 1]
             ahead = gather(s + 1, (0, (f1 - f0) * C - owns[s + 1]) if s + 1 < last else tail_cuts)
-            rounded, own_room, w_room = staging()
-            gate_round(s, rounded, xg, 0, BANK)
-            gate_round(s, rounded, xg, BANK, n)
+            rounded, w_room = staging()
+            mine = n - shares[s]
+            for a in range(0, mine, BANK):
+                gate_round(s, rounded, xg, a, min(a + BANK, mine))
             w_rounded = weights_of(s + 1, w_room)
             nc.gpsimd.tensor_scalar(
                 w_rounded.rearrange("p (e n j) -> p e n j", n=N, j=PACK),
                 w_raw[s + 1][:].rearrange("p e (j n) -> p e n j", j=PACK),
                 1.0, 0.0, op0=ALU.mult, op1=ALU.add)
-            tokens_of(s + 1)
-            for j in range(1, PACK if owns[s + 1] else 0):
-                gather_own(s + 1, xo, j)
-            for a, z in ((0, n),) if n == WIDE else ((0, BANK), (BANK, n)):
-                quantise_x(s, a, z, rounded[:, PACK * a:PACK * z])
-            multiply(s, 0, n)
-            if s + 1 == PASSES:
+            if shares[s]:
+                nc.gpsimd.tensor_tensor(
+                    rounded[:, PACK * mine:PACK * n].rearrange("p (c j) -> p c j", j=PACK),
+                    xg[:, :, mine:n].rearrange("p j c -> p c j"),
+                    shared_gates[e1 * C][:].unsqueeze(2).to_broadcast([P, SHARE, PACK]), ALU.mult)
+            tokens_of(s)
+            for a in range(0, f1 - f0, PACK):
+                quantise_w(s + 1, w_rounded, a, min(a + PACK, f1 - f0))
+            for a in range(0, n, WIDE):
+                quantise_x(s, a, min(a + WIDE, n), rounded[:, PACK * a:PACK * min(a + WIDE, n)])
+            if s == PASSES:
                 open_banks([
                     ("bank7", [(5 * C, C), (6 * C, C)]), ("bank0", [(7 * C, C), (8 * C, HALF)]),
                     ("bank1", [(8 * C + HALF, HALF)])])
-            if s == PASSES:
                 for e in range(*GROUPS[0]):
                     relu(e * C)
-                square(0, GROUPS[0][1] * C)
-            finish_own(s + 1, xo, w_rounded, own_room)
-            if s + 2 < last:
-                xo = ring.tile([P, PACK, C], F32, name="own", align_bytes=64)
-                gather_own(s + 2, xo, 0)
+                square(0, MOST)
+            multiply(s, 0, n)
             xg = ahead
 
+        tokens_of(last)
         rounded = staging()[0]
         pieces = list(zip(tail_cuts, tail_cuts[1:]))
         gate_round(last, rounded, xg, *pieces[0])
@@ -286,7 +259,7 @@ def tile_moe_pre_lin_relu2_kernel(tc, xT, w, b, gate, offs, pos1, pos2, pos3, ou
         relu(7 * C)
         relu(8 * C)
         square(7 * C, 8 * C + HALF)
-        positive = ring.tile([P, HALF], F32, name="own", align_bytes=64)
+        positive = keep.tile([P, HALF], F32, name="positive", align_bytes=64)
         nc.vector.tensor_scalar(
             positive[:], accs[8 * C + HALF][0], bias[:, E - 1:], 0.0, op0=ALU.add, op1=ALU.max)
         nc.vector.tensor_tensor(y[:, S - HALF:], positive[:], positive[:], ALU.mult)

@@ -26,10 +26,10 @@ BANK = 512
 WIDE = 2 * BANK
 SPARE = 8
 GROUPS = ((0, 5), (5, E))
-OWNS = (448, 256, 256, 256, 192, 192, 288, 0)
-SHARE = HALF
+OWNS = (576, 256, 256, 256, 224, 224, 224, 0)
+SHARES = (256, 256, 256, 256, 160, 160, 0)
 MOST = GROUPS[0][1] * C
-OUT_CUTS = (0, 160, 512, T)
+OUT_CUTS = (0, 96, 224, 544, T)
 
 
 def tile_moe_pre_lin_relu2_kernel(tc, xT, w, b, gate, offs, pos1, pos2, pos3, out):
@@ -42,7 +42,7 @@ def tile_moe_pre_lin_relu2_kernel(tc, xT, w, b, gate, offs, pos1, pos2, pos3, ou
         steps = [(e0, e1, g) for e0, e1 in GROUPS for g in range(PASSES)]
         last = len(steps) - 1
         owns = OWNS
-        shares = [SHARE] * (last - 1) + [0]
+        shares = SHARES
 
         slot_tokens = keep.tile([P, S // 16], U16, name="slot_tokens")
         x_rows = xT.rearrange("(g p j) t -> g j p t", p=P, j=PACK)
@@ -63,9 +63,9 @@ def tile_moe_pre_lin_relu2_kernel(tc, xT, w, b, gate, offs, pos1, pos2, pos3, ou
 
         shared_gates = {}
 
-        def load_gate(end):
-            tile = keep.tile([P, SHARE], F32, name=f"gate{end}", align_bytes=64)
-            nc.sync.dma_start(tile[:], gate[0:P, end - SHARE:end])
+        def load_gate(end, n):
+            tile = keep.tile([P, n], F32, name=f"gate{end}", align_bytes=64)
+            nc.sync.dma_start(tile[:], gate[0:P, end - n:end])
             shared_gates[end] = tile
 
         load_plane(0, 0, nc.scalar)
@@ -74,15 +74,15 @@ def tile_moe_pre_lin_relu2_kernel(tc, xT, w, b, gate, offs, pos1, pos2, pos3, ou
         gate_rows = keep.tile([P, P], F32, name="gate_rows")
         nc.sync.dma_start(gate_rows[:], gate.rearrange("r (c p) -> (r c) p", p=P)[0:P])
         load_plane(0, 2, nc.sync)
-        load_w(0)
         load_plane(0, 3, nc.sync)
-        load_gate(MOST)
+        load_w(0)
+        load_gate(MOST, shares[0])
         for g in range(1, PASSES):
-            load_plane(g, 0, nc.sync)
-            load_w(g)
-            for j in range(1, PACK):
+            for j in range(PACK):
                 load_plane(g, j, nc.sync)
-        load_gate(S)
+                if j == 1:
+                    load_w(g)
+        load_gate(S, shares[PASSES])
         bias = keep.tile([P, E], F32, name="bias")
         nc.sync.dma_start(bias[:], b)
         lists = []
@@ -100,7 +100,7 @@ def tile_moe_pre_lin_relu2_kernel(tc, xT, w, b, gate, offs, pos1, pos2, pos3, ou
         gate_cols = keep.tile([P, S // P], F32, name="gate_cols")
         nc.vector.tensor_copy(gate_cols[:], turned[:, :S // P])
         gate_banks = {}
-        for name, s0, n in (("bank0", 0, BANK), ("bank1", BANK, BANK), ("bank7", WIDE, MOST - SHARE - WIDE),
+        for name, s0, n in (("bank0", 0, BANK), ("bank1", BANK, BANK),
                             ("bank2", MOST, BANK), ("bank3", MOST + BANK, BANK)):
             bank = psum.tile([P, BANK], F32, name=name)
             for c in range(n // P):
@@ -228,7 +228,7 @@ def tile_moe_pre_lin_relu2_kernel(tc, xT, w, b, gate, offs, pos1, pos2, pos3, ou
                 nc.gpsimd.tensor_tensor(
                     rounded[:, PACK * mine:PACK * n].rearrange("p (c j) -> p c j", j=PACK),
                     xg[:, :, mine:n].rearrange("p j c -> p c j"),
-                    shared_gates[e1 * C][:].unsqueeze(2).to_broadcast([P, SHARE, PACK]), ALU.mult)
+                    shared_gates[e1 * C][:].unsqueeze(2).to_broadcast([P, shares[s], PACK]), ALU.mult)
             tokens_of(s)
             for a in range(0, f1 - f0, PACK):
                 quantise_w(s + 1, w_rounded, a, min(a + PACK, f1 - f0))
@@ -236,11 +236,12 @@ def tile_moe_pre_lin_relu2_kernel(tc, xT, w, b, gate, offs, pos1, pos2, pos3, ou
                 quantise_x(s, a, min(a + WIDE, n), rounded[:, PACK * a:PACK * min(a + WIDE, n)])
             if s == PASSES:
                 open_banks([
-                    ("bank7", [(5 * C, C), (6 * C, C)]), ("bank0", [(7 * C, C), (8 * C, HALF)]),
+                    ("bank7", [(5 * C, C), (6 * C, C)]), ("bank0", [(8 * C, HALF)]),
                     ("bank1", [(8 * C + HALF, HALF)])])
                 for e in range(*GROUPS[0]):
                     relu(e * C)
                 square(0, MOST)
+                open_banks([("bank4", [(7 * C, C)])])
             multiply(s, 0, n)
             xg = ahead
 
@@ -253,12 +254,11 @@ def tile_moe_pre_lin_relu2_kernel(tc, xT, w, b, gate, offs, pos1, pos2, pos3, ou
                 gate_round(last, rounded, xg, *ahead)
             quantise_x(last, a, z, rounded[:, PACK * a:PACK * z])
             multiply(last, a, z)
-        relu(5 * C)
-        relu(6 * C)
-        square(5 * C, 7 * C)
-        relu(7 * C)
+        for e in (5, 6, 7):
+            relu(e * C)
+        square(5 * C, 8 * C)
         relu(8 * C)
-        square(7 * C, 8 * C + HALF)
+        square(8 * C, 8 * C + HALF)
         positive = keep.tile([P, HALF], F32, name="positive", align_bytes=64)
         nc.vector.tensor_scalar(
             positive[:], accs[8 * C + HALF][0], bias[:, E - 1:], 0.0, op0=ALU.add, op1=ALU.max)
@@ -269,14 +269,28 @@ def tile_moe_pre_lin_relu2_kernel(tc, xT, w, b, gate, offs, pos1, pos2, pos3, ou
         def fetch(r, a, z):
             return y[:].indirect(lists[r][:, a // 16:z // 16])
 
-        a, z = OUT_CUTS[:2]
-        nc.vector.tensor_copy(total[:, 0, a:z], fetch(0, a, z))
-        nc.vector.tensor_tensor(total[:, 1, a:z], fetch(1, a, z), total[:, 0, a:z], ALU.add)
-        nc.vector.tensor_tensor(total[:, 3, a:z], fetch(2, a, z), total[:, 1, a:z], ALU.add)
-        nc.sync.dma_start(out[:, a:z], total[:, 3, a:z])
-        for a, z in zip(OUT_CUTS[1:], OUT_CUTS[2:]):
-            nc.scalar.activation(total[:, 0, a:z], fetch(0, a, z), ACT.Copy)
-            nc.scalar.activation(total[:, 1, a:z], fetch(1, a, z), ACT.Copy)
-            nc.vector.tensor_tensor(total[:, 2, a:z], fetch(2, a, z), total[:, 0, a:z], ALU.add)
-            nc.vector.tensor_tensor(total[:, 3, a:z], total[:, 2, a:z], total[:, 1, a:z], ALU.add)
-            nc.sync.dma_start(out[:, a:z], total[:, 3, a:z])
+        def first(r, a, z):
+            nc.scalar.activation(total[:, r, a:z], fetch(r, a, z), ACT.Copy)
+
+        def add_fetched(r, onto, a, z):
+            nc.vector.tensor_tensor(total[:, r + 1, a:z], fetch(r, a, z), total[:, onto, a:z], ALU.add)
+
+        def add_second(a, z):
+            nc.vector.tensor_tensor(total[:, 2, a:z], total[:, 3, a:z], total[:, 1, a:z], ALU.add)
+            nc.sync.dma_start(out[:, a:z], total[:, 2, a:z])
+
+        parts = list(zip(OUT_CUTS, OUT_CUTS[1:]))
+        once, twice = parts[:2], parts[2:]
+        for a, z in parts:
+            first(0, a, z)
+        for a, z in twice:
+            first(1, a, z)
+        for a, z in once:
+            add_fetched(1, 0, a, z)
+        for a, z in once:
+            add_fetched(2, 2, a, z)
+        nc.sync.dma_start(out[:, :once[1][1]], total[:, 3, :once[1][1]])
+        for a, z in twice:
+            add_fetched(2, 0, a, z)
+        for a, z in twice:
+            add_second(a, z)

@@ -226,9 +226,10 @@ def tile_moe_pre_lin_relu2_kernel(tc, xT, w, b, gate, offs, pos1, pos2, pos3, ou
                 1.0, 0.0, op0=ALU.mult, op1=ALU.add)
             if shares[s]:
                 nc.gpsimd.tensor_tensor(
-                    rounded[:, PACK * mine:PACK * n].rearrange("p (c j) -> p c j", j=PACK),
-                    xg[:, :, mine:n].rearrange("p j c -> p c j"),
-                    shared_gates[e1 * C][:].unsqueeze(2).to_broadcast([P, shares[s], PACK]), ALU.mult)
+                    rounded[:, PACK * mine:PACK * n].rearrange("p (c i j) -> p c j i", i=QUAD, j=PACK),
+                    xg[:, :, mine:n].rearrange("p j (c i) -> p c j i", i=QUAD),
+                    shared_gates[e1 * C][:].rearrange("p (c i) -> p c i", i=QUAD).unsqueeze(2).to_broadcast(
+                        [P, shares[s] // QUAD, PACK, QUAD]), ALU.mult)
             tokens_of(s)
             for a in range(0, f1 - f0, PACK):
                 quantise_w(s + 1, w_rounded, a, min(a + PACK, f1 - f0))

@@ -27,7 +27,8 @@ WIDE = 2 * BANK
 SPARE = 8
 GROUPS = ((0, 5), (5, E))
 OWNS = (576, 256, 256, 256, 224, 224, 224, 0)
-SHARES = (256, 256, 256, 256, 160, 160, 0)
+SHARES = (256, 256, 256, 128, 128, 128, 0)
+CHUNKS = (5, 5, 5, 6, 5, 5, 5)
 MOST = GROUPS[0][1] * C
 OUT_CUTS = (0, 96, 224, 544, T)
 
@@ -55,10 +56,16 @@ def tile_moe_pre_lin_relu2_kernel(tc, xT, w, b, gate, offs, pos1, pos2, pos3, ou
             queue.dma_start(plane[:, :T], x_rows[g, j])
             planes[g, j] = plane
 
+        blocks = [(g, e) for e0, e1, g in steps for e in range(e0, e1)]
+        starts = [sum(CHUNKS[:s]) for s in range(len(CHUNKS) + 1)]
+
         def load_w(s):
-            e0, e1, g = steps[s]
-            raw = ring.tile([P, e1 - e0, PACK * N], F32, name="w_raw", align_bytes=64, bufs=3)
-            nc.sync.dma_start(raw[:], w_rows[g][:, e0:e1])
+            chunk = blocks[starts[s]:starts[s + 1]]
+            raw = ring.tile([P, len(chunk), PACK * N], F32, name="w_raw", align_bytes=64, bufs=3)
+            heads = [i for i, (g, e) in enumerate(chunk) if i == 0 or chunk[i - 1] != (g, e - 1)]
+            for a, z in zip(heads, heads[1:] + [len(chunk)]):
+                g, e = chunk[a]
+                nc.sync.dma_start(raw[:, a:z], w_rows[g][:, e:e + z - a])
             w_raw[s] = raw
 
         shared_gates = {}
@@ -75,13 +82,17 @@ def tile_moe_pre_lin_relu2_kernel(tc, xT, w, b, gate, offs, pos1, pos2, pos3, ou
         nc.sync.dma_start(gate_rows[:], gate.rearrange("r (c p) -> (r c) p", p=P)[0:P])
         load_plane(0, 2, nc.sync)
         load_plane(0, 3, nc.sync)
-        load_w(0)
         load_gate(MOST, shares[0])
-        for g in range(1, PASSES):
+        load_plane(1, 0, nc.sync)
+        load_plane(1, 1, nc.sync)
+        load_w(0)
+        load_plane(1, 2, nc.sync)
+        load_plane(1, 3, nc.sync)
+        for g in range(2, PASSES):
             for j in range(PACK):
                 load_plane(g, j, nc.sync)
-                if j == 1:
-                    load_w(g)
+                if j == 0:
+                    load_w(g - 1)
         load_gate(S, shares[PASSES])
         bias = keep.tile([P, E], F32, name="bias")
         nc.sync.dma_start(bias[:], b)
@@ -90,7 +101,7 @@ def tile_moe_pre_lin_relu2_kernel(tc, xT, w, b, gate, offs, pos1, pos2, pos3, ou
             lst = keep.tile([P, T // 16], U16, name=f"pos{r}")
             nc.sync.dma_start(lst[:], pos)
             lists.append(lst)
-        for s in range(PASSES, len(steps)):
+        for s in range(PASSES - 1, last):
             load_w(s)
 
         identity = keep.tile([P, P], F32, name="identity")
@@ -100,7 +111,7 @@ def tile_moe_pre_lin_relu2_kernel(tc, xT, w, b, gate, offs, pos1, pos2, pos3, ou
         gate_cols = keep.tile([P, S // P], F32, name="gate_cols")
         nc.vector.tensor_copy(gate_cols[:], turned[:, :S // P])
         gate_banks = {}
-        for name, s0, n in (("bank0", 0, BANK), ("bank1", BANK, BANK),
+        for name, s0, n in (("bank0", 0, BANK), ("bank1", BANK, BANK), ("bank7", WIDE, MOST - WIDE),
                             ("bank2", MOST, BANK), ("bank3", MOST + BANK, BANK)):
             bank = psum.tile([P, BANK], F32, name=name)
             for c in range(n // P):
@@ -123,24 +134,17 @@ def tile_moe_pre_lin_relu2_kernel(tc, xT, w, b, gate, offs, pos1, pos2, pos3, ou
         def quantise(codes, scales, src):
             nc.vector.quantize_mx(out=codes.bitcast(FP8X4), scales=scales, in_=src)
 
-        w_made = {}
+        w_codes = keep.tile([P, len(blocks) * N], U32, name="w_codes", align_bytes=64)
+        w_scales = keep.tile([P, len(blocks) * N], U8, name="w_scales", align_bytes=64)
         x_made = {}
 
         def staging():
-            rounded = ring.tile([P, PACK * (MOST + GROUPS[0][1] * N)], BF16, name="rounded", align_bytes=64, bufs=1)
+            rounded = ring.tile([P, PACK * (MOST + max(CHUNKS) * N)], BF16, name="rounded", align_bytes=64, bufs=1)
             return rounded[:, :PACK * MOST], rounded[:, PACK * MOST:]
 
-        def weights_of(s, room):
-            e0, e1, g = steps[s]
-            rounded = room[:, :(e1 - e0) * N * PACK]
-            codes = ring.tile([P, (e1 - e0) * N], U32, name="w_codes", align_bytes=64, bufs=3)
-            scales = ring.tile([P, (e1 - e0) * N], U8, name="w_scales", align_bytes=64, bufs=3)
-            w_made[s] = (codes, scales)
-            return rounded
-
         def quantise_w(s, rounded, a, z):
-            codes, scales = w_made[s]
-            quantise(codes[:, a * N:z * N], scales[:, a * N:z * N], rounded[:, a * N * PACK:z * N * PACK])
+            cols = slice((starts[s] + a) * N, (starts[s] + z) * N)
+            quantise(w_codes[:, cols], w_scales[:, cols], rounded[:, a * N * PACK:z * N * PACK])
 
         def tokens_of(s):
             e0, e1, g = steps[s]
@@ -155,12 +159,11 @@ def tile_moe_pre_lin_relu2_kernel(tc, xT, w, b, gate, offs, pos1, pos2, pos3, ou
         def multiply(s, a, z):
             e0, e1, g = steps[s]
             x_codes, x_scales = x_made[s]
-            w_codes, w_scales = w_made[s]
             for s0 in sorted(accs):
                 acc, m, name = accs[s0]
                 c0 = s0 - e0 * C
                 if a <= c0 < z:
-                    n0 = c0 // C * N
+                    n0 = blocks.index((g, s0 // C)) * N
                     total, left = to_go[name]
                     to_go[name] = [total, left - 1]
                     nc.tensor.matmul_mx(
@@ -199,15 +202,6 @@ def tile_moe_pre_lin_relu2_kernel(tc, xT, w, b, gate, offs, pos1, pos2, pos3, ou
 
         open_banks([("bank4", [(0, C), (C, C)]), ("bank5", [(2 * C, C), (3 * C, C)]), ("bank6", [(4 * C, C)])])
         xg = gather(0, (0, MOST - owns[0]))
-        w_rounded = weights_of(0, staging()[1])
-        e0, e1, g = steps[0]
-        for a, z in ((0, e1 - 1), (e1 - 1, e1)):
-            nc.vector.tensor_copy(
-                w_rounded[:, a * N * PACK:z * N * PACK].rearrange(
-                    "p (e c i j) -> p e c j i", e=z - a, i=QUAD, j=PACK),
-                w_raw[0][:, a:z].rearrange("p e (j c i) -> p e c j i", j=PACK, i=QUAD))
-        for a, z in ((0, e1 - 1), (e1 - 1, e1)):
-            quantise_w(0, w_rounded, a, z)
 
         tail_cuts = (0, 2 * C, 3 * C, 3 * C + HALF, WIDE)
         for s in range(last):
@@ -219,22 +213,23 @@ def tile_moe_pre_lin_relu2_kernel(tc, xT, w, b, gate, offs, pos1, pos2, pos3, ou
             mine = n - shares[s]
             for a in range(0, mine, BANK):
                 gate_round(s, rounded, xg, a, min(a + BANK, mine))
-            w_rounded = weights_of(s + 1, w_room)
+            w_rounded = w_room[:, :CHUNKS[s] * N * PACK]
             nc.gpsimd.tensor_scalar(
                 w_rounded.rearrange("p (e n j) -> p e n j", n=N, j=PACK),
-                w_raw[s + 1][:].rearrange("p e (j n) -> p e n j", j=PACK),
+                w_raw[s][:].rearrange("p e (j n) -> p e n j", j=PACK),
                 1.0, 0.0, op0=ALU.mult, op1=ALU.add)
             if shares[s]:
                 nc.gpsimd.tensor_tensor(
                     rounded[:, PACK * mine:PACK * n].rearrange("p (c i j) -> p c j i", i=QUAD, j=PACK),
                     xg[:, :, mine:n].rearrange("p j (c i) -> p c j i", i=QUAD),
-                    shared_gates[e1 * C][:].rearrange("p (c i) -> p c i", i=QUAD).unsqueeze(2).to_broadcast(
+                    shared_gates[e1 * C][:, shares[e0 // GROUPS[0][1] * PASSES] - shares[s]:].rearrange("p (c i) -> p c i", i=QUAD).unsqueeze(2).to_broadcast(
                         [P, shares[s] // QUAD, PACK, QUAD]), ALU.mult)
             tokens_of(s)
-            for a in range(0, f1 - f0, PACK):
-                quantise_w(s + 1, w_rounded, a, min(a + PACK, f1 - f0))
-            for a in range(0, n, WIDE):
-                quantise_x(s, a, min(a + WIDE, n), rounded[:, PACK * a:PACK * min(a + WIDE, n)])
+            quantise_w(s, w_rounded, 0, PACK)
+            quantise_w(s, w_rounded, PACK, CHUNKS[s])
+            for a, z in ((0, n - WIDE), (n - WIDE, n)):
+                if z > a:
+                    quantise_x(s, a, z, rounded[:, PACK * a:PACK * z])
             if s == PASSES:
                 open_banks([
                     ("bank7", [(5 * C, C), (6 * C, C)]), ("bank0", [(8 * C, HALF)]),

@@ -26,11 +26,12 @@ BANK = 512
 WIDE = 2 * BANK
 SPARE = 8
 GROUPS = ((0, 5), (5, E))
-OWNS = (576, 256, 256, 256, 224, 224, 224, 0)
-SHARES = (256, 256, 256, 128, 128, 128, 0)
-CHUNKS = (5, 5, 5, 6, 5, 5, 5)
 MOST = GROUPS[0][1] * C
-OUT_CUTS = (0, 96, 224, 544, T)
+OWN_ROW = 1
+OWNS = (MOST, 992, 992, 992, 640, 640, 640)
+SHARES = (208, 208, 208, 144, 128, 128, 0)
+CHUNKS = (5, 5, 5, 6, 5, 5, 5)
+OUT_CUTS = (0, 256, 576, T)
 
 
 def tile_moe_pre_lin_relu2_kernel(tc, xT, w, b, gate, offs, pos1, pos2, pos3, out):
@@ -52,7 +53,7 @@ def tile_moe_pre_lin_relu2_kernel(tc, xT, w, b, gate, offs, pos1, pos2, pos3, ou
         w_raw = {}
 
         def load_plane(g, j, queue):
-            plane = keep.tile([P, WIDE + SPARE], F32, name=f"plane{g}{j}", align_bytes=64)
+            plane = keep.tile([P, MOST + SPARE], F32, name=f"plane{g}{j}", align_bytes=64)
             queue.dma_start(plane[:, :T], x_rows[g, j])
             planes[g, j] = plane
 
@@ -172,24 +173,37 @@ def tile_moe_pre_lin_relu2_kernel(tc, xT, w, b, gate, offs, pos1, pos2, pos3, ou
                         rhs=x_codes[:, c0:c0 + m].bitcast(FP8X4), rhs_scale=x_scales[:, c0:c0 + m],
                         start=(left == total), stop=(left == 1))
 
-        def relu(s0):
+        def relu(dst, s0):
             acc, m, name = accs[s0]
-            nc.scalar.activation(y[:, s0:s0 + m], acc, ACT.Relu, bias=bias[:, s0 // C:s0 // C + 1])
+            nc.scalar.activation(dst[:, s0:s0 + m], acc, ACT.Relu, bias=bias[:, s0 // C:s0 // C + 1])
 
-        def square(a, z):
-            nc.scalar.activation(y[:, a:z], y[:, a:z], ACT.Square)
+        def square(src, a, z):
+            nc.scalar.activation(y[:, a:z], src[:, a:z], ACT.Square)
 
-        def gather(s, cuts):
+        def picked(s, j, a, z):
             e0, e1, g = steps[s]
+            return planes[g, j][:].indirect(slot_tokens[:, (e0 * C + a) // 16:(e0 * C + z) // 16])
+
+        def gather(s):
+            e0, e1, g = steps[s]
+            n = (e1 - e0) * C
+            xg = ring.tile([P, PACK, MOST], F32, name="xg", align_bytes=64)
+            own_rows = (OWN_ROW, OWN_ROW + 2) if s == 0 else (OWN_ROW,)
+            for j in range(PACK):
+                if j not in own_rows:
+                    nc.scalar.activation(xg[:, j, :n], picked(s, j, 0, n), ACT.Copy)
+            cut = n - owns[s]
+            for j in own_rows:
+                if cut:
+                    nc.scalar.activation(xg[:, j, :cut], picked(s, j, 0, cut), ACT.Copy)
+                nc.vector.tensor_copy(xg[:, j, cut:n], picked(s, j, cut, n))
+            return xg
+
+        def gather_pieces(s, cuts):
             xg = ring.tile([P, PACK, MOST], F32, name="xg", align_bytes=64)
             for a, z in zip(cuts, cuts[1:]):
                 for j in range(PACK):
-                    picks = slot_tokens[:, (e0 * C + a) // 16:(e0 * C + z) // 16]
-                    nc.scalar.activation(xg[:, j, a:z], planes[g, j][:].indirect(picks), ACT.Copy)
-            a, z = cuts[-1], (e1 - e0) * C
-            for j in range(PACK if z > a else 0):
-                picks = slot_tokens[:, (e0 * C + a) // 16:(e0 * C + z) // 16]
-                nc.vector.tensor_copy(xg[:, j, a:z], planes[g, j][:].indirect(picks))
+                    nc.scalar.activation(xg[:, j, a:z], picked(s, j, a, z), ACT.Copy)
             return xg
 
         def gate_round(s, rounded, xg, a, z):
@@ -201,14 +215,13 @@ def tile_moe_pre_lin_relu2_kernel(tc, xT, w, b, gate, offs, pos1, pos2, pos3, ou
                 weights.unsqueeze(2).to_broadcast([P, (z - a) // QUAD, PACK, QUAD]), ALU.mult)
 
         open_banks([("bank4", [(0, C), (C, C)]), ("bank5", [(2 * C, C), (3 * C, C)]), ("bank6", [(4 * C, C)])])
-        xg = gather(0, (0, MOST - owns[0]))
+        xg = gather(0)
 
         tail_cuts = (0, 2 * C, 3 * C, 3 * C + HALF, WIDE)
         for s in range(last):
             e0, e1, g = steps[s]
             n = (e1 - e0) * C
-            f0, f1, h = steps[s + 1]
-            ahead = gather(s + 1, (0, (f1 - f0) * C - owns[s + 1]) if s + 1 < last else tail_cuts)
+            ahead = gather(s + 1) if s + 1 < last else gather_pieces(last, tail_cuts)
             rounded, w_room = staging()
             mine = n - shares[s]
             for a in range(0, mine, BANK):
@@ -234,27 +247,29 @@ def tile_moe_pre_lin_relu2_kernel(tc, xT, w, b, gate, offs, pos1, pos2, pos3, ou
                 open_banks([
                     ("bank7", [(5 * C, C), (6 * C, C)]), ("bank0", [(8 * C, HALF)]),
                     ("bank1", [(8 * C + HALF, HALF)])])
+                early = keep.tile([P, MOST + SPARE], F32, name="plane00", align_bytes=64)
                 for e in range(*GROUPS[0]):
-                    relu(e * C)
-                square(0, MOST)
+                    relu(early, e * C)
                 open_banks([("bank4", [(7 * C, C)])])
             multiply(s, 0, n)
             xg = ahead
 
         tokens_of(last)
-        rounded = staging()[0]
+        rest = staging()[0]
         pieces = list(zip(tail_cuts, tail_cuts[1:]))
-        gate_round(last, rounded, xg, *pieces[0])
-        for (a, z), ahead in zip(pieces, pieces[1:] + [None]):
-            if ahead:
-                gate_round(last, rounded, xg, *ahead)
-            quantise_x(last, a, z, rounded[:, PACK * a:PACK * z])
+        rooms = [y[:].bitcast(BF16)] + [rest] * (len(pieces) - 1)
+        gate_round(last, rooms[0], xg, *pieces[0])
+        for i, (a, z) in enumerate(pieces):
+            if i + 1 < len(pieces):
+                gate_round(last, rooms[i + 1], xg, *pieces[i + 1])
+            quantise_x(last, a, z, rooms[i][:, PACK * a:PACK * z])
             multiply(last, a, z)
+        square(early, 0, MOST)
         for e in (5, 6, 7):
-            relu(e * C)
-        square(5 * C, 8 * C)
-        relu(8 * C)
-        square(8 * C, 8 * C + HALF)
+            relu(y, e * C)
+        square(y, 5 * C, 8 * C)
+        relu(y, 8 * C)
+        square(y, 8 * C, 8 * C + HALF)
         positive = keep.tile([P, HALF], F32, name="positive", align_bytes=64)
         nc.vector.tensor_scalar(
             positive[:], accs[8 * C + HALF][0], bias[:, E - 1:], 0.0, op0=ALU.add, op1=ALU.max)
@@ -265,28 +280,21 @@ def tile_moe_pre_lin_relu2_kernel(tc, xT, w, b, gate, offs, pos1, pos2, pos3, ou
         def fetch(r, a, z):
             return y[:].indirect(lists[r][:, a // 16:z // 16])
 
-        def first(r, a, z):
-            nc.scalar.activation(total[:, r, a:z], fetch(r, a, z), ACT.Copy)
+        def fetch_alone(row, r, a, z):
+            nc.scalar.activation(total[:, row, a:z], fetch(r, a, z), ACT.Copy)
 
-        def add_fetched(r, onto, a, z):
-            nc.vector.tensor_tensor(total[:, r + 1, a:z], fetch(r, a, z), total[:, onto, a:z], ALU.add)
+        def fetch_onto(r, a, z):
+            nc.vector.tensor_tensor(total[:, 2, a:z], fetch(r, a, z), total[:, 0, a:z], ALU.add)
 
-        def add_second(a, z):
-            nc.vector.tensor_tensor(total[:, 2, a:z], total[:, 3, a:z], total[:, 1, a:z], ALU.add)
-            nc.sync.dma_start(out[:, a:z], total[:, 2, a:z])
-
-        parts = list(zip(OUT_CUTS, OUT_CUTS[1:]))
-        once, twice = parts[:2], parts[2:]
-        for a, z in parts:
-            first(0, a, z)
-        for a, z in twice:
-            first(1, a, z)
-        for a, z in once:
-            add_fetched(1, 0, a, z)
-        for a, z in once:
-            add_fetched(2, 2, a, z)
-        nc.sync.dma_start(out[:, :once[1][1]], total[:, 3, :once[1][1]])
-        for a, z in twice:
-            add_fetched(2, 0, a, z)
-        for a, z in twice:
-            add_second(a, z)
+        left, middle, right = zip(OUT_CUTS, OUT_CUTS[1:])
+        fetch_alone(0, 0, *right)
+        fetch_alone(0, 0, *middle)
+        fetch_alone(1, 0, *left)
+        fetch_alone(1, 1, *middle)
+        fetch_alone(1, 1, *right)
+        nc.vector.tensor_copy(total[:, 0, :left[1]], fetch(1, *left))
+        for a, z in (right, left, middle):
+            fetch_onto(2, a, z)
+        for (a, z), queue in ((left, nc.sync), (middle, nc.scalar), (right, nc.sync)):
+            nc.vector.tensor_tensor(total[:, 3, a:z], total[:, 2, a:z], total[:, 1, a:z], ALU.add)
+            queue.dma_start(out[:, a:z], total[:, 3, a:z])

@@ -28,8 +28,8 @@ SPARE = 8
 GROUPS = ((0, 5), (5, E))
 MOST = GROUPS[0][1] * C
 OWN_ROW = 1
-OWNS = (MOST, 992, 992, 992, 640, 640, 640)
-SHARES = (208, 208, 208, 144, 128, 128, 0)
+OWNS = (MOST, 928, 928, 928, 800, 800, 800)
+SHARES = (192, 192, 192, 128, 112, 112, 144)
 CHUNKS = (5, 5, 5, 6, 5, 5, 5)
 OUT_CUTS = (0, 256, 576, T)
 
@@ -94,7 +94,7 @@ def tile_moe_pre_lin_relu2_kernel(tc, xT, w, b, gate, offs, pos1, pos2, pos3, ou
                 load_plane(g, j, nc.sync)
                 if j == 0:
                     load_w(g - 1)
-        load_gate(S, shares[PASSES])
+        load_gate(S, max(shares[PASSES:]))
         bias = keep.tile([P, E], F32, name="bias")
         nc.sync.dma_start(bias[:], b)
         lists = []
@@ -107,6 +107,9 @@ def tile_moe_pre_lin_relu2_kernel(tc, xT, w, b, gate, offs, pos1, pos2, pos3, ou
 
         identity = keep.tile([P, P], F32, name="identity")
         make_identity(nc, identity[:])
+        unread = keep.tile([P, 2], F32, name="unread")
+        nc.vector.memset(unread[:, :1], 0.0)
+        nc.scalar.activation(unread[:, 1:], unread[:, :1], ACT.Copy)
         turned = psum.tile([P, BANK], F32, name="bank7")
         nc.tensor.transpose(turned[:, :P], gate_rows[:], identity[:])
         gate_cols = keep.tile([P, S // P], F32, name="gate_cols")
@@ -231,12 +234,13 @@ def tile_moe_pre_lin_relu2_kernel(tc, xT, w, b, gate, offs, pos1, pos2, pos3, ou
                 w_rounded.rearrange("p (e n j) -> p e n j", n=N, j=PACK),
                 w_raw[s][:].rearrange("p e (j n) -> p e n j", j=PACK),
                 1.0, 0.0, op0=ALU.mult, op1=ALU.add)
-            if shares[s]:
-                nc.gpsimd.tensor_tensor(
-                    rounded[:, PACK * mine:PACK * n].rearrange("p (c i j) -> p c j i", i=QUAD, j=PACK),
-                    xg[:, :, mine:n].rearrange("p j (c i) -> p c j i", i=QUAD),
-                    shared_gates[e1 * C][:, shares[e0 // GROUPS[0][1] * PASSES] - shares[s]:].rearrange("p (c i) -> p c i", i=QUAD).unsqueeze(2).to_broadcast(
-                        [P, shares[s] // QUAD, PACK, QUAD]), ALU.mult)
+            nc.gpsimd.tensor_tensor(
+                rounded[:, PACK * mine:PACK * n].rearrange("p (c i j) -> p c j i", i=QUAD, j=PACK),
+                xg[:, :, mine:n].rearrange("p j (c i) -> p c j i", i=QUAD),
+                shared_gates[e1 * C][:, shared_gates[e1 * C].shape[1] - shares[s]:].rearrange("p (c i) -> p c i", i=QUAD).unsqueeze(2).to_broadcast(
+                    [P, shares[s] // QUAD, PACK, QUAD]), ALU.mult)
+            if s + 1 == last:
+                gate_round(last, y[:].bitcast(BF16), ahead, 0, tail_cuts[1])
             tokens_of(s)
             quantise_w(s, w_rounded, 0, PACK)
             quantise_w(s, w_rounded, PACK, CHUNKS[s])
@@ -258,7 +262,6 @@ def tile_moe_pre_lin_relu2_kernel(tc, xT, w, b, gate, offs, pos1, pos2, pos3, ou
         rest = staging()[0]
         pieces = list(zip(tail_cuts, tail_cuts[1:]))
         rooms = [y[:].bitcast(BF16)] + [rest] * (len(pieces) - 1)
-        gate_round(last, rooms[0], xg, *pieces[0])
         for i, (a, z) in enumerate(pieces):
             if i + 1 < len(pieces):
                 gate_round(last, rooms[i + 1], xg, *pieces[i + 1])

@@ -28,9 +28,10 @@ SPARE = 8
 GROUPS = ((0, 5), (5, E))
 MOST = GROUPS[0][1] * C
 OWN_ROW = 1
-OWNS = (MOST, 928, 928, 928, 800, 800, 800)
-SHARES = (192, 192, 192, 128, 112, 112, 144)
+OWNS = (MOST // 2, 960, 960, 960, 832, 832, 832)
+SHARES = (208, 208, 208, 144, 128, 128, 160)
 CHUNKS = (5, 5, 5, 6, 5, 5, 5)
+CALL_WORDS = (128, 256, 384, 512, 1024)
 OUT_CUTS = (0, 256, 576, T)
 
 
@@ -78,9 +79,9 @@ def tile_moe_pre_lin_relu2_kernel(tc, xT, w, b, gate, offs, pos1, pos2, pos3, ou
 
         load_plane(0, 0, nc.scalar)
         nc.sync.dma_start(slot_tokens[:], offs)
-        load_plane(0, 1, nc.sync)
         gate_rows = keep.tile([P, P], F32, name="gate_rows")
         nc.sync.dma_start(gate_rows[:], gate.rearrange("r (c p) -> (r c) p", p=P)[0:P])
+        load_plane(0, 1, nc.sync)
         load_plane(0, 2, nc.sync)
         load_plane(0, 3, nc.sync)
         load_gate(MOST, shares[0])
@@ -138,36 +139,34 @@ def tile_moe_pre_lin_relu2_kernel(tc, xT, w, b, gate, offs, pos1, pos2, pos3, ou
         def quantise(codes, scales, src):
             nc.vector.quantize_mx(out=codes.bitcast(FP8X4), scales=scales, in_=src)
 
-        w_codes = keep.tile([P, len(blocks) * N], U32, name="w_codes", align_bytes=64)
-        w_scales = keep.tile([P, len(blocks) * N], U8, name="w_scales", align_bytes=64)
-        x_made = {}
+        made = {}
 
-        def staging():
-            rounded = ring.tile([P, PACK * (MOST + max(CHUNKS) * N)], BF16, name="rounded", align_bytes=64, bufs=1)
-            return rounded[:, :PACK * MOST], rounded[:, PACK * MOST:]
+        def staging(words):
+            return ring.tile([P, PACK * words], BF16, name="rounded", align_bytes=64, bufs=1)
 
-        def quantise_w(s, rounded, a, z):
-            cols = slice((starts[s] + a) * N, (starts[s] + z) * N)
-            quantise(w_codes[:, cols], w_scales[:, cols], rounded[:, a * N * PACK:z * N * PACK])
+        def packed(s, words):
+            codes = ring.tile([P, words], U32, name="codes", align_bytes=64, bufs=3)
+            scales = ring.tile([P, words], U8, name="scales", align_bytes=64, bufs=3)
+            made[s] = (codes, scales)
 
-        def tokens_of(s):
-            e0, e1, g = steps[s]
-            codes = ring.tile([P, (e1 - e0) * C], U32, name="x_codes", align_bytes=64, bufs=3)
-            scales = ring.tile([P, (e1 - e0) * C], U8, name="x_scales", align_bytes=64, bufs=3)
-            x_made[s] = (codes, scales)
-
-        def quantise_x(s, a, z, src):
-            codes, scales = x_made[s]
-            quantise(codes[:, a:z], scales[:, a:z], src)
+        def quantise_words(s, a, z, src):
+            codes, scales = made[s]
+            while a < z:
+                upto = a + max(m for m in CALL_WORDS if m <= z - a)
+                quantise(codes[:, a:upto], scales[:, a:upto], src[:, PACK * a:PACK * upto])
+                a = upto
 
         def multiply(s, a, z):
             e0, e1, g = steps[s]
-            x_codes, x_scales = x_made[s]
+            x_codes, x_scales = made[s]
             for s0 in sorted(accs):
                 acc, m, name = accs[s0]
                 c0 = s0 - e0 * C
                 if a <= c0 < z:
-                    n0 = blocks.index((g, s0 // C)) * N
+                    u = blocks.index((g, s0 // C))
+                    home = max(i for i in range(last) if starts[i] <= u)
+                    w_codes, w_scales = made[home]
+                    n0 = (steps[home][1] - steps[home][0]) * C + (u - starts[home]) * N
                     total, left = to_go[name]
                     to_go[name] = [total, left - 1]
                     nc.tensor.matmul_mx(
@@ -191,14 +190,13 @@ def tile_moe_pre_lin_relu2_kernel(tc, xT, w, b, gate, offs, pos1, pos2, pos3, ou
             e0, e1, g = steps[s]
             n = (e1 - e0) * C
             xg = ring.tile([P, PACK, MOST], F32, name="xg", align_bytes=64)
-            own_rows = (OWN_ROW, OWN_ROW + 2) if s == 0 else (OWN_ROW,)
+            own_rows = range(PACK) if s == 0 else (OWN_ROW,)
             for j in range(PACK):
                 if j not in own_rows:
                     nc.scalar.activation(xg[:, j, :n], picked(s, j, 0, n), ACT.Copy)
             cut = n - owns[s]
             for j in own_rows:
-                if cut:
-                    nc.scalar.activation(xg[:, j, :cut], picked(s, j, 0, cut), ACT.Copy)
+                nc.scalar.activation(xg[:, j, :cut], picked(s, j, 0, cut), ACT.Copy)
                 nc.vector.tensor_copy(xg[:, j, cut:n], picked(s, j, cut, n))
             return xg
 
@@ -220,18 +218,18 @@ def tile_moe_pre_lin_relu2_kernel(tc, xT, w, b, gate, offs, pos1, pos2, pos3, ou
         open_banks([("bank4", [(0, C), (C, C)]), ("bank5", [(2 * C, C), (3 * C, C)]), ("bank6", [(4 * C, C)])])
         xg = gather(0)
 
-        tail_cuts = (0, 2 * C, 3 * C, 3 * C + HALF, WIDE)
+        tail_cuts = (0, 2 * C, 3 * C + HALF, WIDE)
         for s in range(last):
             e0, e1, g = steps[s]
             n = (e1 - e0) * C
             ahead = gather(s + 1) if s + 1 < last else gather_pieces(last, tail_cuts)
-            rounded, w_room = staging()
+            words = n + CHUNKS[s] * N
+            rounded = staging(words)
             mine = n - shares[s]
             for a in range(0, mine, BANK):
                 gate_round(s, rounded, xg, a, min(a + BANK, mine))
-            w_rounded = w_room[:, :CHUNKS[s] * N * PACK]
             nc.gpsimd.tensor_scalar(
-                w_rounded.rearrange("p (e n j) -> p e n j", n=N, j=PACK),
+                rounded[:, PACK * n:].rearrange("p (e n j) -> p e n j", n=N, j=PACK),
                 w_raw[s][:].rearrange("p e (j n) -> p e n j", j=PACK),
                 1.0, 0.0, op0=ALU.mult, op1=ALU.add)
             nc.gpsimd.tensor_tensor(
@@ -241,12 +239,12 @@ def tile_moe_pre_lin_relu2_kernel(tc, xT, w, b, gate, offs, pos1, pos2, pos3, ou
                     [P, shares[s] // QUAD, PACK, QUAD]), ALU.mult)
             if s + 1 == last:
                 gate_round(last, y[:].bitcast(BF16), ahead, 0, tail_cuts[1])
-            tokens_of(s)
-            quantise_w(s, w_rounded, 0, PACK)
-            quantise_w(s, w_rounded, PACK, CHUNKS[s])
-            for a, z in ((0, n - WIDE), (n - WIDE, n)):
-                if z > a:
-                    quantise_x(s, a, z, rounded[:, PACK * a:PACK * z])
+            packed(s, words)
+            quantise_words(s, 0, WIDE, rounded)
+            if s + 1 == last:
+                packed(last, WIDE)
+                quantise_words(last, 0, tail_cuts[1], y[:].bitcast(BF16))
+            quantise_words(s, WIDE, words, rounded)
             if s == PASSES:
                 open_banks([
                     ("bank7", [(5 * C, C), (6 * C, C)]), ("bank0", [(8 * C, HALF)]),
@@ -258,21 +256,19 @@ def tile_moe_pre_lin_relu2_kernel(tc, xT, w, b, gate, offs, pos1, pos2, pos3, ou
             multiply(s, 0, n)
             xg = ahead
 
-        tokens_of(last)
-        rest = staging()[0]
-        pieces = list(zip(tail_cuts, tail_cuts[1:]))
-        rooms = [y[:].bitcast(BF16)] + [rest] * (len(pieces) - 1)
-        for i, (a, z) in enumerate(pieces):
-            if i + 1 < len(pieces):
-                gate_round(last, rooms[i + 1], xg, *pieces[i + 1])
-            quantise_x(last, a, z, rooms[i][:, PACK * a:PACK * z])
+        multiply(last, 0, tail_cuts[1])
+        rounded = staging(WIDE)
+        pieces = list(zip(tail_cuts[1:], tail_cuts[2:]))
+        for a, z in pieces:
+            gate_round(last, rounded, xg, a, z)
+        for a, z in pieces:
+            quantise_words(last, a, z, rounded)
             multiply(last, a, z)
         square(early, 0, MOST)
-        for e in (5, 6, 7):
-            relu(y, e * C)
-        square(y, 5 * C, 8 * C)
-        relu(y, 8 * C)
-        square(y, 8 * C, 8 * C + HALF)
+        for e0, z in ((5, 7 * C), (7, S - HALF)):
+            for e in (e0, e0 + 1):
+                relu(y, e * C)
+            square(y, e0 * C, z)
         positive = keep.tile([P, HALF], F32, name="positive", align_bytes=64)
         nc.vector.tensor_scalar(
             positive[:], accs[8 * C + HALF][0], bias[:, E - 1:], 0.0, op0=ALU.add, op1=ALU.max)

@@ -28,11 +28,11 @@ SPARE = 8
 GROUPS = ((0, 5), (5, E))
 MOST = GROUPS[0][1] * C
 OWN_ROW = 1
-OWNS = (MOST // 2, 960, 960, 960, 832, 832, 832)
-SHARES = (208, 208, 208, 144, 128, 128, 160)
+OWNS = (704, 992, 992, 992, 768, 768, 768)
+SHARES = (208, 208, 208, 136, 112, 112, 152)
 CHUNKS = (5, 5, 5, 6, 5, 5, 5)
 CALL_WORDS = (128, 256, 384, 512, 1024)
-OUT_CUTS = (0, 256, 576, T)
+OUT_CUTS = (0, 288, 640, T)
 
 
 def tile_moe_pre_lin_relu2_kernel(tc, xT, w, b, gate, offs, pos1, pos2, pos3, out):
@@ -79,7 +79,7 @@ def tile_moe_pre_lin_relu2_kernel(tc, xT, w, b, gate, offs, pos1, pos2, pos3, ou
 
         load_plane(0, 0, nc.scalar)
         nc.sync.dma_start(slot_tokens[:], offs)
-        gate_rows = keep.tile([P, P], F32, name="gate_rows")
+        gate_rows = ring.tile([P, P], F32, name="xg", align_bytes=64)
         nc.sync.dma_start(gate_rows[:], gate.rearrange("r (c p) -> (r c) p", p=P)[0:P])
         load_plane(0, 1, nc.sync)
         load_plane(0, 2, nc.sync)
@@ -108,15 +108,12 @@ def tile_moe_pre_lin_relu2_kernel(tc, xT, w, b, gate, offs, pos1, pos2, pos3, ou
 
         identity = keep.tile([P, P], F32, name="identity")
         make_identity(nc, identity[:])
-        unread = keep.tile([P, 2], F32, name="unread")
-        nc.vector.memset(unread[:, :1], 0.0)
-        nc.scalar.activation(unread[:, 1:], unread[:, :1], ACT.Copy)
         turned = psum.tile([P, BANK], F32, name="bank7")
         nc.tensor.transpose(turned[:, :P], gate_rows[:], identity[:])
         gate_cols = keep.tile([P, S // P], F32, name="gate_cols")
         nc.vector.tensor_copy(gate_cols[:], turned[:, :S // P])
         gate_banks = {}
-        for name, s0, n in (("bank0", 0, BANK), ("bank1", BANK, BANK), ("bank7", WIDE, MOST - WIDE),
+        for name, s0, n in (("bank0", 0, BANK), ("bank1", BANK, BANK), ("bank7", WIDE, P),
                             ("bank2", MOST, BANK), ("bank3", MOST + BANK, BANK)):
             bank = psum.tile([P, BANK], F32, name=name)
             for c in range(n // P):
@@ -240,23 +237,22 @@ def tile_moe_pre_lin_relu2_kernel(tc, xT, w, b, gate, offs, pos1, pos2, pos3, ou
             if s + 1 == last:
                 gate_round(last, y[:].bitcast(BF16), ahead, 0, tail_cuts[1])
             packed(s, words)
-            quantise_words(s, 0, WIDE, rounded)
-            if s + 1 == last:
-                packed(last, WIDE)
-                quantise_words(last, 0, tail_cuts[1], y[:].bitcast(BF16))
-            quantise_words(s, WIDE, words, rounded)
+            quantise_words(s, 0, words, rounded)
             if s == PASSES:
                 open_banks([
                     ("bank7", [(5 * C, C), (6 * C, C)]), ("bank0", [(8 * C, HALF)]),
                     ("bank1", [(8 * C + HALF, HALF)])])
-                early = keep.tile([P, MOST + SPARE], F32, name="plane00", align_bytes=64)
-                for e in range(*GROUPS[0]):
-                    relu(early, e * C)
-                open_banks([("bank4", [(7 * C, C)])])
-            multiply(s, 0, n)
+                relu(y, WIDE)
+                open_banks([("bank6", [(7 * C, C)])])
+            if s + 1 < last:
+                multiply(s, 0, n)
             xg = ahead
 
+        packed(last, WIDE)
+        quantise_words(last, 0, tail_cuts[1], y[:].bitcast(BF16))
+        multiply(last - 1, 0, tail_cuts[1])
         multiply(last, 0, tail_cuts[1])
+        multiply(last - 1, tail_cuts[1], WIDE)
         rounded = staging(WIDE)
         pieces = list(zip(tail_cuts[1:], tail_cuts[2:]))
         for a, z in pieces:
@@ -264,15 +260,23 @@ def tile_moe_pre_lin_relu2_kernel(tc, xT, w, b, gate, offs, pos1, pos2, pos3, ou
         for a, z in pieces:
             quantise_words(last, a, z, rounded)
             multiply(last, a, z)
-        square(early, 0, MOST)
-        for e0, z in ((5, 7 * C), (7, S - HALF)):
-            for e in (e0, e0 + 1):
-                relu(y, e * C)
-            square(y, e0 * C, z)
-        positive = keep.tile([P, HALF], F32, name="positive", align_bytes=64)
-        nc.vector.tensor_scalar(
-            positive[:], accs[8 * C + HALF][0], bias[:, E - 1:], 0.0, op0=ALU.add, op1=ALU.max)
-        nc.vector.tensor_tensor(y[:, S - HALF:], positive[:], positive[:], ALU.mult)
+        held = keep.tile([P, MOST + SPARE], F32, name=f"plane{PASSES - 1}{PACK - 1}", align_bytes=64)
+        for s0 in range(0, WIDE, C):
+            relu(held, s0)
+        square(held, 0, WIDE)
+        for e in (5, 6):
+            relu(y, e * C)
+        square(y, WIDE, 7 * C)
+        positive = keep.tile([P, 2 * C], F32, name="positive", align_bytes=64)
+        for s0 in (7 * C, 8 * C, 8 * C + HALF):
+            acc, m, name = accs[s0]
+            nc.vector.tensor_scalar(
+                positive[:, s0 - 7 * C:s0 - 7 * C + m], acc, bias[:, s0 // C:s0 // C + 1], 0.0,
+                op0=ALU.add, op1=ALU.max)
+        nc.scalar.activation(y[:, 7 * C:8 * C], positive[:, :C], ACT.Square)
+        for a in (C, C + HALF):
+            half = positive[:, a:a + HALF]
+            nc.vector.tensor_tensor(y[:, 7 * C + a:7 * C + a + HALF], half, half, ALU.mult)
 
         total = ring.tile([P, 4, T], F32, name="xg", align_bytes=64)
 

@@ -19,20 +19,19 @@ ALU = mybir.AluOpType
 
 P = 128
 PACK = 4
-PASSES = K // (P * PACK)
-HALF = C // 2
-QUAD = 4
 BANK = 512
-WIDE = 2 * BANK
+HALF = S // 2
 SPARE = 8
-GROUPS = ((0, 5), (5, E))
-MOST = GROUPS[0][1] * C
+STEPS = ((0, 0), (0, 1), (1, 0), (1, 1), (2, 0), (3, 0), (2, 1), (3, 1))
 OWN_ROW = 1
-OWNS = (704, 992, 992, 992, 768, 768, 768)
-SHARES = (208, 208, 208, 136, 112, 112, 152)
-CHUNKS = (5, 5, 5, 6, 5, 5, 5)
+OWNS = (576, 896, 896, 896, 896, 896, 896)
+SHARES = (144, 128, 176, 176, 176, 176, 128, 128)
+CHUNKS = ((2, 2, 3), (6,), (5,), (5,), (5,), (5,), (3,))
 CALL_WORDS = (128, 256, 384, 512, 1024)
+TAIL_CUTS = (0, 640, 1024, HALF)
 OUT_CUTS = (0, 288, 640, T)
+RUN_VECTOR = 2
+RUN_GPSIMD = 2
 
 
 def tile_moe_pre_lin_relu2_kernel(tc, xT, w, b, gate, offs, pos1, pos2, pos3, out):
@@ -42,11 +41,7 @@ def tile_moe_pre_lin_relu2_kernel(tc, xT, w, b, gate, offs, pos1, pos2, pos3, ou
         ring = ctx.enter_context(tc.tile_pool(name="ring", bufs=2))
         psum = ctx.enter_context(tc.psum_pool(name="psum", bufs=1))
 
-        steps = [(e0, e1, g) for e0, e1 in GROUPS for g in range(PASSES)]
-        last = len(steps) - 1
-        owns = OWNS
-        shares = SHARES
-
+        last = len(STEPS) - 1
         slot_tokens = keep.tile([P, S // 16], U16, name="slot_tokens")
         x_rows = xT.rearrange("(g p j) t -> g j p t", p=P, j=PACK)
         w_rows = w.rearrange("e (g p j) n -> g p e (j n)", p=P, j=PACK)
@@ -54,48 +49,52 @@ def tile_moe_pre_lin_relu2_kernel(tc, xT, w, b, gate, offs, pos1, pos2, pos3, ou
         w_raw = {}
 
         def load_plane(g, j, queue):
-            plane = keep.tile([P, MOST + SPARE], F32, name=f"plane{g}{j}", align_bytes=64)
+            plane = keep.tile([P, HALF + SPARE], F32, name=f"plane{g % 2}{j}", align_bytes=64)
             queue.dma_start(plane[:, :T], x_rows[g, j])
             planes[g, j] = plane
 
-        blocks = [(g, e) for e0, e1, g in steps for e in range(e0, e1)]
-        starts = [sum(CHUNKS[:s]) for s in range(len(CHUNKS) + 1)]
+        def load_planes(g, rows):
+            for j in rows:
+                load_plane(g, j, nc.sync)
+
+        middle_expert = E // 2
+        blocks = [(g, e) for g, h in STEPS for e in (range(middle_expert + 1), range(middle_expert + 1, E))[h]]
+        sizes = [sum(chunk) for chunk in CHUNKS]
+        starts = [sum(sizes[:s]) for s in range(len(sizes) + 1)]
 
         def load_w(s):
-            chunk = blocks[starts[s]:starts[s + 1]]
-            raw = ring.tile([P, len(chunk), PACK * N], F32, name="w_raw", align_bytes=64, bufs=3)
-            heads = [i for i, (g, e) in enumerate(chunk) if i == 0 or chunk[i - 1] != (g, e - 1)]
-            for a, z in zip(heads, heads[1:] + [len(chunk)]):
-                g, e = chunk[a]
-                nc.sync.dma_start(raw[:, a:z], w_rows[g][:, e:e + z - a])
-            w_raw[s] = raw
+            w_raw[s] = []
+            first = starts[s]
+            for size in CHUNKS[s]:
+                piece = blocks[first:first + size]
+                raw = ring.tile([P, size, PACK * N], F32, name="w_raw", align_bytes=64, bufs=3)
+                heads = [i for i, (g, e) in enumerate(piece) if i == 0 or piece[i - 1] != (g, e - 1)]
+                for a, z in zip(heads, heads[1:] + [size]):
+                    g, e = piece[a]
+                    nc.sync.dma_start(raw[:, a:z], w_rows[g][:, e:e + z - a])
+                w_raw[s].append((first - starts[s], size, raw))
+                first += size
 
-        shared_gates = {}
+        reach = [max(SHARES[s] for s in range(len(STEPS)) if STEPS[s][1] == h) for h in range(2)]
+        gate_near = []
 
-        def load_gate(end, n):
-            tile = keep.tile([P, n], F32, name=f"gate{end}", align_bytes=64)
-            nc.sync.dma_start(tile[:], gate[0:P, end - n:end])
-            shared_gates[end] = tile
+        def load_gate(h):
+            tile = keep.tile([P, reach[h]], F32, name=f"gate_near{h}", align_bytes=64)
+            first = HALF if h else HALF - reach[0]
+            nc.sync.dma_start(tile[:], gate[0:P, first:first + reach[h]])
+            gate_near.append(tile)
 
         load_plane(0, 0, nc.scalar)
         nc.sync.dma_start(slot_tokens[:], offs)
         gate_rows = ring.tile([P, P], F32, name="xg", align_bytes=64)
         nc.sync.dma_start(gate_rows[:], gate.rearrange("r (c p) -> (r c) p", p=P)[0:P])
-        load_plane(0, 1, nc.sync)
-        load_plane(0, 2, nc.sync)
-        load_plane(0, 3, nc.sync)
-        load_gate(MOST, shares[0])
-        load_plane(1, 0, nc.sync)
-        load_plane(1, 1, nc.sync)
+        load_planes(0, range(1, PACK))
         load_w(0)
-        load_plane(1, 2, nc.sync)
-        load_plane(1, 3, nc.sync)
-        for g in range(2, PASSES):
-            for j in range(PACK):
-                load_plane(g, j, nc.sync)
-                if j == 0:
-                    load_w(g - 1)
-        load_gate(S, max(shares[PASSES:]))
+        load_gate(0)
+        load_planes(1, range(1))
+        load_w(1)
+        load_gate(1)
+        load_planes(1, range(1, PACK))
         bias = keep.tile([P, E], F32, name="bias")
         nc.sync.dma_start(bias[:], b)
         lists = []
@@ -103,20 +102,27 @@ def tile_moe_pre_lin_relu2_kernel(tc, xT, w, b, gate, offs, pos1, pos2, pos3, ou
             lst = keep.tile([P, T // 16], U16, name=f"pos{r}")
             nc.sync.dma_start(lst[:], pos)
             lists.append(lst)
-        for s in range(PASSES - 1, last):
-            load_w(s)
+        load_w(2)
+        load_planes(2, range(PACK))
+        load_w(3)
+        load_w(4)
+        load_planes(3, range(PACK))
+        load_w(5)
+        load_w(6)
 
+        zero = keep.tile([P, 1], F32, name="zero")
+        nc.vector.memset(zero[:], 0.0)
         identity = keep.tile([P, P], F32, name="identity")
-        make_identity(nc, identity[:])
+        nc.scalar.activation(identity[:], zero[:].to_broadcast([P, P]), ACT.Copy)
+        make_identity(nc, identity[:], nomemset=True)
         turned = psum.tile([P, BANK], F32, name="bank7")
         nc.tensor.transpose(turned[:, :P], gate_rows[:], identity[:])
         gate_cols = keep.tile([P, S // P], F32, name="gate_cols")
         nc.vector.tensor_copy(gate_cols[:], turned[:, :S // P])
         gate_banks = {}
-        for name, s0, n in (("bank0", 0, BANK), ("bank1", BANK, BANK), ("bank7", WIDE, P),
-                            ("bank2", MOST, BANK), ("bank3", MOST + BANK, BANK)):
-            bank = psum.tile([P, BANK], F32, name=name)
-            for c in range(n // P):
+        for i, s0 in enumerate((0, BANK, S - 2 * BANK, S - BANK)):
+            bank = psum.tile([P, BANK], F32, name=f"bank{i}")
+            for c in range(BANK // P):
                 col = s0 // P + c
                 nc.tensor.transpose(
                     bank[:, c * P:(c + 1) * P], gate_cols[:, col:col + 1].to_broadcast([P, P]), identity[:])
@@ -129,154 +135,164 @@ def tile_moe_pre_lin_relu2_kernel(tc, xT, w, b, gate, offs, pos1, pos2, pos3, ou
         def open_banks(banks):
             for name, sums in banks:
                 bank = psum.tile([N, BANK], F32, name=name)
-                to_go[name] = [PASSES * len(sums)] * 2
+                to_go[name] = [K // (P * PACK) * len(sums)] * 2
                 for s0, m in sums:
-                    accs[s0] = (bank[:, s0 - sums[0][0]:s0 - sums[0][0] + m], m, name)
+                    accs[s0] = (bank, s0 - sums[0][0], m, name)
 
-        def quantise(codes, scales, src):
-            nc.vector.quantize_mx(out=codes.bitcast(FP8X4), scales=scales, in_=src)
-
+        lead = [size * N for size in sizes] + [0]
         made = {}
-
-        def staging(words):
-            return ring.tile([P, PACK * words], BF16, name="rounded", align_bytes=64, bufs=1)
+        ready = {}
+        done = set()
 
         def packed(s, words):
-            codes = ring.tile([P, words], U32, name="codes", align_bytes=64, bufs=3)
-            scales = ring.tile([P, words], U8, name="scales", align_bytes=64, bufs=3)
+            codes = keep.tile([P, words], U32, name=f"codes{s}", align_bytes=64)
+            scales = keep.tile([P, words], U8, name=f"scales{s}", align_bytes=64)
             made[s] = (codes, scales)
 
-        def quantise_words(s, a, z, src):
+        def quantise(s, a, z, src, origin=0):
             codes, scales = made[s]
+            ready[s] = z - lead[s]
             while a < z:
                 upto = a + max(m for m in CALL_WORDS if m <= z - a)
-                quantise(codes[:, a:upto], scales[:, a:upto], src[:, PACK * a:PACK * upto])
+                nc.vector.quantize_mx(
+                    out=codes[:, a:upto].bitcast(FP8X4), scales=scales[:, a:upto], in_=src[:, PACK * (a - origin):PACK * (upto - origin)])
                 a = upto
 
-        def multiply(s, a, z):
-            e0, e1, g = steps[s]
-            x_codes, x_scales = made[s]
-            for s0 in sorted(accs):
-                acc, m, name = accs[s0]
-                c0 = s0 - e0 * C
-                if a <= c0 < z:
-                    u = blocks.index((g, s0 // C))
-                    home = max(i for i in range(last) if starts[i] <= u)
-                    w_codes, w_scales = made[home]
-                    n0 = (steps[home][1] - steps[home][0]) * C + (u - starts[home]) * N
-                    total, left = to_go[name]
-                    to_go[name] = [total, left - 1]
-                    nc.tensor.matmul_mx(
-                        out=acc,
-                        lhsT=w_codes[:, n0:n0 + N].bitcast(FP8X4), lhsT_scale=w_scales[:, n0:n0 + N],
-                        rhs=x_codes[:, c0:c0 + m].bitcast(FP8X4), rhs_scale=x_scales[:, c0:c0 + m],
-                        start=(left == total), stop=(left == 1))
+        def multiply():
+            for s in sorted(ready):
+                g, h = STEPS[s]
+                x_codes, x_scales = made[s]
+                for s0 in sorted(accs):
+                    bank, col, m, name = accs[s0]
+                    c0 = s0 - h * HALF
+                    if 0 <= c0 < min(ready[s], HALF) and (s, s0) not in done:
+                        done.add((s, s0))
+                        u = blocks.index((g, s0 // C))
+                        home = max(i for i in range(last) if starts[i] <= u)
+                        w_codes, w_scales = made[home]
+                        n0 = (u - starts[home]) * N
+                        c0 += lead[s]
+                        total, left = to_go[name]
+                        to_go[name] = [total, left - 1]
+                        nc.tensor.matmul_mx(
+                            out=bank[:, col:col + m],
+                            lhsT=w_codes[:, n0:n0 + N].bitcast(FP8X4), lhsT_scale=w_scales[:, n0:n0 + N],
+                            rhs=x_codes[:, c0:c0 + m].bitcast(FP8X4), rhs_scale=x_scales[:, c0:c0 + m],
+                            start=(left == total), stop=(left == 1))
 
-        def relu(dst, s0):
-            acc, m, name = accs[s0]
-            nc.scalar.activation(dst[:, s0:s0 + m], acc, ACT.Relu, bias=bias[:, s0 // C:s0 // C + 1])
+        def picked(s, j, a, z):
+            g, h = STEPS[s]
+            return planes[g, j][:].indirect(slot_tokens[:, (h * HALF + a) // 16:(h * HALF + z) // 16])
+
+        def gather(s):
+            xg = ring.tile([P, PACK, HALF], F32, name="xg", align_bytes=64)
+            own_rows = range(PACK) if s == 0 else (OWN_ROW,)
+            for j in range(PACK):
+                if j not in own_rows:
+                    nc.scalar.activation(xg[:, j, :], picked(s, j, 0, HALF), ACT.Copy)
+            cut = HALF - OWNS[s]
+            for j in own_rows:
+                nc.scalar.activation(xg[:, j, :cut], picked(s, j, 0, cut), ACT.Copy)
+                nc.vector.tensor_copy(xg[:, j, cut:], picked(s, j, cut, HALF))
+            return xg
+
+        def gather_pieces(s):
+            flat = ring.tile([P, PACK * HALF], F32, name="xg", align_bytes=64)
+            pieces = []
+            for a, z in zip(TAIL_CUTS, TAIL_CUTS[1:]):
+                piece = flat[:, PACK * a:PACK * z].rearrange("p (j c) -> p j c", j=PACK)
+                for j in range(PACK):
+                    nc.scalar.activation(piece[:, j, :], picked(s, j, a, z), ACT.Copy)
+                pieces.append(piece)
+            return pieces
+
+        def times_gate(engine, run, rounded, xg, a, z, weights, origin=0, staged=0):
+            engine.tensor_tensor(
+                rounded[:, PACK * (a - staged):PACK * (z - staged)].rearrange("p (c i j) -> p c j i", i=run, j=PACK),
+                xg[:, :, a - origin:z - origin].rearrange("p j (c i) -> p c j i", i=run),
+                weights.rearrange("p (c i) -> p c i", i=run).unsqueeze(2).to_broadcast(
+                    [P, (z - a) // run, PACK, run]), ALU.mult)
+
+        def vector_products(s, rounded, xg, a, z, origin=0, staged=0):
+            h = STEPS[s][1]
+            for s0 in sorted(gate_banks):
+                lo, hi = max(a, s0 - h * HALF), min(z, s0 + BANK - h * HALF)
+                if lo < hi:
+                    first = h * HALF + lo - s0
+                    times_gate(nc.vector, RUN_VECTOR, rounded, xg, lo, hi, gate_banks[s0][:, first:first + hi - lo], origin, staged)
+
+        def gpsimd_product(s, rounded, xg):
+            n = SHARES[s]
+            if STEPS[s][1]:
+                times_gate(nc.gpsimd, RUN_GPSIMD, rounded, xg, 0, n, gate_near[1][:, :n])
+            else:
+                times_gate(nc.gpsimd, RUN_GPSIMD, rounded, xg, HALF - n, HALF, gate_near[0][:, reach[0] - n:])
+
+        half_c = C // 2
+        open_banks([
+            ("bank4", [(0, C), (C, C)]), ("bank5", [(2 * C, C), (3 * C, C)]),
+            ("bank6", [(4 * C, half_c), (HALF, half_c), (5 * C, C)]), ("bank7", [(6 * C, C)])])
+        xg = gather(0)
+        for s in range(last):
+            h = STEPS[s][1]
+            ahead = gather(s + 1) if s + 1 < last else gather_pieces(last)
+            words = HALF + sizes[s] * N
+            rounded = ring.tile([P, PACK * words], BF16, name="rounded", align_bytes=64, bufs=1)
+            tokens = rounded[:, PACK * lead[s]:]
+            vector_products(s, tokens, xg, SHARES[s] * h, HALF - SHARES[s] * (1 - h))
+            for first, size, raw in w_raw[s]:
+                a = first * N
+                nc.gpsimd.tensor_scalar(
+                    rounded[:, PACK * a:PACK * (a + size * N)].rearrange("p (e n j) -> p e n j", n=N, j=PACK),
+                    raw[:].rearrange("p e (j n) -> p e n j", j=PACK),
+                    1.0, 0.0, op0=ALU.mult, op1=ALU.add)
+            gpsimd_product(s, tokens, xg)
+            packed(s, words)
+            quantise(s, 0, words, rounded)
+            if s == last - 2:
+                open_banks([("bank0", [(7 * C, C), (8 * C, half_c)]), ("bank1", [(8 * C + half_c, half_c)])])
+            multiply()
+            xg = ahead
+
+        rounded = ring.tile([P, PACK * HALF], BF16, name="rounded", align_bytes=64, bufs=1)
+        packed(last, HALF)
+        gpsimd_product(last, rounded, xg[0])
+        vector_products(last, rounded, xg[0], SHARES[last], TAIL_CUTS[1])
+        quantise(last, 0, TAIL_CUTS[1], rounded)
+        multiply()
+        stages = [(rounded, 0)] * (len(xg) - 2) + [(y[:].bitcast(BF16), TAIL_CUTS[-2])]
+        pieces = list(zip(TAIL_CUTS[1:], TAIL_CUTS[2:], xg[1:], stages))
+        for a, z, piece, (stage, staged) in pieces:
+            vector_products(last, stage, piece, a, z, a, staged)
+        for a, z, piece, (stage, staged) in pieces:
+            quantise(last, a, z, stage, staged)
+            multiply()
+
+        def sums_of(s0, m):
+            bank, col = accs[s0][:2]
+            return bank[:, col:col + m]
+
+        def relu(dst, e):
+            nc.scalar.activation(dst[:, e * C:(e + 1) * C], sums_of(e * C, C), ACT.Relu, bias=bias[:, e:e + 1])
 
         def square(src, a, z):
             nc.scalar.activation(y[:, a:z], src[:, a:z], ACT.Square)
 
-        def picked(s, j, a, z):
-            e0, e1, g = steps[s]
-            return planes[g, j][:].indirect(slot_tokens[:, (e0 * C + a) // 16:(e0 * C + z) // 16])
-
-        def gather(s):
-            e0, e1, g = steps[s]
-            n = (e1 - e0) * C
-            xg = ring.tile([P, PACK, MOST], F32, name="xg", align_bytes=64)
-            own_rows = range(PACK) if s == 0 else (OWN_ROW,)
-            for j in range(PACK):
-                if j not in own_rows:
-                    nc.scalar.activation(xg[:, j, :n], picked(s, j, 0, n), ACT.Copy)
-            cut = n - owns[s]
-            for j in own_rows:
-                nc.scalar.activation(xg[:, j, :cut], picked(s, j, 0, cut), ACT.Copy)
-                nc.vector.tensor_copy(xg[:, j, cut:n], picked(s, j, cut, n))
-            return xg
-
-        def gather_pieces(s, cuts):
-            xg = ring.tile([P, PACK, MOST], F32, name="xg", align_bytes=64)
-            for a, z in zip(cuts, cuts[1:]):
-                for j in range(PACK):
-                    nc.scalar.activation(xg[:, j, a:z], picked(s, j, a, z), ACT.Copy)
-            return xg
-
-        def gate_round(s, rounded, xg, a, z):
-            h = a // BANK * BANK
-            weights = gate_banks[steps[s][0] * C + h][:, a - h:z - h].rearrange("p (c i) -> p c i", i=QUAD)
-            nc.vector.tensor_tensor(
-                rounded[:, PACK * a:PACK * z].rearrange("p (c i j) -> p c j i", i=QUAD, j=PACK),
-                xg[:, :, a:z].rearrange("p j (c i) -> p c j i", i=QUAD),
-                weights.unsqueeze(2).to_broadcast([P, (z - a) // QUAD, PACK, QUAD]), ALU.mult)
-
-        open_banks([("bank4", [(0, C), (C, C)]), ("bank5", [(2 * C, C), (3 * C, C)]), ("bank6", [(4 * C, C)])])
-        xg = gather(0)
-
-        tail_cuts = (0, 2 * C, 3 * C + HALF, WIDE)
-        for s in range(last):
-            e0, e1, g = steps[s]
-            n = (e1 - e0) * C
-            ahead = gather(s + 1) if s + 1 < last else gather_pieces(last, tail_cuts)
-            words = n + CHUNKS[s] * N
-            rounded = staging(words)
-            mine = n - shares[s]
-            for a in range(0, mine, BANK):
-                gate_round(s, rounded, xg, a, min(a + BANK, mine))
-            nc.gpsimd.tensor_scalar(
-                rounded[:, PACK * n:].rearrange("p (e n j) -> p e n j", n=N, j=PACK),
-                w_raw[s][:].rearrange("p e (j n) -> p e n j", j=PACK),
-                1.0, 0.0, op0=ALU.mult, op1=ALU.add)
-            nc.gpsimd.tensor_tensor(
-                rounded[:, PACK * mine:PACK * n].rearrange("p (c i j) -> p c j i", i=QUAD, j=PACK),
-                xg[:, :, mine:n].rearrange("p j (c i) -> p c j i", i=QUAD),
-                shared_gates[e1 * C][:, shared_gates[e1 * C].shape[1] - shares[s]:].rearrange("p (c i) -> p c i", i=QUAD).unsqueeze(2).to_broadcast(
-                    [P, shares[s] // QUAD, PACK, QUAD]), ALU.mult)
-            if s + 1 == last:
-                gate_round(last, y[:].bitcast(BF16), ahead, 0, tail_cuts[1])
-            packed(s, words)
-            quantise_words(s, 0, words, rounded)
-            if s == PASSES:
-                open_banks([
-                    ("bank7", [(5 * C, C), (6 * C, C)]), ("bank0", [(8 * C, HALF)]),
-                    ("bank1", [(8 * C + HALF, HALF)])])
-                relu(y, WIDE)
-                open_banks([("bank6", [(7 * C, C)])])
-            if s + 1 < last:
-                multiply(s, 0, n)
-            xg = ahead
-
-        packed(last, WIDE)
-        quantise_words(last, 0, tail_cuts[1], y[:].bitcast(BF16))
-        multiply(last - 1, 0, tail_cuts[1])
-        multiply(last, 0, tail_cuts[1])
-        multiply(last - 1, tail_cuts[1], WIDE)
-        rounded = staging(WIDE)
-        pieces = list(zip(tail_cuts[1:], tail_cuts[2:]))
-        for a, z in pieces:
-            gate_round(last, rounded, xg, a, z)
-        for a, z in pieces:
-            quantise_words(last, a, z, rounded)
-            multiply(last, a, z)
-        held = keep.tile([P, MOST + SPARE], F32, name=f"plane{PASSES - 1}{PACK - 1}", align_bytes=64)
-        for s0 in range(0, WIDE, C):
-            relu(held, s0)
-        square(held, 0, WIDE)
-        for e in (5, 6):
-            relu(y, e * C)
-        square(y, WIDE, 7 * C)
+        held = keep.tile([P, HALF + SPARE], F32, name="plane13", align_bytes=64)
+        for e in range(4):
+            relu(held, e)
+        for e in range(4, 7):
+            relu(y, e)
+        square(held, 2 * C, 4 * C)
+        square(y, 4 * C, 7 * C)
+        nc.vector.tensor_tensor(y[:, :2 * C], held[:, :2 * C], held[:, :2 * C], ALU.mult)
         positive = keep.tile([P, 2 * C], F32, name="positive", align_bytes=64)
-        for s0 in (7 * C, 8 * C, 8 * C + HALF):
-            acc, m, name = accs[s0]
+        for s0, m in ((7 * C, C), (8 * C, half_c), (8 * C + half_c, half_c)):
             nc.vector.tensor_scalar(
-                positive[:, s0 - 7 * C:s0 - 7 * C + m], acc, bias[:, s0 // C:s0 // C + 1], 0.0,
+                positive[:, s0 - 7 * C:s0 - 7 * C + m], sums_of(s0, m), bias[:, s0 // C:s0 // C + 1], 0.0,
                 op0=ALU.add, op1=ALU.max)
-        nc.scalar.activation(y[:, 7 * C:8 * C], positive[:, :C], ACT.Square)
-        for a in (C, C + HALF):
-            half = positive[:, a:a + HALF]
-            nc.vector.tensor_tensor(y[:, 7 * C + a:7 * C + a + HALF], half, half, ALU.mult)
+        for a, z in ((0, C + half_c), (C + half_c, 2 * C)):
+            nc.vector.tensor_tensor(y[:, 7 * C + a:7 * C + z], positive[:, a:z], positive[:, a:z], ALU.mult)
 
         total = ring.tile([P, 4, T], F32, name="xg", align_bytes=64)
 

@@ -24,8 +24,8 @@ HALF = S // 2
 SPARE = 8
 STEPS = ((0, 0), (0, 1), (1, 0), (1, 1), (2, 0), (3, 0), (2, 1), (3, 1))
 OWN_ROW = 1
-OWNS = (576, 896, 896, 896, 896, 896, 896)
-SHARES = (144, 128, 176, 176, 176, 176, 128, 128)
+OWNS = (576, 992, 992, 992, 992, 992, 992)
+SHARES = (160, 144, 192, 192, 192, 192, 128, 128)
 CHUNKS = ((2, 2, 3), (6,), (5,), (5,), (5,), (5,), (3,))
 CALL_WORDS = (128, 256, 384, 512, 1024)
 TAIL_CUTS = (0, 640, 1024, HALF)

@@ -24,11 +24,12 @@ HALF = S // 2
 SPARE = 8
 STEPS = ((0, 0), (0, 1), (1, 0), (1, 1), (2, 0), (3, 0), (2, 1), (3, 1))
 OWN_ROW = 1
-OWNS = (576, 992, 992, 992, 992, 992, 992)
-SHARES = (160, 144, 192, 192, 192, 192, 128, 128)
+OWNS = (576, 1056, 1056, 1056, 1056, 1056, 1056)
+SHARES = (192, 176, 224, 224, 224, 224, 144, 160)
 CHUNKS = ((2, 2, 3), (6,), (5,), (5,), (5,), (5,), (3,))
 CALL_WORDS = (128, 256, 384, 512, 1024)
 TAIL_CUTS = (0, 640, 1024, HALF)
+TAIL_SHARE = 96
 OUT_CUTS = (0, 288, 640, T)
 RUN_VECTOR = 2
 RUN_GPSIMD = 2
@@ -107,6 +108,8 @@ def tile_moe_pre_lin_relu2_kernel(tc, xT, w, b, gate, offs, pos1, pos2, pos3, ou
         load_w(3)
         load_w(4)
         load_planes(3, range(PACK))
+        gate_tail = keep.tile([P, TAIL_SHARE], F32, name="gate_tail", align_bytes=64)
+        nc.sync.dma_start(gate_tail[:], gate[0:P, HALF + TAIL_CUTS[1]:HALF + TAIL_CUTS[1] + TAIL_SHARE])
         load_w(5)
         load_w(6)
 
@@ -260,12 +263,12 @@ def tile_moe_pre_lin_relu2_kernel(tc, xT, w, b, gate, offs, pos1, pos2, pos3, ou
         vector_products(last, rounded, xg[0], SHARES[last], TAIL_CUTS[1])
         quantise(last, 0, TAIL_CUTS[1], rounded)
         multiply()
-        stages = [(rounded, 0)] * (len(xg) - 2) + [(y[:].bitcast(BF16), TAIL_CUTS[-2])]
-        pieces = list(zip(TAIL_CUTS[1:], TAIL_CUTS[2:], xg[1:], stages))
-        for a, z, piece, (stage, staged) in pieces:
-            vector_products(last, stage, piece, a, z, a, staged)
-        for a, z, piece, (stage, staged) in pieces:
-            quantise(last, a, z, stage, staged)
+        second, third = TAIL_CUTS[1:3]
+        times_gate(nc.gpsimd, RUN_GPSIMD, rounded, xg[1], second, second + TAIL_SHARE, gate_tail[:], second, second)
+        vector_products(last, rounded, xg[1], second + TAIL_SHARE, third, second, second)
+        vector_products(last, y[:].bitcast(BF16), xg[2], third, HALF, third, third)
+        for a, z, stage in ((second, third, rounded), (third, HALF, y[:].bitcast(BF16))):
+            quantise(last, a, z, stage, a)
             multiply()
 
         def sums_of(s0, m):

@@ -24,9 +24,9 @@ HALF = S // 2
 SPARE = 8
 STEPS = ((0, 0), (0, 1), (1, 0), (1, 1), (2, 0), (3, 0), (2, 1), (3, 1))
 OWN_ROW = 1
-OWNS = (576, 1056, 1056, 1056, 1056, 1056, 1056)
-SHARES = (192, 176, 224, 224, 224, 224, 144, 160)
-CHUNKS = ((2, 2, 3), (6,), (5,), (5,), (5,), (5,), (3,))
+OWNS = (576, 1056, 1088, 1056, 1088, 1056, 1088)
+SHARES = (240, 304, 256, 256, 208, 208, 128, 160)
+CHUNKS = ((2, 2, 2), (4,), (5,), (5,), (6,), (6,), (4,))
 CALL_WORDS = (128, 256, 384, 512, 1024)
 TAIL_CUTS = (0, 640, 1024, HALF)
 TAIL_SHARE = 96
@@ -45,7 +45,7 @@ def tile_moe_pre_lin_relu2_kernel(tc, xT, w, b, gate, offs, pos1, pos2, pos3, ou
         last = len(STEPS) - 1
         slot_tokens = keep.tile([P, S // 16], U16, name="slot_tokens")
         x_rows = xT.rearrange("(g p j) t -> g j p t", p=P, j=PACK)
-        w_rows = w.rearrange("e (g p j) n -> g p e (j n)", p=P, j=PACK)
+        w_rows = w.rearrange("e (g p j) n -> g e p j n", p=P, j=PACK)
         planes = {}
         w_raw = {}
 
@@ -68,11 +68,9 @@ def tile_moe_pre_lin_relu2_kernel(tc, xT, w, b, gate, offs, pos1, pos2, pos3, ou
             first = starts[s]
             for size in CHUNKS[s]:
                 piece = blocks[first:first + size]
-                raw = ring.tile([P, size, PACK * N], F32, name="w_raw", align_bytes=64, bufs=3)
-                heads = [i for i, (g, e) in enumerate(piece) if i == 0 or piece[i - 1] != (g, e - 1)]
-                for a, z in zip(heads, heads[1:] + [size]):
-                    g, e = piece[a]
-                    nc.sync.dma_start(raw[:, a:z], w_rows[g][:, e:e + z - a])
+                raw = ring.tile([P, PACK, size * N], F32, name="w_raw", align_bytes=64, bufs=3)
+                for i, (g, e) in enumerate(piece):
+                    nc.sync.dma_start(raw[:, :, i * N:(i + 1) * N], w_rows[g, e])
                 w_raw[s].append((first - starts[s], size, raw))
                 first += size
 
@@ -92,10 +90,10 @@ def tile_moe_pre_lin_relu2_kernel(tc, xT, w, b, gate, offs, pos1, pos2, pos3, ou
         load_planes(0, range(1, PACK))
         load_w(0)
         load_gate(0)
-        load_planes(1, range(1))
+        load_planes(1, (1, 0))
         load_w(1)
         load_gate(1)
-        load_planes(1, range(1, PACK))
+        load_planes(1, (2, 3))
         bias = keep.tile([P, E], F32, name="bias")
         nc.sync.dma_start(bias[:], b)
         lists = []
@@ -107,7 +105,7 @@ def tile_moe_pre_lin_relu2_kernel(tc, xT, w, b, gate, offs, pos1, pos2, pos3, ou
         load_planes(2, range(PACK))
         load_w(3)
         load_w(4)
-        load_planes(3, range(PACK))
+        load_planes(3, (1, 0, 2, 3))
         gate_tail = keep.tile([P, TAIL_SHARE], F32, name="gate_tail", align_bytes=64)
         nc.sync.dma_start(gate_tail[:], gate[0:P, HALF + TAIL_CUTS[1]:HALF + TAIL_CUTS[1] + TAIL_SHARE])
         load_w(5)
@@ -246,8 +244,8 @@ def tile_moe_pre_lin_relu2_kernel(tc, xT, w, b, gate, offs, pos1, pos2, pos3, ou
             for first, size, raw in w_raw[s]:
                 a = first * N
                 nc.gpsimd.tensor_scalar(
-                    rounded[:, PACK * a:PACK * (a + size * N)].rearrange("p (e n j) -> p e n j", n=N, j=PACK),
-                    raw[:].rearrange("p e (j n) -> p e n j", j=PACK),
+                    rounded[:, PACK * a:PACK * (a + size * N)].rearrange("p (c i j) -> p c j i", i=RUN_GPSIMD, j=PACK),
+                    raw[:].rearrange("p j (c i) -> p c j i", i=RUN_GPSIMD),
                     1.0, 0.0, op0=ALU.mult, op1=ALU.add)
             gpsimd_product(s, tokens, xg)
             packed(s, words)

@@ -24,9 +24,12 @@ HALF = S // 2
 SPARE = 8
 STEPS = ((0, 0), (0, 1), (1, 0), (1, 1), (2, 0), (3, 0), (2, 1), (3, 1))
 OWN_ROW = 1
-OWNS = (576, 1056, 1088, 1056, 1088, 1056, 1088)
-SHARES = (240, 304, 256, 256, 208, 208, 128, 160)
-CHUNKS = ((2, 2, 2), (4,), (5,), (5,), (6,), (6,), (4,))
+OWNS = (576, 1088, 1088, 1088, 1088, 1088, 1088)
+SHARES = (208, 224, 272, 272, 272, 272, 128, 160)
+CHUNKS = ((2, 2, 3), (5,), (5,), (5,), (5,), (5,), (4,))
+PAIRED_FROM = 2
+FRONT = 640
+OPENING = 256
 CALL_WORDS = (128, 256, 384, 512, 1024)
 TAIL_CUTS = (0, 640, 1024, HALF)
 TAIL_SHARE = 96
@@ -45,7 +48,7 @@ def tile_moe_pre_lin_relu2_kernel(tc, xT, w, b, gate, offs, pos1, pos2, pos3, ou
         last = len(STEPS) - 1
         slot_tokens = keep.tile([P, S // 16], U16, name="slot_tokens")
         x_rows = xT.rearrange("(g p j) t -> g j p t", p=P, j=PACK)
-        w_rows = w.rearrange("e (g p j) n -> g e p j n", p=P, j=PACK)
+        w_rows = w.rearrange("e (g p j) n -> g p e (j n)", p=P, j=PACK)
         planes = {}
         w_raw = {}
 
@@ -68,9 +71,18 @@ def tile_moe_pre_lin_relu2_kernel(tc, xT, w, b, gate, offs, pos1, pos2, pos3, ou
             first = starts[s]
             for size in CHUNKS[s]:
                 piece = blocks[first:first + size]
-                raw = ring.tile([P, PACK, size * N], F32, name="w_raw", align_bytes=64, bufs=3)
-                for i, (g, e) in enumerate(piece):
-                    nc.sync.dma_start(raw[:, :, i * N:(i + 1) * N], w_rows[g, e])
+                raw = ring.tile([P, size * PACK * N], F32, name="w_raw", align_bytes=64, bufs=3)
+                if s < PAIRED_FROM:
+                    by_block = raw[:].rearrange("p (e x) -> p e x", e=size)
+                    heads = [i for i, (g, e) in enumerate(piece) if i == 0 or piece[i - 1] != (g, e - 1)]
+                    for a, z in zip(heads, heads[1:] + [size]):
+                        g, e = piece[a]
+                        nc.sync.dma_start(by_block[:, a:z], w_rows[g][:, e:e + z - a])
+                else:
+                    by_row = raw[:].rearrange("p (j x) -> p j x", j=PACK)
+                    for i, (g, e) in enumerate(piece):
+                        nc.sync.dma_start(
+                            by_row[:, :, i * N:(i + 1) * N], w_rows[g][:, e].rearrange("p (j n) -> p j n", j=PACK))
                 w_raw[s].append((first - starts[s], size, raw))
                 first += size
 
@@ -79,8 +91,7 @@ def tile_moe_pre_lin_relu2_kernel(tc, xT, w, b, gate, offs, pos1, pos2, pos3, ou
 
         def load_gate(h):
             tile = keep.tile([P, reach[h]], F32, name=f"gate_near{h}", align_bytes=64)
-            first = HALF if h else HALF - reach[0]
-            nc.sync.dma_start(tile[:], gate[0:P, first:first + reach[h]])
+            nc.sync.dma_start(tile[:], gate[0:P, h * HALF + FRONT - reach[h]:h * HALF + FRONT])
             gate_near.append(tile)
 
         load_plane(0, 0, nc.scalar)
@@ -121,7 +132,7 @@ def tile_moe_pre_lin_relu2_kernel(tc, xT, w, b, gate, offs, pos1, pos2, pos3, ou
         gate_cols = keep.tile([P, S // P], F32, name="gate_cols")
         nc.vector.tensor_copy(gate_cols[:], turned[:, :S // P])
         gate_banks = {}
-        for i, s0 in enumerate((0, BANK, S - 2 * BANK, S - BANK)):
+        for i, s0 in enumerate((0, FRONT, HALF, HALF + FRONT)):
             bank = psum.tile([P, BANK], F32, name=f"bank{i}")
             for c in range(BANK // P):
                 col = s0 // P + c
@@ -171,8 +182,8 @@ def tile_moe_pre_lin_relu2_kernel(tc, xT, w, b, gate, offs, pos1, pos2, pos3, ou
                         u = blocks.index((g, s0 // C))
                         home = max(i for i in range(last) if starts[i] <= u)
                         w_codes, w_scales = made[home]
-                        n0 = (u - starts[home]) * N
-                        c0 += lead[s]
+                        n0 = FRONT + (u - starts[home]) * N
+                        c0 += lead[s] * (c0 >= FRONT)
                         total, left = to_go[name]
                         to_go[name] = [total, left - 1]
                         nc.tensor.matmul_mx(
@@ -223,42 +234,44 @@ def tile_moe_pre_lin_relu2_kernel(tc, xT, w, b, gate, offs, pos1, pos2, pos3, ou
                     times_gate(nc.vector, RUN_VECTOR, rounded, xg, lo, hi, gate_banks[s0][:, first:first + hi - lo], origin, staged)
 
         def gpsimd_product(s, rounded, xg):
-            n = SHARES[s]
-            if STEPS[s][1]:
-                times_gate(nc.gpsimd, RUN_GPSIMD, rounded, xg, 0, n, gate_near[1][:, :n])
-            else:
-                times_gate(nc.gpsimd, RUN_GPSIMD, rounded, xg, HALF - n, HALF, gate_near[0][:, reach[0] - n:])
+            h = STEPS[s][1]
+            times_gate(nc.gpsimd, RUN_GPSIMD, rounded, xg, FRONT - SHARES[s], FRONT, gate_near[h][:, reach[h] - SHARES[s]:])
 
         half_c = C // 2
         open_banks([
-            ("bank4", [(0, C), (C, C)]), ("bank5", [(2 * C, C), (3 * C, C)]),
+            ("bank4", [(0, C), (C, C)]), ("bank5", [(2 * C, half_c), (FRONT, half_c), (3 * C, C)]),
             ("bank6", [(4 * C, half_c), (HALF, half_c), (5 * C, C)]), ("bank7", [(6 * C, C)])])
+        rounded = keep.tile([P, PACK * (HALF + max(lead))], BF16, name="rounded", align_bytes=64)
         xg = gather(0)
         for s in range(last):
-            h = STEPS[s][1]
             ahead = gather(s + 1) if s + 1 < last else gather_pieces(last)
-            words = HALF + sizes[s] * N
-            rounded = ring.tile([P, PACK * words], BF16, name="rounded", align_bytes=64, bufs=1)
-            tokens = rounded[:, PACK * lead[s]:]
-            vector_products(s, tokens, xg, SHARES[s] * h, HALF - SHARES[s] * (1 - h))
+            words = HALF + lead[s]
+            vector_products(s, rounded, xg, 0, FRONT - SHARES[s])
+            vector_products(s, rounded, xg, FRONT, HALF, 0, -lead[s])
             for first, size, raw in w_raw[s]:
-                a = first * N
-                nc.gpsimd.tensor_scalar(
-                    rounded[:, PACK * a:PACK * (a + size * N)].rearrange("p (c i j) -> p c j i", i=RUN_GPSIMD, j=PACK),
-                    raw[:].rearrange("p j (c i) -> p c j i", i=RUN_GPSIMD),
-                    1.0, 0.0, op0=ALU.mult, op1=ALU.add)
-            gpsimd_product(s, tokens, xg)
+                a = FRONT + first * N
+                stage = rounded[:, PACK * a:PACK * (a + size * N)]
+                if s < PAIRED_FROM:
+                    pattern = (stage.rearrange("p (e n j) -> p e n j", n=N, j=PACK),
+                               raw[:].rearrange("p (e j n) -> p e n j", n=N, j=PACK))
+                else:
+                    pattern = (stage.rearrange("p (c i j) -> p c j i", i=RUN_GPSIMD, j=PACK),
+                               raw[:].rearrange("p (j c i) -> p c j i", i=RUN_GPSIMD, j=PACK))
+                nc.gpsimd.tensor_scalar(*pattern, 1.0, 0.0, op0=ALU.mult, op1=ALU.add)
+            gpsimd_product(s, rounded, xg)
             packed(s, words)
-            quantise(s, 0, words, rounded)
+            closing = min(words, OPENING + 3 * BANK)
+            for a, z in ((0, OPENING), (closing, words), (OPENING, closing)):
+                quantise(s, a, z, rounded)
+            ready[s] = HALF
             if s == last - 2:
                 open_banks([("bank0", [(7 * C, C), (8 * C, half_c)]), ("bank1", [(8 * C + half_c, half_c)])])
             multiply()
             xg = ahead
 
-        rounded = ring.tile([P, PACK * HALF], BF16, name="rounded", align_bytes=64, bufs=1)
         packed(last, HALF)
         gpsimd_product(last, rounded, xg[0])
-        vector_products(last, rounded, xg[0], SHARES[last], TAIL_CUTS[1])
+        vector_products(last, rounded, xg[0], 0, FRONT - SHARES[last])
         quantise(last, 0, TAIL_CUTS[1], rounded)
         multiply()
         second, third = TAIL_CUTS[1:3]

@@ -24,8 +24,8 @@ HALF = S // 2
 SPARE = 8
 STEPS = ((0, 0), (0, 1), (1, 0), (1, 1), (2, 0), (3, 0), (2, 1), (3, 1))
 OWN_ROW = 1
-OWNS = (576, 1088, 1088, 1088, 1088, 1088, 1088)
-SHARES = (208, 224, 272, 272, 272, 272, 128, 160)
+OWNS = (576, 1056, 1056, 1056, 1056, 1056, 1056)
+SHARES = (192, 208, 256, 256, 256, 256, 128, 160)
 CHUNKS = ((2, 2, 3), (5,), (5,), (5,), (5,), (5,), (4,))
 PAIRED_FROM = 2
 FRONT = 640
@@ -277,8 +277,9 @@ def tile_moe_pre_lin_relu2_kernel(tc, xT, w, b, gate, offs, pos1, pos2, pos3, ou
         second, third = TAIL_CUTS[1:3]
         times_gate(nc.gpsimd, RUN_GPSIMD, rounded, xg[1], second, second + TAIL_SHARE, gate_tail[:], second, second)
         vector_products(last, rounded, xg[1], second + TAIL_SHARE, third, second, second)
-        vector_products(last, y[:].bitcast(BF16), xg[2], third, HALF, third, third)
-        for a, z, stage in ((second, third, rounded), (third, HALF, y[:].bitcast(BF16))):
+        closing_stage = y[:, half_c:C + half_c].bitcast(BF16)
+        vector_products(last, closing_stage, xg[2], third, HALF, third, third)
+        for a, z, stage in ((second, third, rounded), (third, HALF, closing_stage)):
             quantise(last, a, z, stage, a)
             multiply()
 
@@ -293,20 +294,26 @@ def tile_moe_pre_lin_relu2_kernel(tc, xT, w, b, gate, offs, pos1, pos2, pos3, ou
             nc.scalar.activation(y[:, a:z], src[:, a:z], ACT.Square)
 
         held = keep.tile([P, HALF + SPARE], F32, name="plane13", align_bytes=64)
-        for e in range(4):
+        for e in (1, 2, 3, 0):
             relu(held, e)
         for e in range(4, 7):
             relu(y, e)
-        square(held, 2 * C, 4 * C)
         square(y, 4 * C, 7 * C)
-        nc.vector.tensor_tensor(y[:, :2 * C], held[:, :2 * C], held[:, :2 * C], ALU.mult)
+        nc.gpsimd.tensor_tensor(y[:, C:4 * C], held[:, C:4 * C], held[:, C:4 * C], ALU.mult)
+
+        def times_relu(s0, m, positive_part):
+            nc.vector.scalar_tensor_tensor(
+                y[:, s0:s0 + m], sums_of(s0, m), bias[:, s0 // C:s0 // C + 1], positive_part,
+                op0=ALU.add, op1=ALU.mult)
+
+        times_relu(0, C, held[:, :C])
         positive = keep.tile([P, 2 * C], F32, name="positive", align_bytes=64)
         for s0, m in ((7 * C, C), (8 * C, half_c), (8 * C + half_c, half_c)):
             nc.vector.tensor_scalar(
                 positive[:, s0 - 7 * C:s0 - 7 * C + m], sums_of(s0, m), bias[:, s0 // C:s0 // C + 1], 0.0,
                 op0=ALU.add, op1=ALU.max)
-        for a, z in ((0, C + half_c), (C + half_c, 2 * C)):
-            nc.vector.tensor_tensor(y[:, 7 * C + a:7 * C + z], positive[:, a:z], positive[:, a:z], ALU.mult)
+        for s0, m in ((7 * C, C), (8 * C, half_c), (8 * C + half_c, half_c)):
+            times_relu(s0, m, positive[:, s0 - 7 * C:s0 - 7 * C + m])
 
         total = ring.tile([P, 4, T], F32, name="xg", align_bytes=64)
 

@@ -25,11 +25,11 @@ SPARE = 8
 STEPS = ((0, 0), (0, 1), (1, 0), (1, 1), (2, 0), (3, 0), (2, 1), (3, 1))
 OWN_ROW = 1
 OWNS = (576, 1056, 1056, 1056, 1056, 1056, 1056)
-SHARES = (192, 208, 256, 256, 256, 256, 128, 160)
-CHUNKS = ((2, 2, 3), (5,), (5,), (5,), (5,), (5,), (4,))
+SHARES = (192, 208, 256, 256, 256, 208, 128, 160)
+CHUNKS = ((2, 2, 2), (5,), (5,), (5,), (5,), (6,), (4,))
 PAIRED_FROM = 2
 FRONT = 640
-OPENING = 256
+WIDE = 1024
 CALL_WORDS = (128, 256, 384, 512, 1024)
 TAIL_CUTS = (0, 640, 1024, HALF)
 TAIL_SHARE = 96
@@ -260,8 +260,8 @@ def tile_moe_pre_lin_relu2_kernel(tc, xT, w, b, gate, offs, pos1, pos2, pos3, ou
                 nc.gpsimd.tensor_scalar(*pattern, 1.0, 0.0, op0=ALU.mult, op1=ALU.add)
             gpsimd_product(s, rounded, xg)
             packed(s, words)
-            closing = min(words, OPENING + 3 * BANK)
-            for a, z in ((0, OPENING), (closing, words), (OPENING, closing)):
+            closing = FRONT + lead[s]
+            for a, z in ((0, closing - WIDE), (closing - WIDE, closing), (closing, words)):
                 quantise(s, a, z, rounded)
             ready[s] = HALF
             if s == last - 2:

@@ -25,7 +25,7 @@ SPARE = 8
 STEPS = ((0, 0), (0, 1), (1, 0), (1, 1), (2, 0), (3, 0), (2, 1), (3, 1))
 OWN_ROW = 1
 OWNS = (576, 1056, 1056, 1056, 1056, 1056, 1056)
-SHARES = (192, 208, 256, 256, 256, 208, 128, 160)
+SHARES = (232, 208, 256, 256, 256, 208, 128, 160)
 CHUNKS = ((2, 2, 2), (5,), (5,), (5,), (5,), (6,), (4,))
 PAIRED_FROM = 2
 FRONT = 640

from contextlib import ExitStack

import concourse.mybir as mybir
from concourse.masks import make_identity

K, T, E, C, N = 2048, 768, 9, 256, 128
S = E * C
FLOPS = 2 * K * N * S
BYTES = 4 * (K * T + E * K * N + N * E + S + N * T) + 2 * 128 * (S + 3 * T) // 16

F32 = mybir.dt.float32
BF16 = mybir.dt.bfloat16
U32 = mybir.dt.uint32
U16 = mybir.dt.uint16
U8 = mybir.dt.uint8
FP8X4 = mybir.dt.float8_e4m3fn_x4
ACT = mybir.ActivationFunctionType
ALU = mybir.AluOpType

P = 128
PACK = 4
BANK = 512
HALF = S // 2
SPARE = 8
STEPS = ((0, 0), (0, 1), (1, 0), (1, 1), (2, 0), (3, 0), (2, 1), (3, 1))
OWN_ROW = 1
OWNS = (576, 1056, 1056, 1056, 1056, 1056, 1056)
SHARES = (232, 208, 256, 256, 256, 208, 128, 160)
CHUNKS = ((2, 2, 2), (5,), (5,), (5,), (5,), (6,), (4,))
PAIRED_FROM = 2
FRONT = 640
WIDE = 1024
CALL_WORDS = (128, 256, 384, 512, 1024)
TAIL_CUTS = (0, 640, 1024, HALF)
TAIL_SHARE = 96
OUT_CUTS = (0, 288, 640, T)
RUN_VECTOR = 2
RUN_GPSIMD = 2


def tile_moe_pre_lin_relu2_kernel(tc, xT, w, b, gate, offs, pos1, pos2, pos3, out):
    nc = tc.nc
    with ExitStack() as ctx:
        keep = ctx.enter_context(tc.tile_pool(name="keep", bufs=1))
        ring = ctx.enter_context(tc.tile_pool(name="ring", bufs=2))
        psum = ctx.enter_context(tc.psum_pool(name="psum", bufs=1))

        last = len(STEPS) - 1
        slot_tokens = keep.tile([P, S // 16], U16, name="slot_tokens")
        x_rows = xT.rearrange("(g p j) t -> g j p t", p=P, j=PACK)
        w_rows = w.rearrange("e (g p j) n -> g p e (j n)", p=P, j=PACK)
        planes = {}
        w_raw = {}

        def load_plane(g, j, queue):
            plane = keep.tile([P, HALF + SPARE], F32, name=f"plane{g % 2}{j}", align_bytes=64)
            queue.dma_start(plane[:, :T], x_rows[g, j])
            planes[g, j] = plane

        def load_planes(g, rows):
            for j in rows:
                load_plane(g, j, nc.sync)

        middle_expert = E // 2
        blocks = [(g, e) for g, h in STEPS for e in (range(middle_expert + 1), range(middle_expert + 1, E))[h]]
        sizes = [sum(chunk) for chunk in CHUNKS]
        starts = [sum(sizes[:s]) for s in range(len(sizes) + 1)]

        def load_w(s):
            w_raw[s] = []
            first = starts[s]
            for size in CHUNKS[s]:
                piece = blocks[first:first + size]
                raw = ring.tile([P, size * PACK * N], F32, name="w_raw", align_bytes=64, bufs=3)
                if s < PAIRED_FROM:
                    by_block = raw[:].rearrange("p (e x) -> p e x", e=size)
                    heads = [i for i, (g, e) in enumerate(piece) if i == 0 or piece[i - 1] != (g, e - 1)]
                    for a, z in zip(heads, heads[1:] + [size]):
                        g, e = piece[a]
                        nc.sync.dma_start(by_block[:, a:z], w_rows[g][:, e:e + z - a])
                else:
                    by_row = raw[:].rearrange("p (j x) -> p j x", j=PACK)
                    for i, (g, e) in enumerate(piece):
                        nc.sync.dma_start(
                            by_row[:, :, i * N:(i + 1) * N], w_rows[g][:, e].rearrange("p (j n) -> p j n", j=PACK))
                w_raw[s].append((first - starts[s], size, raw))
                first += size

        reach = [max(SHARES[s] for s in range(len(STEPS)) if STEPS[s][1] == h) for h in range(2)]
        gate_near = []

        def load_gate(h):
            tile = keep.tile([P, reach[h]], F32, name=f"gate_near{h}", align_bytes=64)
            nc.sync.dma_start(tile[:], gate[0:P, h * HALF + FRONT - reach[h]:h * HALF + FRONT])
            gate_near.append(tile)

        load_plane(0, 0, nc.scalar)
        nc.sync.dma_start(slot_tokens[:], offs)
        gate_rows = ring.tile([P, P], F32, name="xg", align_bytes=64)
        nc.sync.dma_start(gate_rows[:], gate.rearrange("r (c p) -> (r c) p", p=P)[0:P])
        load_planes(0, range(1, PACK))
        load_w(0)
        load_gate(0)
        load_planes(1, (1, 0))
        load_w(1)
        load_gate(1)
        load_planes(1, (2, 3))
        bias = keep.tile([P, E], F32, name="bias")
        nc.sync.dma_start(bias[:], b)
        lists = []
        for r, pos in enumerate((pos1, pos2, pos3)):
            lst = keep.tile([P, T // 16], U16, name=f"pos{r}")
            nc.sync.dma_start(lst[:], pos)
            lists.append(lst)
        load_w(2)
        load_planes(2, range(PACK))
        load_w(3)
        load_w(4)
        load_planes(3, (1, 0, 2, 3))
        gate_tail = keep.tile([P, TAIL_SHARE], F32, name="gate_tail", align_bytes=64)
        nc.sync.dma_start(gate_tail[:], gate[0:P, HALF + TAIL_CUTS[1]:HALF + TAIL_CUTS[1] + TAIL_SHARE])
        load_w(5)
        load_w(6)

        zero = keep.tile([P, 1], F32, name="zero")
        nc.vector.memset(zero[:], 0.0)
        identity = keep.tile([P, P], F32, name="identity")
        nc.scalar.activation(identity[:], zero[:].to_broadcast([P, P]), ACT.Copy)
        make_identity(nc, identity[:], nomemset=True)
        turned = psum.tile([P, BANK], F32, name="bank7")
        nc.tensor.transpose(turned[:, :P], gate_rows[:], identity[:])
        gate_cols = keep.tile([P, S // P], F32, name="gate_cols")
        nc.vector.tensor_copy(gate_cols[:], turned[:, :S // P])
        gate_banks = {}
        for i, s0 in enumerate((0, FRONT, HALF, HALF + FRONT)):
            bank = psum.tile([P, BANK], F32, name=f"bank{i}")
            for c in range(BANK // P):
                col = s0 // P + c
                nc.tensor.transpose(
                    bank[:, c * P:(c + 1) * P], gate_cols[:, col:col + 1].to_broadcast([P, P]), identity[:])
            gate_banks[s0] = bank

        y = keep.tile([P, S], F32, name="y", align_bytes=64)
        accs = {}
        to_go = {}

        def open_banks(banks):
            for name, sums in banks:
                bank = psum.tile([N, BANK], F32, name=name)
                to_go[name] = [K // (P * PACK) * len(sums)] * 2
                for s0, m in sums:
                    accs[s0] = (bank, s0 - sums[0][0], m, name)

        lead = [size * N for size in sizes] + [0]
        made = {}
        ready = {}
        done = set()

        def packed(s, words):
            codes = keep.tile([P, words], U32, name=f"codes{s}", align_bytes=64)
            scales = keep.tile([P, words], U8, name=f"scales{s}", align_bytes=64)
            made[s] = (codes, scales)

        def quantise(s, a, z, src, origin=0):
            codes, scales = made[s]
            ready[s] = z - lead[s]
            while a < z:
                upto = a + max(m for m in CALL_WORDS if m <= z - a)
                nc.vector.quantize_mx(
                    out=codes[:, a:upto].bitcast(FP8X4), scales=scales[:, a:upto], in_=src[:, PACK * (a - origin):PACK * (upto - origin)])
                a = upto

        def multiply():
            for s in sorted(ready):
                g, h = STEPS[s]
                x_codes, x_scales = made[s]
                for s0 in sorted(accs):
                    bank, col, m, name = accs[s0]
                    c0 = s0 - h * HALF
                    if 0 <= c0 < min(ready[s], HALF) and (s, s0) not in done:
                        done.add((s, s0))
                        u = blocks.index((g, s0 // C))
                        home = max(i for i in range(last) if starts[i] <= u)
                        w_codes, w_scales = made[home]
                        n0 = FRONT + (u - starts[home]) * N
                        c0 += lead[s] * (c0 >= FRONT)
                        total, left = to_go[name]
                        to_go[name] = [total, left - 1]
                        nc.tensor.matmul_mx(
                            out=bank[:, col:col + m],
                            lhsT=w_codes[:, n0:n0 + N].bitcast(FP8X4), lhsT_scale=w_scales[:, n0:n0 + N],
                            rhs=x_codes[:, c0:c0 + m].bitcast(FP8X4), rhs_scale=x_scales[:, c0:c0 + m],
                            start=(left == total), stop=(left == 1))

        def picked(s, j, a, z):
            g, h = STEPS[s]
            return planes[g, j][:].indirect(slot_tokens[:, (h * HALF + a) // 16:(h * HALF + z) // 16])

        def gather(s):
            xg = ring.tile([P, PACK, HALF], F32, name="xg", align_bytes=64)
            own_rows = range(PACK) if s == 0 else (OWN_ROW,)
            for j in range(PACK):
                if j not in own_rows:
                    nc.scalar.activation(xg[:, j, :], picked(s, j, 0, HALF), ACT.Copy)
            cut = HALF - OWNS[s]
            for j in own_rows:
                nc.scalar.activation(xg[:, j, :cut], picked(s, j, 0, cut), ACT.Copy)
                nc.vector.tensor_copy(xg[:, j, cut:], picked(s, j, cut, HALF))
            return xg

        def gather_pieces(s):
            flat = ring.tile([P, PACK * HALF], F32, name="xg", align_bytes=64)
            pieces = []
            for a, z in zip(TAIL_CUTS, TAIL_CUTS[1:]):
                piece = flat[:, PACK * a:PACK * z].rearrange("p (j c) -> p j c", j=PACK)
                for j in range(PACK):
                    nc.scalar.activation(piece[:, j, :], picked(s, j, a, z), ACT.Copy)
                pieces.append(piece)
            return pieces

        def times_gate(engine, run, rounded, xg, a, z, weights, origin=0, staged=0):
            engine.tensor_tensor(
                rounded[:, PACK * (a - staged):PACK * (z - staged)].rearrange("p (c i j) -> p c j i", i=run, j=PACK),
                xg[:, :, a - origin:z - origin].rearrange("p j (c i) -> p c j i", i=run),
                weights.rearrange("p (c i) -> p c i", i=run).unsqueeze(2).to_broadcast(
                    [P, (z - a) // run, PACK, run]), ALU.mult)

        def vector_products(s, rounded, xg, a, z, origin=0, staged=0):
            h = STEPS[s][1]
            for s0 in sorted(gate_banks):
                lo, hi = max(a, s0 - h * HALF), min(z, s0 + BANK - h * HALF)
                if lo < hi:
                    first = h * HALF + lo - s0
                    times_gate(nc.vector, RUN_VECTOR, rounded, xg, lo, hi, gate_banks[s0][:, first:first + hi - lo], origin, staged)

        def gpsimd_product(s, rounded, xg):
            h = STEPS[s][1]
            times_gate(nc.gpsimd, RUN_GPSIMD, rounded, xg, FRONT - SHARES[s], FRONT, gate_near[h][:, reach[h] - SHARES[s]:])

        half_c = C // 2
        open_banks([
            ("bank4", [(0, C), (C, C)]), ("bank5", [(2 * C, half_c), (FRONT, half_c), (3 * C, C)]),
            ("bank6", [(4 * C, half_c), (HALF, half_c), (5 * C, C)]), ("bank7", [(6 * C, C)])])
        rounded = keep.tile([P, PACK * (HALF + max(lead))], BF16, name="rounded", align_bytes=64)
        xg = gather(0)
        for s in range(last):
            ahead = gather(s + 1) if s + 1 < last else gather_pieces(last)
            words = HALF + lead[s]
            vector_products(s, rounded, xg, 0, FRONT - SHARES[s])
            vector_products(s, rounded, xg, FRONT, HALF, 0, -lead[s])
            for first, size, raw in w_raw[s]:
                a = FRONT + first * N
                stage = rounded[:, PACK * a:PACK * (a + size * N)]
                if s < PAIRED_FROM:
                    pattern = (stage.rearrange("p (e n j) -> p e n j", n=N, j=PACK),
                               raw[:].rearrange("p (e j n) -> p e n j", n=N, j=PACK))
                else:
                    pattern = (stage.rearrange("p (c i j) -> p c j i", i=RUN_GPSIMD, j=PACK),
                               raw[:].rearrange("p (j c i) -> p c j i", i=RUN_GPSIMD, j=PACK))
                nc.gpsimd.tensor_scalar(*pattern, 1.0, 0.0, op0=ALU.mult, op1=ALU.add)
            gpsimd_product(s, rounded, xg)
            packed(s, words)
            closing = FRONT + lead[s]
            for a, z in ((0, closing - WIDE), (closing - WIDE, closing), (closing, words)):
                quantise(s, a, z, rounded)
            ready[s] = HALF
            if s == last - 2:
                open_banks([("bank0", [(7 * C, C), (8 * C, half_c)]), ("bank1", [(8 * C + half_c, half_c)])])
            multiply()
            xg = ahead

        packed(last, HALF)
        gpsimd_product(last, rounded, xg[0])
        vector_products(last, rounded, xg[0], 0, FRONT - SHARES[last])
        quantise(last, 0, TAIL_CUTS[1], rounded)
        multiply()
        second, third = TAIL_CUTS[1:3]
        times_gate(nc.gpsimd, RUN_GPSIMD, rounded, xg[1], second, second + TAIL_SHARE, gate_tail[:], second, second)
        vector_products(last, rounded, xg[1], second + TAIL_SHARE, third, second, second)
        closing_stage = y[:, half_c:C + half_c].bitcast(BF16)
        vector_products(last, closing_stage, xg[2], third, HALF, third, third)
        for a, z, stage in ((second, third, rounded), (third, HALF, closing_stage)):
            quantise(last, a, z, stage, a)
            multiply()

        def sums_of(s0, m):
            bank, col = accs[s0][:2]
            return bank[:, col:col + m]

        def relu(dst, e):
            nc.scalar.activation(dst[:, e * C:(e + 1) * C], sums_of(e * C, C), ACT.Relu, bias=bias[:, e:e + 1])

        def square(src, a, z):
            nc.scalar.activation(y[:, a:z], src[:, a:z], ACT.Square)

        held = keep.tile([P, HALF + SPARE], F32, name="plane13", align_bytes=64)
        for e in (1, 2, 3, 0):
            relu(held, e)
        for e in range(4, 7):
            relu(y, e)
        square(y, 4 * C, 7 * C)
        nc.gpsimd.tensor_tensor(y[:, C:4 * C], held[:, C:4 * C], held[:, C:4 * C], ALU.mult)

        def times_relu(s0, m, positive_part):
            nc.vector.scalar_tensor_tensor(
                y[:, s0:s0 + m], sums_of(s0, m), bias[:, s0 // C:s0 // C + 1], positive_part,
                op0=ALU.add, op1=ALU.mult)

        times_relu(0, C, held[:, :C])
        positive = keep.tile([P, 2 * C], F32, name="positive", align_bytes=64)
        for s0, m in ((7 * C, C), (8 * C, half_c), (8 * C + half_c, half_c)):
            nc.vector.tensor_scalar(
                positive[:, s0 - 7 * C:s0 - 7 * C + m], sums_of(s0, m), bias[:, s0 // C:s0 // C + 1], 0.0,
                op0=ALU.add, op1=ALU.max)
        for s0, m in ((7 * C, C), (8 * C, half_c), (8 * C + half_c, half_c)):
            times_relu(s0, m, positive[:, s0 - 7 * C:s0 - 7 * C + m])

        total = ring.tile([P, 4, T], F32, name="xg", align_bytes=64)

        def fetch(r, a, z):
            return y[:].indirect(lists[r][:, a // 16:z // 16])

        def fetch_alone(row, r, a, z):
            nc.scalar.activation(total[:, row, a:z], fetch(r, a, z), ACT.Copy)

        def fetch_onto(r, a, z):
            nc.vector.tensor_tensor(total[:, 2, a:z], fetch(r, a, z), total[:, 0, a:z], ALU.add)

        left, middle, right = zip(OUT_CUTS, OUT_CUTS[1:])
        fetch_alone(0, 0, *right)
        fetch_alone(0, 0, *middle)
        fetch_alone(1, 0, *left)
        fetch_alone(1, 1, *middle)
        fetch_alone(1, 1, *right)
        nc.vector.tensor_copy(total[:, 0, :left[1]], fetch(1, *left))
        for a, z in (right, left, middle):
            fetch_onto(2, a, z)
        for (a, z), queue in ((left, nc.sync), (middle, nc.scalar), (right, nc.sync)):
            nc.vector.tensor_tensor(total[:, 3, a:z], total[:, 2, a:z], total[:, 1, a:z], ALU.add)
            queue.dma_start(out[:, a:z], total[:, 3, a:z])
